import numpy as np, ml_dtypes
CORES = [25,29,65,69,153,157,193,197]
N = 8
import mx_ref
BF = ml_dtypes.bfloat16
def gentries(a):
    return np.ascontiguousarray(a.reshape(8, 16, -1).transpose(0, 2, 1)).reshape(8, -1)
def gtable(e):
    e = np.asarray(e); return np.ascontiguousarray(e.reshape(8, -1, 16).transpose(0, 2, 1)).reshape(128, -1).astype(np.int32)
def gcols(t, e):
    v = np.concatenate([t.reshape(8, 16, -1, 4), np.zeros((8, 16, 1, 4), BF)], axis=2)
    return np.ascontiguousarray(np.stack([v[g][:, e[g]] for g in range(8)])).reshape(128, -1)
def tile(rs):
    return np.stack(rs, axis=2).reshape(128, -1).astype(BF)
def cut(t, i, w=512):
    return t[:, w * i:w * i + w]
def pick(q, e):
    c = np.concatenate([q[0].reshape(128, -1, 4), np.zeros((128, 1, 4), np.uint8)], axis=1); s = np.concatenate([q[1], np.ones((16, 1), np.uint8)], axis=1)
    return (np.ascontiguousarray(c[:, e].reshape(128, -1)), np.ascontiguousarray(s[:, e]))
def join(*qs):
    return (np.concatenate([q[0] for q in qs], axis=1), np.concatenate([q[1] for q in qs], axis=1))
def put(q, e, v):
    c, s = q[0].reshape(128, -1, 4).copy(), q[1].copy(); c[:, e] = v[0].reshape(128, -1, 4); s[:, e] = v[1]
    return (c.reshape(128, -1), s)
def pk(c, s):
    return (np.ascontiguousarray(c), mx_ref.live(s))
def emit(q):
    return q[0], q[1]
def packed(v, rng):
    q = [mx_ref.quantize(np.ascontiguousarray(v[r])) for r in range(N)]
    return np.stack([a for a, b in q]), np.stack([mx_ref.plane(b, rng) for a, b in q])
def values_of_codes():
    e, c = np.zeros((128, 128, 4), np.float32), np.zeros((128, 2, 4), np.uint8)
    e[np.arange(128), np.arange(128), 0] = 1
    c[:127, :, 0] = np.arange(256).reshape(2, 128).T[:127]
    return mx_ref.matmul(mx_ref.quantize(e.reshape(128, 512).astype(BF)), (c.reshape(128, 8), np.full((16, 2), 127, np.uint8))).T.reshape(-1).astype(np.float64)
CODE_VALUE, SCALE_VALUE = values_of_codes(), 2.0 ** (np.arange(256) - 127.0)
def decode(q):
    return (CODE_VALUE[q[0]].reshape(16, 8, -1, 4) * SCALE_VALUE[q[1]][:, None, :, None] + 0.0).reshape(128, -1).astype(np.float32)
def f(rng, *shape):
    return mx_ref.flush((rng.standard_normal(shape, dtype=np.float32) * np.exp2(rng.integers(-2, 3, shape[:-1] + (1,)))).astype(BF))
def wide(rng, *shape, cols=0):
    v = rng.standard_normal(shape, dtype=np.float32) * np.exp2(rng.integers(-12, 13, shape)).astype(np.float32)
    if cols: v *= np.repeat(np.exp2(rng.integers(-cols, cols + 1, shape[:-2] + (1, shape[-1] // 4))) * (rng.random(shape[:-2] + (1, shape[-1] // 4)) > 0.0625), 4, axis=-1).astype(np.float32)
    return mx_ref.flush(v.astype(BF))
C, K, R = 224, 96, 3
def order(p):
    return np.argsort(-(p[::16] + np.float32(0.0)), axis=1, kind="stable")
def larger(a, b):
    return np.maximum(a.astype(np.float32), b.astype(np.float32)).astype(BF)
def numbers_of(rng):
    return {"x": np.array(f(rng, N, 128, 4 * C)), "u": np.array(f(rng, N, 128, 512)), "v": np.array(f(rng, N, 128, 512))}
def weights(rng, still=[]):
    w = np.array(f(rng, N, 128, 2048)).reshape(N, 8, 16, 4, 8, 16, 4)
    for i in still:
        w[:, :, i] = 0
        w[:, :, :, :, :, i] = 0
    c, p = packed(w.reshape(N, 128, 2048), rng)
    return {"wc": c, "ws": p}
def lists_of(rng):
    return np.stack([gtable(rng.integers(0, C, (8, R * C))) for r in range(N)])
def signs(rng):
    return np.stack([rng.permutation(8) % 2 * 2.0 - 1.0 for r in range(N)])
def setup_inputs(rng):
    return {**numbers_of(rng), **weights(rng), "nb": lists_of(rng)}
def setup_inputs_ties(rng):
    d = numbers_of(rng)
    e = rng.permutation(N)
    x = d["x"].reshape(N, 8, 16, C, 4)
    for r in range(N):
        k = np.zeros(C, int) if r == e[0] else rng.permutation(C) % 3
        a = x[r][:, :8, :3].copy()
        a[:, :, 2] = 0
        x[r][:, :8] = a[:, :, k]
    x[e[1]][:, :8] = 0
    u = d["u"].reshape(N, 8, 16, 8, 16, 4)
    k = u.copy()
    u[:, :, :, :, :3] = 0
    for g in range(8): u[:, g, :8, g, :3] = k[:, g, :8, g, :3]
    return {"x": x.reshape(N, 128, 4 * C), "u": u.reshape(N, 128, 512), "v": d["v"], **weights(rng, range(8)), "nb": lists_of(rng)}
def setup_inputs_near(rng):
    d = numbers_of(rng)
    x = d["x"].astype(np.float32).reshape(N, 8, 16, C, 4)
    u = d["u"].reshape(N, 128, 128, 4)
    x[:, :, 0] = 0
    x[:, :, 10] = 0
    for i in range(3): u[:, :, i::16] = 0
    c = rng.permutation(8) % 2 * 2.0 - 1.0
    first = int(rng.integers(N))
    upper = np.arange(C) // (C // 2)
    for n in range(N):
        r = (first + n) % N
        i = (np.arange(C) + rng.integers(0, C, (8, 1))) % (C // 2) * 2 + upper
        one = n < N // 2
        s = i // 2 if one else i
        size = 1.0 if one else 2.0 ** -7
        k = 1.0 if one and n % 2 == 0 else 2.0 ** -30
        if one:
            x[r, :, 0, :, 0] = c[:, None]
            for g in rng.permutation(8)[:4]: x[r, g, 0, rng.integers(C), 0] *= np.float32(2.0 ** 30)
        z = ((s[:, :, None] >> np.arange(8)) & 1) * np.exp2(np.arange(8) - 23.0) * size
        x[r, :, 8] = z[:, :, :4]
        x[r, :, 9] = z[:, :, 4:]
        x[r, :, 10, :, 0] = rng.integers(-1, 2, (8, C)) * 2.0 ** -23 * size
        x[r, :, 11:] = rng.integers(4, 8, (8, 5, C, 4)) * rng.choice([-1.0, 1.0], (8, 5, C, 4)) * 2.0 ** -20 * size
        for h in range(0, 128, 16):
            u[r, h, h:h + 2, 0] = k
            u[r, h + 8:h + 10, h] = k
            u[r, h + 8:h + 10, h + 1] = (k * rng.choice([-1.0, 1.0], (2, 4))).astype(np.float32).astype(BF)
            u[r, h + 10, h + 2, 0] = k
    return {"x": x.reshape(N, 128, 4 * C).astype(BF), "u": u.reshape(N, 128, 512), "v": d["v"], **weights(rng, [0, 8, 9, 10, 11, 12, 13, 14, 15]), "nb": lists_of(rng)}
def setup_inputs_huge(rng):
    d = numbers_of(rng)
    c = np.stack([rng.permutation(C) % 2 * 2.0 - 1.0 for r in range(N)])
    low = (int(rng.integers(N)) + np.arange(N // 2)) % N
    c[low] = -1
    size = np.where(c < 0, -2.0 ** 30, 2.0 ** 28)
    size[low, C - K:] *= 0.7
    x = (0.6 + 0.2 * rng.random((N, 128, C, 4))) * size[:, None, :, None]
    u = d["u"].reshape(N, 128, 128, 4)
    for i in range(3):
        a = 2.0 ** 30 * (1 - 0.25 * rng.random((N, 128, 8, 4))) * signs(rng)[:, None, :, None]
        u[:, :, i::16] = a.astype(np.float32).astype(BF)
    w = np.zeros((N, 128, 4, 128, 4), np.float32)
    i = np.arange(128)
    for b in range(4): w[:, i, b, i, b] = 16 - 32 * (i % 2)
    wc, ws = packed(w.reshape(N, 128, 2048).astype(BF), rng)
    return {"x": x.astype(np.float32).reshape(N, 128, 4 * C).astype(BF), "u": u.reshape(N, 128, 512), "v": d["v"], "wc": wc, "ws": ws, "nb": lists_of(rng)}
def setup_inputs_chains(rng):
    d = numbers_of(rng)
    x = d["x"].astype(np.float32).reshape(N, 8, 16, C, 4)
    u = d["u"].reshape(N, 128, 128, 4)
    h, e, k = rng.permutation(8).tolist(), rng.permutation(N), np.arange(N)[:, None]
    x[:, :, :3] = 0
    x[:, :, 0, :, 0] = rng.integers(1, 8, (N, 8, C))
    x[:, h[0], 0, :, 0] = 1 + k
    x[:, h[1], 0, :, 0] = N - k
    x[:, :, 1, :, 0] = rng.integers(1, 16, (N, 8, C))
    x[:, :, 2, :, 0] = rng.integers(-1, 2, (N, 8, C))
    x[e[0], :, 2, :, 0] = 0
    x[e[1], :, 2, :, 0] = -1
    for i in range(3): u[:, :, i::16] = 0
    for g in range(8):
        i = 16 * g
        u[:, i + (0 if g in h[2:6] else 1), i, 0] = -1 if g in h[4:6] else 1
        u[:, i, i + 1, 0] = 1
        u[:, i + 2, i + 2, 0] = 1
    nb = rng.integers(0, C, (N, 8, R, C))
    for r in range(N):
        q = rng.permutation(8)
        nb[r, q[0]] = rng.integers(0, C)
        nb[r, q[1]] = np.arange(C)
        nb[r, q[2]] = C - 1 - np.arange(C)
        nb[r, q[3]] = (np.arange(C) + 1) % C
    nb = np.stack([gtable(nb[r].reshape(8, R * C)) for r in range(N)])
    return {"x": x.reshape(N, 128, 4 * C).astype(BF), "u": u.reshape(N, 128, 512), "v": d["v"], **weights(rng, [0, 1, 2]), "nb": nb}
def setup_inputs_spread(rng):
    d = setup_inputs(rng)
    d["x"] = wide(rng, N, 128, 4 * C, cols=6)
    return d
def check_inputs(d):
    b = []
    for k in ("x", "u", "v"):
        a = np.abs(d[k].astype(np.float32))
        if not (np.isfinite(a).all() and ((a == 0) | (a >= 2.0 ** -30) & (a <= 2.0 ** 30)).all()): b.append("a value of " + k)
    if ((d["wc"] & 0x7F) == 0x7F).any(): b.append("a code of wc that is no number")
    none, least, most = [emit(mx_ref.quantize(np.full((128, 16), k, np.float32).astype(BF)))[1][0, 0] for k in (0.0, 2.0 ** -30, 2.0 ** 30)]
    for r in range(N):
        s = mx_ref.live(d["ws"][r])
        if ((s != none) & ((s < least) | (s > most))).any(): b.append("a scale of ws")
    if (d["nb"] < 0).any() or (d["nb"] >= C).any(): b.append("an entry of nb")
    return b
def reference(x, u, v, wc, ws, nb):
    qu = [mx_ref.quantize(u[r]) for r in range(N)]
    lay = [pk(wc[r], ws[r]) for r in range(N)]
    now = [x[r] for r in range(N)]
    far = [gentries(nb[r]).reshape(8, R, C) for r in range(N)]
    guests = [np.zeros((128, 0), BF) for r in range(N)]
    place = np.arange(C)
    p = np.zeros((N, 8, C), np.int64) + place
    for t in range(R):
        sent = []
        for r in range(N):
            s = mx_ref.matmul(qu[r], mx_ref.quantize(now[r]))
            p[r] = np.where(s[2::16] < 0, place, p[r])
            sent.append(mx_ref.quantize(gcols(now[r], order(s)[:, :K])))
        came = decode(join(*sent)).astype(BF)
        for r in range(N):
            guests[r] = np.concatenate([guests[r], cut(came, (r - 1) % N, 4 * K)], axis=1)
            pool = np.concatenate([now[r], guests[r]], axis=1)
            cand = np.stack([p[r], np.take_along_axis(p[r], far[r][:, t], axis=1), np.zeros((8, C), np.int64) + C + K * t + place % K])
            met = [larger(now[r], gcols(pool, cand[k])) for k in range(3)]
            best = np.argmax(np.stack([mx_ref.matmul(qu[r], mx_ref.quantize(met[k]))[1::16] + np.float32(0.0) for k in range(3)]), axis=0)
            p[r] = np.take_along_axis(cand, best[None], axis=0)[0]
            q = mx_ref.quantize(gcols(np.concatenate(met, axis=1), best * C + place))
            now[r] = tile([np.maximum(mx_ref.matmul(pick(lay[r], np.arange(128 * b, 128 * b + 128)), q), np.float32(0.0)) * np.float32(0.015625) + now[r][:, b::4].astype(np.float32) for b in range(4)])
    y, op = np.zeros((N, 128, C), np.float32), np.zeros((N, 8, C), np.float32)
    oc, osc = np.zeros((N, 128, 4 * C), np.uint8), np.zeros((N, 16, C), np.uint8)
    for r in range(N):
        q = mx_ref.quantize(now[r])
        y[r] = mx_ref.matmul(mx_ref.quantize(v[r]), q)
        op[r] = p[r]
        oc[r], osc[r] = emit(q)
    return {"y": y, "op": op, "oc": oc, "osc": osc}

@@ -1,0 +1,480 @@
+from concourse.mybir import dt, AluOpType, ActivationFunctionType
+
+C, K, R = 224, 96, 3
+F32, BF, I32, U16, U8, X4 = "float32", "bfloat16", "int32", "uint16", "uint8", "float8_e4m3fn_x4"
+
+
+def _sb(n, d):
+    return ("sbuf", [128, n], d)
+
+
+SCRATCH = {
+    "pool": _sb(4 * C + 12 * K, BF), "ub": _sb(512, BF), "vb": _sb(512, BF), "nbi": _sb(42, I32), "nbo": _sb(42, U16),
+    "qu": _sb(128, X4), "su": _sb(128, U8), "qU": _sb(384, X4), "sU": _sb(384, U8),
+    "qv": _sb(128, X4), "sv": _sb(128, U8), "qw": _sb(512, X4), "sw": _sb(512, U8),
+    "pki": _sb(24, I32), "pko": _sb(24, U16), "i16": _sb(226, I32), "i4": _sb(226, I32), "pci": _sb(1, I32),
+    "d16": _sb(226, I32), "d4": _sb(226, I32), "b16": _sb(226, F32), "b4": _sb(226, F32), "a16": _sb(C, F32),
+    "c16": _sb(C, F32), "ctlS": _sb(C, F32), "seg": _sb(C, BF), "ctl16": _sb(C, F32), "ctl16b": _sb(2 * C, BF),
+    "ctl4": _sb(C, F32), "ctl4f": _sb(C, F32), "a0": _sb(4 * C, BF), "xc": _sb(4 * C, BF), "nrow": _sb(C, F32),
+    "m8i": _sb(8, I32), "m8": _sb(8, F32), "bd": _sb(512, BF), "qbd": _sb(128, X4), "sbd": _sb(128, U8),
+    "qti": _sb(2, I32), "qtf": _sb(2, F32), "col": _sb(10, F32), "base16": _sb(14, F32),
+    "eb": _sb(516, BF), "qe": _sb(512, X4), "se": _sb(512, U8),
+    "ms": _sb(C, F32), "xs": _sb(C, F32), "cmp": _sb(2560, BF), "qc": _sb(640, X4), "sc": _sb(640, U8),
+    "junk": _sb(1456, BF), "acc": _sb(14, F32), "ds": _sb(C, BF), "cs": _sb(C, F32), "t1": _sb(14, F32),
+    "rko": _sb(14, U16), "erow": _sb(C, F32), "es": _sb(K, F32),
+    "dd": _sb(4 * C, BF), "jw": _sb(1024 + 4 * C, BF), "zw": _sb(1024 + 4 * C, BF), "zz": _sb(4 * C, BF),
+    "qj0": _sb(C, X4), "sj0": _sb(C, U8), "qj1": _sb(C, X4), "sj1": _sb(C, U8), "qj2": _sb(C, X4), "sj2": _sb(C, U8),
+    "qz": _sb(C, X4), "sz": _sb(C, U8),
+    "pw0": _sb(4 * C, F32), "pw1": _sb(4 * C, F32), "pw2": _sb(3 * C, F32), "oprow": _sb(C, F32),
+    "ps0": _sb(C, F32), "ps1": _sb(C, F32), "po0": _sb(56, U16), "nb4": _sb(3 * 56, U16),
+    "s0": _sb(C, F32), "m01": _sb(C, F32), "f1": _sb(C, F32), "f2": _sb(C, F32), "fs1": _sb(C, F32), "fs2": _sb(C, F32),
+    "fo1": _sb(56, U16), "fo2": _sb(56, U16),
+    "sg": _sb(C, BF), "fl": _sb(2 * C, BF), "fl0": _sb(C, BF), "ll": _sb(2 * C, BF), "ll0": _sb(C, BF),
+    "w12": _sb(14, F32), "w3": _sb(14, F32), "w4": _sb(14, F32), "wo": _sb(14, U16),
+    "rl": _sb(4 * C, F32), "yb": _sb(C, F32),
+    "qx3": _sb(C, X4), "sx3": _sb(C, U8),
+    "ps": ("psum", [128, 4096], F32),
+}
+for _t in range(R):
+    for _p in ("x", "l", "r"):
+        SCRATCH["q%s%d" % (_p, _t)] = _sb(C, X4)
+        SCRATCH["s%s%d" % (_p, _t)] = _sb(C, U8)
+        SCRATCH["e%s%d" % (_p, _t)] = _sb(24, U16)
+
+NDMA = 16
+SEMAPHORES = ["cv", "ca", "ct", "cg", "sent"] + ["dma%d" % i for i in range(NDMA)] \
+    + ["aq%d" % t for t in range(R)] + ["ae%d" % t for t in range(R)]
+QSEM = {"v": "cv", "a": "ca", "t": "ct", "g": "cg"}
+H = 1.0e29
+
+
+def V(name, a=0, b=None, s=1):
+    if b is None:
+        b = SCRATCH[name][1][1]
+    return (name, a, b, s)
+
+
+def P(bank, n=C):
+    return ("ps", 512 * bank, 512 * bank + n, 1)
+
+
+def bits(v):
+    name, a, b, s = v
+    if name == "ps":
+        return 1 << (a // 512)
+    if s == 1:
+        return ((1 << (b - a)) - 1) << a
+    m = 0
+    for i in range(a, b, s):
+        m |= 1 << i
+    return m
+
+
+def emit(g, T, ops, tail):
+    eng = {"v": g.vector, "a": g.scalar, "t": g.tensor, "g": g, "s": g.sync}
+    hist = {}
+    for i, o in enumerate(ops):
+        deps = set()
+        acc = [(v, False) for v in o["r"]] + [(v, True) for v in o["w"]]
+        for v, wr in acc:
+            m = bits(v)
+            for j, mj, wj in hist.get(v[0], []):
+                if not (m & mj):
+                    continue
+                same = ops[j]["q"] == o["q"] and not ops[j]["dma"] and not o["dma"]
+                if v[0] == "ps":
+                    if not same:
+                        deps.add(j)
+                    elif wr and not o["acc"]:
+                        deps.add(j)
+                elif wr or wj:
+                    deps.add(j)
+        for v, wr in acc:
+            hist.setdefault(v[0], []).append((i, bits(v), wr))
+        o["deps"] = deps
+    known = {}
+    for i, o in enumerate(ops):
+        kq = known.setdefault(o["q"], set())
+        need = []
+        for j in sorted(o["deps"], reverse=True):
+            if j not in kq:
+                need.append(j)
+                kq |= ops[j]["done"]
+        o["need"] = need
+        o["done"] = set(kq) | {i}
+        for j in need:
+            ops[j]["inc"] = True
+    count = {q: 0 for q in QSEM}
+    ndma = 0
+    waited = {}
+    for o in ops:
+        e = eng[o["q"]]
+        want = {}
+        for j in o["need"]:
+            s, val = ops[j]["sig"]
+            want[s] = max(want.get(s, 0), val)
+        for s, val in o["ext"]:
+            want[s] = max(want.get(s, 0), val)
+        for s, val in want.items():
+            if waited.get((o["q"], s), 0) < val:
+                e.wait_ge(T.sem[s], val)
+                waited[(o["q"], s)] = val
+        ins = o["f"](e)
+        if o["dma"]:
+            s = "dma%d" % ndma
+            ndma += 1
+            ins.then_inc(T.sem[s], 16)
+            o["sig"] = (s, 16)
+        elif o["inc"]:
+            count[o["q"]] += 1
+            o["sig"] = (QSEM[o["q"]], count[o["q"]])
+            ins.then_inc(T.sem[QSEM[o["q"]]], 1)
+    for o in ops:
+        if o["dma"]:
+            s = o["sig"][0]
+            if not any(k[1] == s for k in waited):
+                eng[o["q"]].wait_ge(T.sem[s], 16)
+    for s, val in tail:
+        g.wait_ge(T.sem[s], val)
+
+
+def hop(src, dst, topo):
+    if topo.may_write(src, dst):
+        return dst
+    can = [c for c in topo.cores_of(src) if topo.may_write(c, dst)]
+    near = [c for c in can if topo.die(c) == topo.die(src)]
+    return (near or can)[0]
+
+
+def send(g, T, topo, src, dst, out, in_, sem):
+    rid, pid = topo.addr(dst, src)
+    g.remote_dma(out, in_, T.sem[sem], T.sem["sent"], pid, rid, topo.mask(src, dst))
+    return len(topo.engines(src, dst))
+
+
+def relay_program(g, core, T, topo, src, dst):
+    n_in = len(topo.engines(src, core))
+    total = 0
+    for t in range(R):
+        g.wait_ge(T.sem["aq%d" % t], 2 * n_in)
+        total += send(g, T, topo, core, dst, T["ql%d" % t][:].bitcast(dt.uint8), T["qr%d" % t][:].bitcast(dt.uint8), "aq%d" % t)
+        total += send(g, T, topo, core, dst, T["sl%d" % t][:], T["sr%d" % t][:], "aq%d" % t)
+        g.wait_ge(T.sem["ae%d" % t], n_in)
+        total += send(g, T, topo, core, dst, T["el%d" % t][:], T["er%d" % t][:], "ae%d" % t)
+    g.wait_ge(T.sem["sent"], total)
+
+
+def rank_program(g, core, T, topo):
+    cores = list(T.cores)
+    n = len(cores)
+    rank = T.rank_of(core)
+    if rank is None:
+        for i in range(n):
+            src, dst = cores[i], cores[(i + 1) % n]
+            if hop(src, dst, topo) == core:
+                relay_program(g, core, T, topo, src, dst)
+        return
+    nxt, prv = cores[(rank + 1) % n], cores[(rank - 1) % n]
+    to = hop(core, nxt, topo)
+    pre = "l" if to == nxt else "r"
+    last = hop(prv, core, topo)
+    n_in = len(topo.engines(prv if last == core else last, core))
+    n_out = len(topo.engines(core, to))
+
+    A, AF = AluOpType, ActivationFunctionType
+    ops = []
+
+    def ap(v):
+        name, a, b, s = v
+        return T[name][:, a:b] if s == 1 else T[name][:, a:b:s]
+
+    def op(q, f, r, w, dma=False, ext=(), acc=False):
+        ops.append({"q": q, "f": f, "r": list(r), "w": list(w), "dma": dma, "ext": list(ext), "acc": acc, "inc": False})
+
+    def isv(x):
+        return isinstance(x, tuple)
+
+    def val(x):
+        return ap(x) if isv(x) else x
+
+    def src(v, off):
+        return ap(v) if off is None else ap(v).indirect(ap(off))
+
+    def memset(o, c):
+        op("v", lambda e: e.memset(ap(o), c), [], [o])
+
+    def copy(o, i):
+        op("v", lambda e: e.tensor_copy(ap(o), ap(i)), [i], [o])
+
+    def gather(o, win, off):
+        op("v", lambda e: e.tensor_copy(ap(o), src(win, off)), [win, off], [o])
+
+    def scatter(win, off, i):
+        op("v", lambda e: e.tensor_copy(src(win, off), ap(i)), [i, off], [win])
+
+    def tt(o, a, b, f, off=None, ext=()):
+        op("v", lambda e: e.tensor_tensor(ap(o), src(a, off), ap(b), f), [a, b] + ([off] if off else []), [o], ext=ext)
+
+    def ts(o, a, s1, f1, s2=None, f2=None):
+        r = [a] + [x for x in (s1, s2) if isv(x)]
+        if f2 is None:
+            op("v", lambda e: e.tensor_scalar(ap(o), ap(a), val(s1), None, f1), r, [o])
+        else:
+            op("v", lambda e: e.tensor_scalar(ap(o), ap(a), val(s1), val(s2), f1, f2), r, [o])
+
+    def scan(o, d0, d1, init, f0, f1):
+        op("v", lambda e: e.tensor_tensor_scan(ap(o), ap(d0), ap(d1), init, f0, f1), [d0, d1], [o])
+
+    def quant(q, s, a, b, i):
+        op("v", lambda e: e.quantize_mx(T[q][:, a:b], T[s][:, a:b], ap(i)), [i], [V(q, a, b), V(s, a, b)])
+
+    def act(o, i, f, bias=0.0, scale=1.0, off=None, accum=None, ext=()):
+        r = [i] + ([bias] if isv(bias) else []) + ([off] if off else [])
+        if accum is not None:
+            op("a", lambda e: e.activation(ap(o), ap(i), f, bias=bias, accum_out=ap(accum)), r, [o, accum])
+        elif f == AF.Copy:
+            op("a", lambda e: e.activation(ap(o), src(i, off), f), r, [o], ext=ext)
+        else:
+            op("a", lambda e: e.activation(ap(o), ap(i), f, bias=val(bias), scale=scale), r, [o], ext=ext)
+
+    def mm(bank, wq, ws, wa, xq, xs, xa, xb, start=True, stop=True, ext=()):
+        o = P(bank, xb - xa)
+        op("t", lambda e: e.matmul_mx(ap(o), T[wq][:, wa:wa + 128], T[ws][:, wa:wa + 128], T[xq][:, xa:xb], T[xs][:, xa:xb], start, stop),
+           [V(wq, wa, wa + 128), V(ws, wa, wa + 128), V(xq, xa, xb), V(xs, xa, xb)], [o], ext=ext, acc=not start)
+
+    def iota(o, pattern, base, cm):
+        if SCRATCH[o[0]][2] == I32:
+            op("g", lambda e: e.iota(ap(o), pattern, base, cm), [], [o])
+        else:
+            op("g", lambda e: e.iota(ap(o), pattern, base, cm, allow_small_or_imprecise_dtypes=True), [], [o])
+
+    def dma(q, out, in_, r, w):
+        op(q, lambda e: e.dma_start(out, in_), r, w, dma=True)
+
+    def remote(kind, t):
+        i = V("%sx%d" % (kind, t))
+        o, s = T["%s%s%d" % (kind, pre, t)][:], T[i[0]][:]
+        if kind == "q":
+            o, s = o.bitcast(dt.uint8), s.bitcast(dt.uint8)
+        op("g", lambda e: send(e, T, topo, core, to, o, s, ("ae%d" if kind == "e" else "aq%d") % t), [i], [])
+
+    def pick(a, b):
+        c, d = a // 16, b // 16
+        op("v", lambda e: e.tensor_copy(T["qU"][:, a:b].bitcast(dt.uint32), T["qu"][:, 0:128].bitcast(dt.uint32).indirect(T["pko"][:, c:d])),
+           [V("qu"), V("pko", c, d)], [V("qU", a, b)])
+        act(V("sU", a, b), V("su"), AF.Copy, off=V("pko", c, d))
+
+    X = V("pool", 0, 4 * C)
+    IOTA = V("pw0", 0, C)
+    C1, C16, K4, C4, C4F, QB, K16, C0, END16 = [V("col", k, k + 1) for k in range(9)]
+    QF, TF = V("qtf", 0, 1), V("qtf", 1, 2)
+    TILE = [0, 224, 384, 512]
+
+    def slot(m, cnt):
+        k = 14 - m
+        a = 4 * TILE[k // 4] + k % 4
+        return V("cmp", a, a + 4 * (cnt - 1) + 1, 4)
+
+    def list4(o, row, tmp):
+        scan(tmp, row, V("ctl4"), 2048.0, A.min, A.add)
+        ts(o, (tmp[0], 3, C, 4), C4, A.add, 4.0, A.mult)
+
+    dma("a", T.ub[:], T.u[:], [], [V("ub")])
+    dma("s", T.pool[:, 0:4 * C], T.x[:], [], [X])
+    dma("s", T.nbi[:], T.nb[:], [], [V("nbi")])
+    dma("s", T.jw[:, 0:4 * C], T.x[:], [], [V("jw", 0, 4 * C)])
+    dma("s", T.qw[:].bitcast(dt.uint8), T.wc[:], [], [V("qw")])
+    dma("s", T.sw[:], T.ws[:], [], [V("sw")])
+    dma("s", T.vb[:], T.v[:], [], [V("vb")])
+    iota(V("i16"), [[1, 226]], 128, -1)
+    iota(V("pki"), [[1, 3], [16, 8]], 0, 0)
+    iota(V("i4"), [[4, 226]], 131, -1)
+    iota(V("pci"), [[1, 1]], 0, 1)
+    iota(IOTA, [[1, C]], 0, 0)
+    memset(V("ctlS"), 0.0)
+    memset(V("cmp", 4 * 432, 4 * 640), 0.0)
+    memset(V("ctlS", 0, C, 16), H)
+    ts(V("m8i"), V("i16", 15, 128, 16), 4, A.arith_shift_right)
+    ts(V("d16"), V("i16"), 15, A.bitwise_and)
+    ts(V("m8"), V("m8i"), 8.0, A.is_equal)
+    ts(V("b16"), V("d16"), 0.0, A.is_equal, -1024.0, A.mult)
+    copy(V("pko"), V("pki"))
+    memset(V("acc", 0, 1), 0.0)
+    ts(V("d4"), V("i4"), 2, A.arith_shift_right, 3, A.bitwise_and)
+    act(V("seg"), V("ctlS"), AF.Relu, bias=1.0, scale=-1.0)
+    for c in range(8):
+        act(V("bd", 64 * c, 64 * c + 64), V("ctlS", 1, 129, 2), AF.Identity, bias=V("m8", c, c + 1))
+    act(V("c16"), V("b16", 0, C), AF.Identity, bias=0.5 * H, scale=H / 1024.0)
+    memset(V("cmp", 4 * 176, 4 * 224), 0.0)
+    quant("qu", "su", 0, 128, V("ub"))
+    pick(0, 128)
+
+    for t in range(R):
+        qx, sx = "qx%d" % t, "sx%d" % t
+        pw = "pw%d" % t
+        win = V("pool", 0, 4 * C + 4 * K * t)
+        nb4 = V("nb4", 56 * t, 56 * t + 56)
+        quant(qx, sx, 0, C, X)
+        mm(0, "qU", "sU", 0, qx, sx, 0, C)
+        remote("q", t)
+        remote("s", t)
+        if t == 0:
+            ts(V("b4"), V("d4"), 0.0, A.is_equal, -1024.0, A.mult)
+            quant("qbd", "sbd", 0, 128, V("bd"))
+            act(V("ctl16"), V("b16", 1, C + 1), AF.Identity, bias=-1024.0, scale=-17.0)
+            act(V("ctl4"), V("b4", 1, C + 1), AF.Identity, bias=-1024.0, scale=-5.0)
+            act(END16, V("ctl16", 15, 16), AF.Copy)
+            iota(V("pw0", 2 * C, 2 * C + 2 * K), [[0, 2], [1, K]], C, 0)
+            iota(V("pw0", 2 * C + 2 * K, 3 * C), [[1, C - 2 * K]], C, 0)
+            iota(V("pw0", 3 * C, 4 * C), [[1, C]], 0, 0)
+        else:
+            mm(1, "qU", "sU", 256, qx, sx, 0, C)
+            list4(nb4, V("nrow"), V("ps1"))
+            act(V("sg"), P(1), AF.Sign)
+            act(V("fl0"), V("sg"), AF.Relu, scale=-3.0 * C)
+        tt(V("ms"), P(0), V("c16"), A.max)
+        if t == 0:
+            memset(V("cmp", 4 * 336, 4 * 384), 0.0)
+        scan(V("xs"), V("ctlS"), V("ms"), 0.0, A.add, A.min)
+        if t == 0:
+            ts(V("qti", 0, 1), V("pci"), 15, A.bitwise_and)
+        for m in range(13, 0, -1):
+            if m == 12:
+                tt(slot(14, C), P(0), V("xs"), A.is_gt)
+            ts(slot(m, 16 * m), P(0, 16 * m), V("xs", 16 * m + 15, 16 * m + 16), A.is_ge)
+            act(V("junk", 8 * m * (m - 1), 8 * m * (m + 1)), slot(m, 16 * m), AF.Identity, bias=-1.0, accum=V("acc", m, m + 1))
+            if m == 10:
+                quant("qc", "sc", 0, 224, V("cmp", 0, 896))
+                mm(2, "qbd", "sbd", 0, "qc", "sc", 0, 224, True, False)
+            if m == 6:
+                quant("qc", "sc", 224, 384, V("cmp", 896, 1536))
+                mm(2, "qbd", "sbd", 0, "qc", "sc", 224, 384, False, False)
+        scan(V("ds"), V("seg"), slot(14, C), 0.0, A.mult, A.add)
+        wide = 640 if t == 0 else 544
+        quant("qc", "sc", 384, wide, V("cmp", 1536, 4 * wide))
+        mm(2, "qbd", "sbd", 0, "qc", "sc", 384, 512, False, False)
+        mm(2, "qbd", "sbd", 0, "qc", "sc", 512, 640, False, True)
+        tt(V("t1"), V("acc"), V("ds", 15, C, 16), A.add)
+        if t == 0:
+            ts(V("qti", 1, 2), V("pci"), 3, A.bitwise_and)
+            ts(K16, V("d16", 0, 1), 1024.0, A.mult, V("b16", 0, 1), A.add)
+        else:
+            scan(V("ll0"), V("fl0"), V("ctl16b", 0, C), 2048.0, A.min, A.add)
+            act(V("xc"), X, AF.Copy)
+        ts(V("ctl16", 15, C, 16), V("t1"), -1.0, A.mult, END16, A.add)
+        if t == 0:
+            copy(V("qtf"), V("qti"))
+            ts(K4, V("d4", 0, 1), 1024.0, A.mult, V("b4", 0, 1), A.add)
+            act(C0, K16, AF.Identity, bias=208.0, scale=-1.0)
+            act(C1, QF, AF.Identity, bias=C0)
+            act(C4, TF, AF.Identity, bias=K4, scale=0.25)
+            act(C4F, QF, AF.Identity, bias=K4, scale=1.0 / 1024.0)
+        else:
+            tt(V("w3"), V("w12"), V("ll0", 15, C, 16), A.max)
+        scan(V("cs"), P(2), V("ctl16"), 2048.0, A.min, A.add)
+        if t > 0:
+            tt(V("w4"), V("w3"), V("base16"), A.add)
+        else:
+            copy(V("nbo"), V("nbi"))
+        ts(V("rko"), V("cs", 15, C, 16), -1.0, A.mult, C1, A.add)
+        if t > 0:
+            copy(V("wo"), V("w4"))
+            act(V(pw, 0, C), V("pw%d" % (t - 1)), AF.Copy, off=V("wo"))
+        act(V(pw, C, 2 * C), V(pw, 0, C), AF.Copy, off=V("nbo", 14 * t, 14 * t + 14))
+        scatter(V("erow"), V("rko"), IOTA)
+        scan(V("es"), V("erow", 0, K), V("ctl4", 0, K), 2048.0, A.min, A.add)
+        ts(V("ex%d" % t), V("es", 3, K, 4), C4, A.add, 4.0, A.mult)
+        remote("e", t)
+
+        if t == 0:
+            for u in (1, 2):
+                iota(V("pw%d" % u, 2 * C, 2 * C + 2 * K), [[0, 2], [1, K]], C + K * u, 0)
+                iota(V("pw%d" % u, 2 * C + 2 * K, 3 * C), [[1, C - 2 * K]], C + K * u, 0)
+            iota(V("pw1", 3 * C, 4 * C), [[1, C]], 0, 0)
+            memset(V("eb"), 0.0)
+            scan(V("ps1"), V(pw, C, 2 * C), V("ctl4"), 2048.0, A.min, A.add)
+            ts(V("eb", 3, 512, 4), V("i16", 0, 128), 128.0, A.is_equal)
+            ts(nb4, V("ps1", 3, C, 4), C4, A.add, 4.0, A.mult)
+            for b in range(4):
+                quant("qe", "se", 128 * b, 128 * b + 128, V("eb", 3 - b, 515 - b))
+            pick(128, 256)
+            act(V("ctl4f"), V("ctl4"), AF.Copy)
+            act(V("ctl4f", 3, C, 4), V("pw0", 0, C, 4), AF.Identity, bias=V("ctl4", 3, 4), scale=1.0 / 256.0)
+            near, same = X, V("jw", 0, 4 * C)
+        else:
+            list4(V("po0"), V(pw, 0, C), V("ps0"))
+            act(V("a0"), win, AF.Copy, off=V("po0"))
+            near, same = V("a0"), X
+        for b in range(4):
+            mm(4 + b, "qe", "se", 128 * b, "ql%d" % t, "sl%d" % t, 0, C, ext=[("aq%d" % t, 2 * n_in)])
+        if t == 0:
+            mm(3, "qU", "sU", 128, qx, sx, 0, C)
+        else:
+            tt(V("jw", 0, 4 * C), win, V("xc"), A.max, off=V("po0"))
+            quant("qj0", "sj0", 0, C, V("jw", 0, 4 * C))
+            mm(3, "qU", "sU", 128, "qj0", "sj0", 0, C)
+        for b in range(4):
+            act(V("dd", b, 4 * C, 4), P(4 + b), AF.Copy)
+        act(V("s0"), P(3), AF.Copy)
+        tt(V("jw", 1024, 1024 + 4 * C), near, same, A.max, off=nb4)
+        quant("qj1", "sj1", 0, C, V("jw", 1024, 1024 + 4 * C))
+        mm(1, "qU", "sU", 128, "qj1", "sj1", 0, C)
+        if t == 0:
+            memset(V("jw", 4 * C, 1024), 0.0)
+            memset(V("zw", 4 * C, 1024), 0.0)
+            act(V("a16"), V("b16", 1, C + 1), AF.Identity, scale=-2.0)
+            pick(256, 384)
+        if t == 1:
+            quant("qv", "sv", 0, 128, V("vb"))
+        tt(V("f1"), P(1), V("s0"), A.is_gt)
+        scan(V("fs1"), V("f1"), V("ctl4f"), 2048.0, A.min, A.add)
+        ts(V("fo1"), V("fs1", 3, C, 4), C4F, A.add, 1024.0, A.mult)
+        if t == 0:
+            tt(V("ctl16b", 0, C), V("a16"), V("b16", 0, C), A.add)
+
+        el, got = "el%d" % t, [("ae%d" % t, n_in)]
+        gs = 4 * C + 4 * K * t
+        act(V("pool", gs, gs + 4 * K), V("dd"), AF.Copy, off=V(el), ext=got)
+        act(V("zw", 0, 4 * C), V("jw"), AF.Copy, off=V("fo1"))
+        tt(V("zw", 1024, 1024 + 4 * K), V("dd"), V("pool", 0, 4 * K), A.max, off=V(el), ext=got)
+        for a, b in ((K, 2 * K), (2 * K, C)):
+            tt(V("zw", 1024 + 4 * a, 1024 + 4 * b), V("pool", gs, gs + 4 * (b - a)), V("pool", 4 * a, 4 * b), A.max)
+        quant("qj2", "sj2", 0, C, V("zw", 1024, 1024 + 4 * C))
+        mm(3, "qU", "sU", 128, "qj2", "sj2", 0, C)
+        tt(V("m01"), P(1), V("s0"), A.max)
+        tt(V("f2"), P(3), V("m01"), A.is_gt)
+        scan(V("fs2"), V("f2"), V("ctl4f"), 2048.0, A.min, A.add)
+        act(V("fl", 0, C), V("f1"), AF.Identity, scale=float(C))
+        ts(V("fo2"), V("fs2", 3, C, 4), C4F, A.add, 1024.0, A.mult)
+        act(V("zz", 2 * C, 4 * C), V("zw"), AF.Copy, off=V("fo2", 28, 56))
+        gather(V("zz", 0, 2 * C), V("zw"), V("fo2", 0, 28))
+        act(V("fl", C, 2 * C), V("f2"), AF.Identity, scale=2.0 * C)
+        if t == 0:
+            act(V("ctl16b", C, 2 * C), V("ctl16b", 0, C), AF.Copy)
+        quant("qz", "sz", 0, C, V("zz"))
+        for b in range(4):
+            mm(4 + b, "qw", "sw", 128 * b, "qz", "sz", 0, C)
+        scan(V("ll"), V("fl"), V("ctl16b"), 2048.0, A.min, A.add)
+        tt(V("w12"), V("ll", 15, C, 16), V("ll", C + 15, 2 * C, 16), A.max)
+        for b in range(4):
+            act(V("rl", C * b, C * b + C), P(4 + b), AF.Relu, scale=0.015625)
+            tt(V("pool", b, 4 * C, 4), V("rl", C * b, C * b + C), V("pool", b, 4 * C, 4), A.add)
+        if t < R - 1:
+            act(V("nrow"), IOTA, AF.Copy, off=V("nbo", 14 * t + 14, 14 * t + 28))
+        if t == 0:
+            act(C16, V("b16", 0, 1), AF.Identity, bias=1024.0, scale=2.0)
+            act(QB, QF, AF.Identity, bias=C16)
+            act(V("base16"), V("pw0", 0, C, 16), AF.Identity, bias=QB)
+
+    quant("qx3", "sx3", 0, C, X)
+    mm(0, "qv", "sv", 0, "qx3", "sx3", 0, C)
+    dma("s", T.oc[:], T.qx3[:].bitcast(dt.uint8), [V("qx3")], [])
+    for k in range(4):
+        dma("a" if k < 2 else "s", T.osc[4 * k:4 * k + 4, :], T.sx3[32 * k:32 * k + 4, :], [V("sx3")], [])
+    tt(V("w4"), V("w12"), V("base16"), A.add)
+    copy(V("wo"), V("w4"))
+    act(V("oprow"), V("pw2"), AF.Copy, off=V("wo"))
+    copy(V("yb"), P(0))
+    dma("s", T.y[:], T.yb[:], [V("yb")], [])
+    dma("a", T.op[:], T.oprow[0:128:16, :], [V("oprow")], [])
+    emit(g, T, ops, [("sent", 3 * R * n_out)])

@@ -15,7 +15,7 @@ SCRATCH = {
     "pki": _sb(24, I32), "pko": _sb(24, U16), "i16": _sb(226, I32), "i4": _sb(226, I32), "pci": _sb(1, I32),
     "d16": _sb(226, I32), "d4": _sb(226, I32), "b16": _sb(226, F32), "b4": _sb(226, F32), "a16": _sb(C, F32),
     "c16": _sb(C, F32), "ctlS": _sb(C, F32), "seg": _sb(C, BF), "ctl16": _sb(C, F32), "ctl16b": _sb(2 * C, BF),
-    "ctl4": _sb(C, F32), "ctl4f": _sb(C, F32), "a0": _sb(4 * C, BF), "xc": _sb(4 * C, BF), "nrow": _sb(C, F32),
+    "ctl4": _sb(C, F32), "ctl4f": _sb(C, F32), "a0": _sb(4 * C, BF), "a1": _sb(4 * C, BF), "nrow": _sb(C, F32),
     "m8i": _sb(8, I32), "m8": _sb(8, F32), "bd": _sb(512, BF), "qbd": _sb(128, X4), "sbd": _sb(128, U8),
     "qti": _sb(2, I32), "qtf": _sb(2, F32), "col": _sb(10, F32), "base16": _sb(14, F32),
     "eb": _sb(516, BF), "qe": _sb(512, X4), "se": _sb(512, U8),
@@ -46,6 +46,7 @@ SEMAPHORES = ["cv", "ca", "ct", "cg", "sent"] + ["dma%d" % i for i in range(NDMA
     + ["aq%d" % t for t in range(R)] + ["ae%d" % t for t in range(R)]
 QSEM = {"v": "cv", "a": "ca", "t": "ct", "g": "cg"}
 H = 1.0e29
+HALF = [(0, C // 2), (C // 2, C)]
 
 
 def V(name, a=0, b=None, s=1):
@@ -138,29 +139,42 @@ def emit(g, T, ops, tail):
         g.wait_ge(T.sem[s], val)
 
 
-def hop(src, dst, topo):
+def helpers(src, dst, topo):
     if topo.may_write(src, dst):
-        return dst
+        return None
     can = [c for c in topo.cores_of(src) if topo.may_write(c, dst)]
     near = [c for c in can if topo.die(c) == topo.die(src)]
-    return (near or can)[0]
+    far = [c for c in can if topo.die(c) != topo.die(src)]
+    return [near[0], near[1], far[0]]
 
 
-def send(g, T, topo, src, dst, out, in_, sem):
+def send(g, T, topo, src, dst, out, in_, sem, part=None):
     rid, pid = topo.addr(dst, src)
-    g.remote_dma(out, in_, T.sem[sem], T.sem["sent"], pid, rid, topo.mask(src, dst))
-    return len(topo.engines(src, dst))
+    use = topo.engines(src, dst)
+    if part is not None:
+        h = len(use) // 2
+        use = use[h * part:h * part + h]
+    g.remote_dma(out, in_, T.sem[sem], T.sem["sent"], pid, rid, sum(1 << e for e in use))
+    return len(use)
 
 
-def relay_program(g, core, T, topo, src, dst):
+def codes(T, name, a=0, b=C):
+    return T[name][:, a:b].bitcast(dt.uint8)
+
+
+def relay_program(g, core, T, topo, src, dst, role):
     n_in = len(topo.engines(src, core))
     total = 0
     for t in range(R):
-        g.wait_ge(T.sem["aq%d" % t], 2 * n_in)
-        total += send(g, T, topo, core, dst, T["ql%d" % t][:].bitcast(dt.uint8), T["qr%d" % t][:].bitcast(dt.uint8), "aq%d" % t)
-        total += send(g, T, topo, core, dst, T["sl%d" % t][:], T["sr%d" % t][:], "aq%d" % t)
-        g.wait_ge(T.sem["ae%d" % t], n_in)
-        total += send(g, T, topo, core, dst, T["el%d" % t][:], T["er%d" % t][:], "ae%d" % t)
+        if role == 0:
+            g.wait_ge(T.sem["aq%d" % t], n_in)
+            total += send(g, T, topo, core, dst, T["sl%d" % t][:], T["sr%d" % t][:], "aq%d" % t)
+            g.wait_ge(T.sem["ae%d" % t], n_in)
+            total += send(g, T, topo, core, dst, T["el%d" % t][:], T["er%d" % t][:], "ae%d" % t)
+        else:
+            a, b = HALF[role - 1]
+            g.wait_ge(T.sem["aq%d" % t], n_in // 2)
+            total += send(g, T, topo, core, dst, codes(T, "ql%d" % t, a, b), codes(T, "qr%d" % t, a, b), "aq%d" % t)
     g.wait_ge(T.sem["sent"], total)
 
 
@@ -171,15 +185,19 @@ def rank_program(g, core, T, topo):
     if rank is None:
         for i in range(n):
             src, dst = cores[i], cores[(i + 1) % n]
-            if hop(src, dst, topo) == core:
-                relay_program(g, core, T, topo, src, dst)
+            via = helpers(src, dst, topo)
+            if via and core in via:
+                relay_program(g, core, T, topo, src, dst, via.index(core))
         return
     nxt, prv = cores[(rank + 1) % n], cores[(rank - 1) % n]
-    to = hop(core, nxt, topo)
-    pre = "l" if to == nxt else "r"
-    last = hop(prv, core, topo)
-    n_in = len(topo.engines(prv if last == core else last, core))
-    n_out = len(topo.engines(core, to))
+    via, came = helpers(core, nxt, topo), helpers(prv, core, topo)
+    if came:
+        n_list = len(topo.engines(came[0], core))
+        n_tile = sum(len(topo.engines(c, core)) for c in came)
+    else:
+        n_list = len(topo.engines(prv, core))
+        n_tile = 2 * n_list
+    n_out = len(topo.engines(core, via[0] if via else nxt))
 
     A, AF = AluOpType, ActivationFunctionType
     ops = []
@@ -231,7 +249,7 @@ def rank_program(g, core, T, topo):
     def act(o, i, f, bias=0.0, scale=1.0, off=None, accum=None, ext=()):
         r = [i] + ([bias] if isv(bias) else []) + ([off] if off else [])
         if accum is not None:
-            op("a", lambda e: e.activation(ap(o), ap(i), f, bias=bias, accum_out=ap(accum)), r, [o, accum])
+            op("a", lambda e: e.activation(ap(o), ap(i), f, bias=bias, scale=scale, accum_out=ap(accum)), r, [o, accum])
         elif f == AF.Copy:
             op("a", lambda e: e.activation(ap(o), src(i, off), f), r, [o], ext=ext)
         else:
@@ -252,11 +270,16 @@ def rank_program(g, core, T, topo):
         op(q, lambda e: e.dma_start(out, in_), r, w, dma=True)
 
     def remote(kind, t):
-        i = V("%sx%d" % (kind, t))
-        o, s = T["%s%s%d" % (kind, pre, t)][:], T[i[0]][:]
-        if kind == "q":
-            o, s = o.bitcast(dt.uint8), s.bitcast(dt.uint8)
-        op("g", lambda e: send(e, T, topo, core, to, o, s, ("ae%d" if kind == "e" else "aq%d") % t), [i], [])
+        name, sem = "%sx%d" % (kind, t), ("ae%d" if kind == "e" else "aq%d") % t
+        there = "%s%s%d" % (kind, "r" if via else "l", t)
+        if kind != "q":
+            op("g", lambda e: send(e, T, topo, core, via[0] if via else nxt, T[there][:], T[name][:], sem), [V(name)], [])
+        elif via:
+            for k in (1, 0):
+                a, b = HALF[k]
+                op("g", lambda e, k=k, a=a, b=b: send(e, T, topo, core, via[1 + k], codes(T, there, a, b), codes(T, name, a, b), sem, k), [V(name)], [])
+        else:
+            op("g", lambda e: send(e, T, topo, core, nxt, codes(T, there), codes(T, name), sem), [V(name)], [])
 
     def pick(a, b):
         c, d = a // 16, b // 16
@@ -275,17 +298,15 @@ def rank_program(g, core, T, topo):
         a = 4 * TILE[k // 4] + k % 4
         return V("cmp", a, a + 4 * (cnt - 1) + 1, 4)
 
-    def list4(o, row, tmp):
-        scan(tmp, row, V("ctl4"), 2048.0, A.min, A.add)
-        ts(o, (tmp[0], 3, C, 4), C4, A.add, 4.0, A.mult)
+    def held4(tmp, row):
+        scan(tmp, row, V("ctl4", 0, row[2] - row[1]), 2048.0, A.min, A.add)
+
+    def list4(o, tmp):
+        ts(o, (tmp[0], 3, tmp[2], 4), C4, A.add, 4.0, A.mult)
 
     dma("a", T.ub[:], T.u[:], [], [V("ub")])
     dma("s", T.pool[:, 0:4 * C], T.x[:], [], [X])
     dma("s", T.nbi[:], T.nb[:], [], [V("nbi")])
-    dma("s", T.jw[:, 0:4 * C], T.x[:], [], [V("jw", 0, 4 * C)])
-    dma("s", T.qw[:].bitcast(dt.uint8), T.wc[:], [], [V("qw")])
-    dma("s", T.sw[:], T.ws[:], [], [V("sw")])
-    dma("s", T.vb[:], T.v[:], [], [V("vb")])
     iota(V("i16"), [[1, 226]], 128, -1)
     iota(V("pki"), [[1, 3], [16, 8]], 0, 0)
     iota(V("i4"), [[4, 226]], 131, -1)
@@ -327,9 +348,14 @@ def rank_program(g, core, T, topo):
             iota(V("pw0", 2 * C, 2 * C + 2 * K), [[0, 2], [1, K]], C, 0)
             iota(V("pw0", 2 * C + 2 * K, 3 * C), [[1, C - 2 * K]], C, 0)
             iota(V("pw0", 3 * C, 4 * C), [[1, C]], 0, 0)
+            dma("s", T.jw[:, 0:4 * C], T.x[:], [V(sx)], [V("jw", 0, 4 * C)])
+            dma("s", T.qw[:].bitcast(dt.uint8), T.wc[:], [], [V("qw")])
+            dma("s", T.sw[:], T.ws[:], [], [V("sw")])
+            dma("s", T.vb[:], T.v[:], [], [V("vb")])
         else:
             mm(1, "qU", "sU", 256, qx, sx, 0, C)
-            list4(nb4, V("nrow"), V("ps1"))
+            held4(V("ps1"), V("nrow"))
+            list4(nb4, V("ps1"))
             act(V("sg"), P(1), AF.Sign)
             act(V("fl0"), V("sg"), AF.Relu, scale=-3.0 * C)
         tt(V("ms"), P(0), V("c16"), A.max)
@@ -338,32 +364,33 @@ def rank_program(g, core, T, topo):
         scan(V("xs"), V("ctlS"), V("ms"), 0.0, A.add, A.min)
         if t == 0:
             ts(V("qti", 0, 1), V("pci"), 15, A.bitwise_and)
-        for m in range(13, 0, -1):
+        for m in (13, 12, 11, 10, 9, 8, 7, 6, 5, 4, 3, 2, 1):
             if m == 12:
                 tt(slot(14, C), P(0), V("xs"), A.is_gt)
             ts(slot(m, 16 * m), P(0, 16 * m), V("xs", 16 * m + 15, 16 * m + 16), A.is_ge)
-            act(V("junk", 8 * m * (m - 1), 8 * m * (m + 1)), slot(m, 16 * m), AF.Identity, bias=-1.0, accum=V("acc", m, m + 1))
+            act(V("junk", 8 * m * (m - 1), 8 * m * (m + 1)), slot(m, 16 * m), AF.Identity, bias=1.0, scale=-1.0, accum=V("acc", m, m + 1))
             if m == 10:
                 quant("qc", "sc", 0, 224, V("cmp", 0, 896))
                 mm(2, "qbd", "sbd", 0, "qc", "sc", 0, 224, True, False)
             if m == 6:
                 quant("qc", "sc", 224, 384, V("cmp", 896, 1536))
                 mm(2, "qbd", "sbd", 0, "qc", "sc", 224, 384, False, False)
-        scan(V("ds"), V("seg"), slot(14, C), 0.0, A.mult, A.add)
+        if t > 0:
+            scan(V("ll0"), V("fl0"), V("ctl16b", 0, C), 2048.0, A.min, A.add)
+        else:
+            copy(V("nbo"), V("nbi"))
         wide = 640 if t == 0 else 544
         quant("qc", "sc", 384, wide, V("cmp", 1536, 4 * wide))
         mm(2, "qbd", "sbd", 0, "qc", "sc", 384, 512, False, False)
         mm(2, "qbd", "sbd", 0, "qc", "sc", 512, 640, False, True)
-        tt(V("t1"), V("acc"), V("ds", 15, C, 16), A.add)
         if t == 0:
+            act(V(pw, C, 2 * C), V(pw, 0, C), AF.Copy, off=V("nbo", 0, 14))
             ts(V("qti", 1, 2), V("pci"), 3, A.bitwise_and)
+            scan(V("ds"), V("seg"), slot(14, C), 0.0, A.mult, A.add)
             ts(K16, V("d16", 0, 1), 1024.0, A.mult, V("b16", 0, 1), A.add)
-        else:
-            scan(V("ll0"), V("fl0"), V("ctl16b", 0, C), 2048.0, A.min, A.add)
-            act(V("xc"), X, AF.Copy)
-        ts(V("ctl16", 15, C, 16), V("t1"), -1.0, A.mult, END16, A.add)
-        if t == 0:
+            tt(V("t1"), V("acc"), V("ds", 15, C, 16), A.subtract)
             copy(V("qtf"), V("qti"))
+            ts(V("ctl16", 15, C, 16), V("t1"), END16, A.add)
             ts(K4, V("d4", 0, 1), 1024.0, A.mult, V("b4", 0, 1), A.add)
             act(C0, K16, AF.Identity, bias=208.0, scale=-1.0)
             act(C1, QF, AF.Identity, bias=C0)
@@ -371,19 +398,26 @@ def rank_program(g, core, T, topo):
             act(C4F, QF, AF.Identity, bias=K4, scale=1.0 / 1024.0)
         else:
             tt(V("w3"), V("w12"), V("ll0", 15, C, 16), A.max)
-        scan(V("cs"), P(2), V("ctl16"), 2048.0, A.min, A.add)
-        if t > 0:
+            scan(V("ds"), V("seg"), slot(14, C), 0.0, A.mult, A.add)
             tt(V("w4"), V("w3"), V("base16"), A.add)
-        else:
-            copy(V("nbo"), V("nbi"))
-        ts(V("rko"), V("cs", 15, C, 16), -1.0, A.mult, C1, A.add)
-        if t > 0:
+            tt(V("t1"), V("acc"), V("ds", 15, C, 16), A.subtract)
             copy(V("wo"), V("w4"))
             act(V(pw, 0, C), V("pw%d" % (t - 1)), AF.Copy, off=V("wo"))
-        act(V(pw, C, 2 * C), V(pw, 0, C), AF.Copy, off=V("nbo", 14 * t, 14 * t + 14))
+            ts(V("ctl16", 15, C, 16), V("t1"), END16, A.add)
+        scan(V("cs"), P(2), V("ctl16"), 2048.0, A.min, A.add)
+        ts(V("rko"), V("cs", 15, C, 16), -1.0, A.mult, C1, A.add)
+        if t > 0:
+            held4(V("ps0"), V(pw, 0, C))
+            list4(V("po0"), V("ps0"))
+            act(V("a0"), win, AF.Copy, off=V("po0"))
+            act(V("a1"), V("a0"), AF.Copy, off=nb4)
+        else:
+            held4(V("ps1"), V(pw, C, 2 * C))
+            list4(nb4, V("ps1"))
+            act(V("a1"), X, AF.Copy, off=nb4)
         scatter(V("erow"), V("rko"), IOTA)
-        scan(V("es"), V("erow", 0, K), V("ctl4", 0, K), 2048.0, A.min, A.add)
-        ts(V("ex%d" % t), V("es", 3, K, 4), C4, A.add, 4.0, A.mult)
+        held4(V("es"), V("erow", 0, K))
+        list4(V("ex%d" % t), V("es"))
         remote("e", t)
 
         if t == 0:
@@ -392,35 +426,26 @@ def rank_program(g, core, T, topo):
                 iota(V("pw%d" % u, 2 * C + 2 * K, 3 * C), [[1, C - 2 * K]], C + K * u, 0)
             iota(V("pw1", 3 * C, 4 * C), [[1, C]], 0, 0)
             memset(V("eb"), 0.0)
-            scan(V("ps1"), V(pw, C, 2 * C), V("ctl4"), 2048.0, A.min, A.add)
-            ts(V("eb", 3, 512, 4), V("i16", 0, 128), 128.0, A.is_equal)
-            ts(nb4, V("ps1", 3, C, 4), C4, A.add, 4.0, A.mult)
-            for b in range(4):
-                quant("qe", "se", 128 * b, 128 * b + 128, V("eb", 3 - b, 515 - b))
             pick(128, 256)
+            ts(V("eb", 3, 512, 4), V("i16", 0, 128), 128.0, A.is_equal)
+            mm(3, "qU", "sU", 128, qx, sx, 0, C)
             act(V("ctl4f"), V("ctl4"), AF.Copy)
             act(V("ctl4f", 3, C, 4), V("pw0", 0, C, 4), AF.Identity, bias=V("ctl4", 3, 4), scale=1.0 / 256.0)
-            near, same = X, V("jw", 0, 4 * C)
+            memset(V("jw", 4 * C, 1024), 0.0)
+            for b in range(4):
+                quant("qe", "se", 128 * b, 128 * b + 128, V("eb", 3 - b, 515 - b))
         else:
-            list4(V("po0"), V(pw, 0, C), V("ps0"))
-            act(V("a0"), win, AF.Copy, off=V("po0"))
-            near, same = V("a0"), X
-        for b in range(4):
-            mm(4 + b, "qe", "se", 128 * b, "ql%d" % t, "sl%d" % t, 0, C, ext=[("aq%d" % t, 2 * n_in)])
-        if t == 0:
-            mm(3, "qU", "sU", 128, qx, sx, 0, C)
-        else:
-            tt(V("jw", 0, 4 * C), win, V("xc"), A.max, off=V("po0"))
+            tt(V("jw", 0, 4 * C), V("a0"), X, A.max)
             quant("qj0", "sj0", 0, C, V("jw", 0, 4 * C))
             mm(3, "qU", "sU", 128, "qj0", "sj0", 0, C)
-        for b in range(4):
-            act(V("dd", b, 4 * C, 4), P(4 + b), AF.Copy)
         act(V("s0"), P(3), AF.Copy)
-        tt(V("jw", 1024, 1024 + 4 * C), near, same, A.max, off=nb4)
+        for b in range(4):
+            mm(4 + b, "qe", "se", 128 * b, "ql%d" % t, "sl%d" % t, 0, C, ext=[("aq%d" % t, n_tile)])
+            act(V("dd", b, 4 * C, 4), P(4 + b), AF.Copy)
+        tt(V("jw", 1024, 1024 + 4 * C), V("a1"), X, A.max)
         quant("qj1", "sj1", 0, C, V("jw", 1024, 1024 + 4 * C))
         mm(1, "qU", "sU", 128, "qj1", "sj1", 0, C)
         if t == 0:
-            memset(V("jw", 4 * C, 1024), 0.0)
             memset(V("zw", 4 * C, 1024), 0.0)
             act(V("a16"), V("b16", 1, C + 1), AF.Identity, scale=-2.0)
             pick(256, 384)
@@ -432,7 +457,7 @@ def rank_program(g, core, T, topo):
         if t == 0:
             tt(V("ctl16b", 0, C), V("a16"), V("b16", 0, C), A.add)
 
-        el, got = "el%d" % t, [("ae%d" % t, n_in)]
+        el, got = "el%d" % t, [("ae%d" % t, n_list)]
         gs = 4 * C + 4 * K * t
         act(V("pool", gs, gs + 4 * K), V("dd"), AF.Copy, off=V(el), ext=got)
         act(V("zw", 0, 4 * C), V("jw"), AF.Copy, off=V("fo1"))
@@ -461,6 +486,8 @@ def rank_program(g, core, T, topo):
             tt(V("pool", b, 4 * C, 4), V("rl", C * b, C * b + C), V("pool", b, 4 * C, 4), A.add)
         if t < R - 1:
             act(V("nrow"), IOTA, AF.Copy, off=V("nbo", 14 * t + 14, 14 * t + 28))
+        if t > 0:
+            act(V(pw, C, 2 * C), V(pw, 0, C), AF.Copy, off=V("nbo", 14 * t, 14 * t + 14))
         if t == 0:
             act(C16, V("b16", 0, 1), AF.Identity, bias=1024.0, scale=2.0)
             act(QB, QF, AF.Identity, bias=C16)

@@ -1,6 +1,8 @@
 from concourse.mybir import dt, AluOpType, ActivationFunctionType
 
 C, K, R = 224, 96, 3
+CA = 128
+CB = C - 128
 F32, BF, I32, U16, U8, X4 = "float32", "bfloat16", "int32", "uint16", "uint8", "float8_e4m3fn_x4"
 
 
@@ -10,43 +12,44 @@ def _sb(n, d):
 
 SCRATCH = {
     "pool": _sb(4 * C + 12 * K, BF), "ub": _sb(512, BF), "vb": _sb(512, BF), "nbi": _sb(42, I32), "nbo": _sb(42, U16),
+    "nbd": ("dram", [8, 4, 4, 42], I32), "nbt": _sb(168, I32), "nb4": _sb(168, U16),
     "qu": _sb(128, X4), "su": _sb(128, U8), "qU": _sb(384, X4), "sU": _sb(384, U8),
     "qv": _sb(128, X4), "sv": _sb(128, U8), "qw": _sb(512, X4), "sw": _sb(512, U8),
-    "pki": _sb(24, I32), "pko": _sb(24, U16), "i16": _sb(226, I32), "i4": _sb(226, I32), "pci": _sb(1, I32),
-    "d16": _sb(226, I32), "d4": _sb(226, I32), "b16": _sb(226, F32), "b4": _sb(226, F32), "a16": _sb(C, F32),
-    "c16": _sb(C, F32), "ctlS": _sb(C, F32), "seg": _sb(C, BF), "ctl16": _sb(C, F32), "ctl16b": _sb(2 * C, BF),
-    "ctl4": _sb(C, F32), "ctl4f": _sb(C, F32), "a0": _sb(4 * C, BF), "a1": _sb(4 * C, BF), "nrow": _sb(C, F32),
-    "m8i": _sb(8, I32), "m8": _sb(8, F32), "bd": _sb(512, BF), "qbd": _sb(128, X4), "sbd": _sb(128, U8),
-    "qti": _sb(2, I32), "qtf": _sb(2, F32), "col": _sb(10, F32), "base16": _sb(14, F32),
+    "pki": _sb(24, I32), "pko": _sb(24, U16), "qti": _sb(5, I32), "qtf": _sb(5, F32), "r16": _sb(240, BF),
+    "c16": _sb(C + 1, F32), "ctlS": _sb(C, F32), "seg": _sb(C, BF), "ctl16": _sb(C, F32), "ctl4": _sb(C, F32),
+    "ctlA": _sb(C, BF), "ctlB": _sb(C, BF), "ctlX": _sb(C, BF), "ctlP0": _sb(C, BF), "ctlP1": _sb(C, BF),
+    "e4": _sb(4, F32), "m4": _sb(4, F32), "k4": _sb(4, F32), "kk4": _sb(4, F32), "o2": _sb(16, F32), "o5": _sb(16, F32),
+    "a0": _sb(4 * C, BF), "a1": _sb(4 * C, BF),
+    "m8": _sb(8, F32), "bd": _sb(512, BF), "qbd": _sb(128, X4), "sbd": _sb(128, U8), "col": _sb(16, F32),
     "eb": _sb(516, BF), "qe": _sb(512, X4), "se": _sb(512, U8),
     "ms": _sb(C, F32), "xs": _sb(C, F32), "cmp": _sb(2560, BF), "qc": _sb(640, X4), "sc": _sb(640, U8),
     "junk": _sb(1456, BF), "acc": _sb(14, F32), "ds": _sb(C, BF), "cs": _sb(C, F32), "t1": _sb(14, F32),
     "rko": _sb(14, U16), "erow": _sb(C, F32), "es": _sb(K, F32),
-    "dd": _sb(4 * C, BF), "jw": _sb(1024 + 4 * C, BF), "zw": _sb(1024 + 4 * C, BF), "zz": _sb(4 * C, BF),
-    "qj0": _sb(C, X4), "sj0": _sb(C, U8), "qj1": _sb(C, X4), "sj1": _sb(C, U8), "qj2": _sb(C, X4), "sj2": _sb(C, U8),
-    "qz": _sb(C, X4), "sz": _sb(C, U8),
-    "pw0": _sb(4 * C, F32), "pw1": _sb(4 * C, F32), "pw2": _sb(3 * C, F32), "oprow": _sb(C, F32),
-    "ps0": _sb(C, F32), "ps1": _sb(C, F32), "po0": _sb(56, U16), "nb4": _sb(3 * 56, U16),
-    "s0": _sb(C, F32), "m01": _sb(C, F32), "f1": _sb(C, F32), "f2": _sb(C, F32), "fs1": _sb(C, F32), "fs2": _sb(C, F32),
-    "fo1": _sb(56, U16), "fo2": _sb(56, U16),
-    "sg": _sb(C, BF), "fl": _sb(2 * C, BF), "fl0": _sb(C, BF), "ll": _sb(2 * C, BF), "ll0": _sb(C, BF),
-    "w12": _sb(14, F32), "w3": _sb(14, F32), "w4": _sb(14, F32), "wo": _sb(14, U16),
+    "dd": _sb(4 * C, BF), "zw": _sb(2048 + 4 * C, BF), "zz": _sb(4 * C, BF),
+    "qj0": _sb(C, X4), "sj0": _sb(C, U8), "qj1": _sb(C, X4), "sj1": _sb(C, U8),
+    "qj2": _sb(256, X4), "sj2": _sb(256, U8), "qz": _sb(256, X4), "sz": _sb(256, U8),
+    "pw0": _sb(1280, F32), "pw1": _sb(1280, F32), "pw2": _sb(1280, F32), "oprow": _sb(C, F32),
+    "ps0": _sb(C, F32), "po0": _sb(56, U16),
+    "s0": _sb(C, F32), "m01": _sb(C, F32), "f1": _sb(C, BF), "f2": _sb(C, BF), "h1": _sb(C, BF), "h2": _sb(C, BF),
+    "h1h": _sb(56, F32), "hm": _sb(56, F32), "fo": _sb(56, U16),
+    "sg": _sb(C, BF), "f0": _sb(C, BF), "l0": _sb(C, BF), "l1": _sb(C, BF), "l12": _sb(C, BF),
+    "wm": _sb(14, F32), "wo": _sb(14, U16),
     "rl": _sb(4 * C, F32), "yb": _sb(C, F32),
-    "qx3": _sb(C, X4), "sx3": _sb(C, U8),
+    "qx3": _sb(256, X4), "sx3": _sb(256, U8),
     "ps": ("psum", [128, 4096], F32),
 }
 for _t in range(R):
     for _p in ("x", "l", "r"):
-        SCRATCH["q%s%d" % (_p, _t)] = _sb(C, X4)
-        SCRATCH["s%s%d" % (_p, _t)] = _sb(C, U8)
+        SCRATCH["q%s%d" % (_p, _t)] = _sb(256 if _p == "x" else C, X4)
+        SCRATCH["s%s%d" % (_p, _t)] = _sb(256 if _p == "x" else C, U8)
         SCRATCH["e%s%d" % (_p, _t)] = _sb(24, U16)
 
 NDMA = 16
 SEMAPHORES = ["cv", "ca", "ct", "cg", "sent"] + ["dma%d" % i for i in range(NDMA)] \
     + ["aq%d" % t for t in range(R)] + ["ae%d" % t for t in range(R)]
 QSEM = {"v": "cv", "a": "ca", "t": "ct", "g": "cg"}
-H = 1.0e29
-HALF = [(0, C // 2), (C // 2, C)]
+H = 2.0 ** 96
+HALF = [(0, CA), (CA, C)]
 
 
 def V(name, a=0, b=None, s=1):
@@ -55,8 +58,8 @@ def V(name, a=0, b=None, s=1):
     return (name, a, b, s)
 
 
-def P(bank, n=C):
-    return ("ps", 512 * bank, 512 * bank + n, 1)
+def P(bank, a=0, b=C):
+    return ("ps", 512 * bank + a, 512 * bank + b, 1)
 
 
 def bits(v):
@@ -80,7 +83,7 @@ def emit(g, T, ops, tail):
         for v, wr in acc:
             m = bits(v)
             for j, mj, wj in hist.get(v[0], []):
-                if not (m & mj):
+                if not (m & mj) or (o["dma"] and o["dma"] == ops[j]["dma"]):
                     continue
                 same = ops[j]["q"] == o["q"] and not ops[j]["dma"] and not o["dma"]
                 if v[0] == "ps":
@@ -105,8 +108,11 @@ def emit(g, T, ops, tail):
         o["done"] = set(kq) | {i}
         for j in need:
             ops[j]["inc"] = True
+    groups = {}
+    for o in ops:
+        if o["dma"]:
+            groups.setdefault(o["dma"], ["dma%d" % len(groups), 0, o["q"]])[1] += 16
     count = {q: 0 for q in QSEM}
-    ndma = 0
     waited = {}
     for o in ops:
         e = eng[o["q"]]
@@ -122,19 +128,16 @@ def emit(g, T, ops, tail):
                 waited[(o["q"], s)] = val
         ins = o["f"](e)
         if o["dma"]:
-            s = "dma%d" % ndma
-            ndma += 1
+            s, val, _ = groups[o["dma"]]
             ins.then_inc(T.sem[s], 16)
-            o["sig"] = (s, 16)
+            o["sig"] = (s, val)
         elif o["inc"]:
             count[o["q"]] += 1
             o["sig"] = (QSEM[o["q"]], count[o["q"]])
             ins.then_inc(T.sem[QSEM[o["q"]]], 1)
-    for o in ops:
-        if o["dma"]:
-            s = o["sig"][0]
-            if not any(k[1] == s for k in waited):
-                eng[o["q"]].wait_ge(T.sem[s], 16)
+    for s, val, q in groups.values():
+        if not any(k[1] == s for k in waited):
+            eng[q].wait_ge(T.sem[s], val)
     for s, val in tail:
         g.wait_ge(T.sem[s], val)
 
@@ -145,7 +148,7 @@ def helpers(src, dst, topo):
     can = [c for c in topo.cores_of(src) if topo.may_write(c, dst)]
     near = [c for c in can if topo.die(c) == topo.die(src)]
     far = [c for c in can if topo.die(c) != topo.die(src)]
-    return [near[0], near[1], far[0]]
+    return [near[0], far[0], near[1]]
 
 
 def send(g, T, topo, src, dst, out, in_, sem, part=None):
@@ -206,7 +209,7 @@ def rank_program(g, core, T, topo):
         name, a, b, s = v
         return T[name][:, a:b] if s == 1 else T[name][:, a:b:s]
 
-    def op(q, f, r, w, dma=False, ext=(), acc=False):
+    def op(q, f, r, w, dma=None, ext=(), acc=False):
         ops.append({"q": q, "f": f, "r": list(r), "w": list(w), "dma": dma, "ext": list(ext), "acc": acc, "inc": False})
 
     def isv(x):
@@ -247,16 +250,19 @@ def rank_program(g, core, T, topo):
         op("v", lambda e: e.quantize_mx(T[q][:, a:b], T[s][:, a:b], ap(i)), [i], [V(q, a, b), V(s, a, b)])
 
     def act(o, i, f, bias=0.0, scale=1.0, off=None, accum=None, ext=()):
-        r = [i] + ([bias] if isv(bias) else []) + ([off] if off else [])
+        r = [i] + [x for x in (bias, scale) if isv(x)] + ([off] if off else [])
         if accum is not None:
             op("a", lambda e: e.activation(ap(o), ap(i), f, bias=bias, scale=scale, accum_out=ap(accum)), r, [o, accum])
         elif f == AF.Copy:
             op("a", lambda e: e.activation(ap(o), src(i, off), f), r, [o], ext=ext)
         else:
-            op("a", lambda e: e.activation(ap(o), ap(i), f, bias=val(bias), scale=scale), r, [o], ext=ext)
+            op("a", lambda e: e.activation(ap(o), ap(i), f, bias=val(bias), scale=val(scale)), r, [o], ext=ext)
+
+    def lin(o, i, scale, bias):
+        act(o, i, AF.Identity, bias=bias, scale=scale)
 
     def mm(bank, wq, ws, wa, xq, xs, xa, xb, start=True, stop=True, ext=()):
-        o = P(bank, xb - xa)
+        o = P(bank, 0, xb - xa)
         op("t", lambda e: e.matmul_mx(ap(o), T[wq][:, wa:wa + 128], T[ws][:, wa:wa + 128], T[xq][:, xa:xb], T[xs][:, xa:xb], start, stop),
            [V(wq, wa, wa + 128), V(ws, wa, wa + 128), V(xq, xa, xb), V(xs, xa, xb)], [o], ext=ext, acc=not start)
 
@@ -266,20 +272,19 @@ def rank_program(g, core, T, topo):
         else:
             op("g", lambda e: e.iota(ap(o), pattern, base, cm, allow_small_or_imprecise_dtypes=True), [], [o])
 
-    def dma(q, out, in_, r, w):
-        op(q, lambda e: e.dma_start(out, in_), r, w, dma=True)
+    def dma(q, group, out, in_, r, w):
+        op(q, lambda e: e.dma_start(out, in_), r, w, dma=group)
 
-    def remote(kind, t):
+    def remote(kind, t, k=None):
         name, sem = "%sx%d" % (kind, t), ("ae%d" if kind == "e" else "aq%d") % t
         there = "%s%s%d" % (kind, "r" if via else "l", t)
-        if kind != "q":
-            op("g", lambda e: send(e, T, topo, core, via[0] if via else nxt, T[there][:], T[name][:], sem), [V(name)], [])
-        elif via:
-            for k in (1, 0):
-                a, b = HALF[k]
-                op("g", lambda e, k=k, a=a, b=b: send(e, T, topo, core, via[1 + k], codes(T, there, a, b), codes(T, name, a, b), sem, k), [V(name)], [])
+        if kind == "q":
+            a, b = HALF[k]
+            op("g", lambda e: send(e, T, topo, core, via[1 + k] if via else nxt, codes(T, there, a, b), codes(T, name, a, b), sem, k),
+               [V(name, a, b)], [])
         else:
-            op("g", lambda e: send(e, T, topo, core, nxt, codes(T, there), codes(T, name), sem), [V(name)], [])
+            w = SCRATCH[there][1][1]
+            op("g", lambda e: send(e, T, topo, core, via[0] if via else nxt, T[there][:], T[name][:, 0:w], sem), [V(name, 0, w)], [])
 
     def pick(a, b):
         c, d = a // 16, b // 16
@@ -289,14 +294,30 @@ def rank_program(g, core, T, topo):
 
     X = V("pool", 0, 4 * C)
     IOTA = V("pw0", 0, C)
-    C1, C16, K4, C4, C4F, QB, K16, C0, END16 = [V("col", k, k + 1) for k in range(9)]
-    QF, TF = V("qtf", 0, 1), V("qtf", 1, 2)
+    C1, C4, CZ, CW, KX, END16, TEND, TA, TB, TC, TD, TE, TF, TG = [V("col", k, k + 1) for k in range(14)]
+    QF, GF, BF_, AF_, PF = [V("qtf", k, k + 1) for k in range(5)]
     TILE = [0, 224, 384, 512]
 
-    def slot(m, cnt):
+    def cols(name, a, b, at=0):
+        return V(name, at + 4 * a, at + 4 * b)
+
+    def lane(m, a, b):
         k = 14 - m
-        a = 4 * TILE[k // 4] + k % 4
-        return V("cmp", a, a + 4 * (cnt - 1) + 1, 4)
+        s = 4 * TILE[k // 4] + k % 4
+        return V("cmp", s + 4 * a, s + 4 * (b - 1) + 1, 4)
+
+    def slot(m, bank):
+        ts(lane(m, 0, 16 * m), P(bank, 0, 16 * m), V("xs", 16 * m + 15, 16 * m + 16), A.is_ge)
+        act(V("junk", 8 * m * (m - 1), 8 * m * (m + 1)), lane(m, 0, 16 * m), AF.Identity, bias=1.0, scale=-1.0, accum=V("acc", m, m + 1))
+
+    def own(bank, a, b):
+        tt(V("ms", a, b), P(bank, a, b), V("c16", a, b), A.add)
+
+    def hold(a, b):
+        scan(V("xs", a, b), V("ctlS", a, b), V("ms", a, b), 0.0, A.add, A.min)
+
+    def diag(bank, a, b):
+        tt(lane(14, a, b), P(bank, a, b), V("xs", a, b), A.is_gt)
 
     def held4(tmp, row):
         scan(tmp, row, V("ctl4", 0, row[2] - row[1]), 2048.0, A.min, A.add)
@@ -304,204 +325,329 @@ def rank_program(g, core, T, topo):
     def list4(o, tmp):
         ts(o, (tmp[0], 3, tmp[2], 4), C4, A.add, 4.0, A.mult)
 
-    dma("a", T.ub[:], T.u[:], [], [V("ub")])
-    dma("s", T.pool[:, 0:4 * C], T.x[:], [], [X])
-    dma("s", T.nbi[:], T.nb[:], [], [V("nbi")])
-    iota(V("i16"), [[1, 226]], 128, -1)
+    def flags(o, f, ctl, a=0, b=C):
+        scan(V(o, a, b), V(f, a, b), V(ctl, a, b), -1.0, A.max, A.add)
+
+    def relu(b, bank, a, e, at=0):
+        act(V("rl", C * b + a, C * b + e), P(bank, at, at + e - a), AF.Relu, scale=0.015625)
+
+    def add(b, a, e):
+        xb = V("pool", 4 * a + b, 4 * e, 4)
+        tt(xb, V("rl", C * b + a, C * b + e), xb, A.add)
+
+    def pointer_rows(t):
+        pw = "pw%d" % t
+        if t > 0:
+            iota(V(pw, C, 256), [[1, 256 - C]], 0, 0)
+        iota(V(pw, 256 + C, 512), [[1, 256 - C]], 0, 0)
+        iota(V(pw, 512, 512 + 3 * K), [[0, 3], [1, K]], C + K * t, 0)
+        iota(V(pw, 768, 768 + 3 * K), [[0, 3], [1, K]], C + K * t, 0)
+        if t < R - 1:
+            iota(V(pw, 1024, 1024 + C), [[1, C]], 0, 0)
+
+    dma("a", "u", T.ub[:], T.u[:], [], [V("ub")])
+    dma("s", "xa", T.pool[:, 0:4 * CA], T.x[:, 0:4 * CA], [], [cols("pool", 0, CA)])
+    dma("s", "xb", T.pool[:, 4 * CA:4 * C], T.x[:, 4 * CA:4 * C], [], [cols("pool", CA, C)])
+    dma("s", "nbd", T.nbd[:], T.nb[:], [], [("nbd", 0, 1, 1)])
+    dma("s", "nbi", T.nbi[:], T.nb[:], [], [V("nbi")])
+    iota(V("qti", 4, 5), [[1, 1]], 0, 1)
     iota(V("pki"), [[1, 3], [16, 8]], 0, 0)
-    iota(V("i4"), [[4, 226]], 131, -1)
-    iota(V("pci"), [[1, 1]], 0, 1)
-    iota(IOTA, [[1, C]], 0, 0)
+    iota(V("r16"), [[0, 15], [1, 16]], 0, 0)
+    iota(V("pw0", 0, 256), [[1, 256]], 0, 0)
     memset(V("ctlS"), 0.0)
-    memset(V("cmp", 4 * 432, 4 * 640), 0.0)
-    memset(V("ctlS", 0, C, 16), H)
-    ts(V("m8i"), V("i16", 15, 128, 16), 4, A.arith_shift_right)
-    ts(V("d16"), V("i16"), 15, A.bitwise_and)
-    ts(V("m8"), V("m8i"), 8.0, A.is_equal)
-    ts(V("b16"), V("d16"), 0.0, A.is_equal, -1024.0, A.mult)
+    memset(cols("pool", C, 256), 0.0)
+    ts(V("qti", 0, 1), V("qti", 4, 5), 15, A.bitwise_and)
+    ts(V("qti", 1, 2), V("qti", 4, 5), 4, A.arith_shift_right)
+    ts(V("qti", 2, 3), V("qti", 4, 5), 3, A.bitwise_and)
+    ts(V("qti", 3, 4), V("qti", 4, 5), 2, A.arith_shift_right, 3, A.bitwise_and)
     copy(V("pko"), V("pki"))
+    memset(V("ctlS", 0, C, 16), H)
+    copy(V("qtf"), V("qti"))
+    memset(V("cmp", 4 * 432, 4 * 640), 0.0)
+    ts(V("c16"), V("r16", 0, C + 1), QF, A.not_equal, H, A.mult)
     memset(V("acc", 0, 1), 0.0)
-    ts(V("d4"), V("i4"), 2, A.arith_shift_right, 3, A.bitwise_and)
-    act(V("seg"), V("ctlS"), AF.Relu, bias=1.0, scale=-1.0)
-    for c in range(8):
-        act(V("bd", 64 * c, 64 * c + 64), V("ctlS", 1, 129, 2), AF.Identity, bias=V("m8", c, c + 1))
-    act(V("c16"), V("b16", 0, C), AF.Identity, bias=0.5 * H, scale=H / 1024.0)
     memset(V("cmp", 4 * 176, 4 * 224), 0.0)
+    memset(V("cmp", 4 * 336, 4 * 384), 0.0)
+    act(V("seg"), V("ctlS"), AF.Relu, bias=1.0, scale=-1.0)
     quant("qu", "su", 0, 128, V("ub"))
+    ts(V("m8"), V("pw0", 0, 8), GF, A.is_equal)
+    ts(V("e4"), V("pw0", 0, 4), AF_, A.is_equal)
     pick(0, 128)
+    for c in range(8):
+        lin(V("bd", 64 * c, 64 * c + 64), V("pw0", 0, 64), 0.0, V("m8", c, c + 1))
+    lin(V("ctl16"), V("c16", 1, C + 1), -17408.0 / H, 16384.0)
+    lin(V("kk4"), V("e4"), 5120.0, -1024.0)
+    lin(TA, V("c16", 0, 1), -17408.0 / H, 1232.0)
+    lin(TB, AF_, -1024.0, 4096.0)
+    act(END16, V("ctl16", 15, 16), AF.Copy)
+    lin(C1, QF, 1025.0, TA)
+    lin(TC, V("e4", 0, 1), -5120.0, TB)
+    quant("qx0", "sx0", 0, CA, cols("pool", 0, CA))
+    mm(4, "qU", "sU", 0, "qx0", "sx0", 0, CA)
+    remote("q", 0, 0)
 
     for t in range(R):
         qx, sx = "qx%d" % t, "sx%d" % t
         pw = "pw%d" % t
-        win = V("pool", 0, 4 * C + 4 * K * t)
-        nb4 = V("nb4", 56 * t, 56 * t + 56)
-        quant(qx, sx, 0, C, X)
-        mm(0, "qU", "sU", 0, qx, sx, 0, C)
-        remote("q", t)
-        remote("s", t)
-        if t == 0:
-            ts(V("b4"), V("d4"), 0.0, A.is_equal, -1024.0, A.mult)
+        first, last = t == 0, t == R - 1
+
+        def unpack(b):
+            mm(b, "qe", "se", 128 * b, "ql%d" % t, "sl%d" % t, 0, C, ext=[("aq%d" % t, n_tile)])
+
+        quant(qx, sx, CA, 256, cols("pool", CA, 256))
+        if first:
+            memset(V("eb"), 0.0)
+            own(4, 0, CA)
             quant("qbd", "sbd", 0, 128, V("bd"))
-            act(V("ctl16"), V("b16", 1, C + 1), AF.Identity, bias=-1024.0, scale=-17.0)
-            act(V("ctl4"), V("b4", 1, C + 1), AF.Identity, bias=-1024.0, scale=-5.0)
-            act(END16, V("ctl16", 15, 16), AF.Copy)
-            iota(V("pw0", 2 * C, 2 * C + 2 * K), [[0, 2], [1, K]], C, 0)
-            iota(V("pw0", 2 * C + 2 * K, 3 * C), [[1, C - 2 * K]], C, 0)
-            iota(V("pw0", 3 * C, 4 * C), [[1, C]], 0, 0)
-            dma("s", T.jw[:, 0:4 * C], T.x[:], [V(sx)], [V("jw", 0, 4 * C)])
-            dma("s", T.qw[:].bitcast(dt.uint8), T.wc[:], [], [V("qw")])
-            dma("s", T.sw[:], T.ws[:], [], [V("sw")])
-            dma("s", T.vb[:], T.v[:], [], [V("vb")])
+            hold(0, CA)
+            ts(V("eb", 3, 512, 4), V("pw0", 0, 128), PF, A.is_equal)
+        mm(5, "qU", "sU", 0, qx, sx, 0, C)
+        remote("q", t, 1)
+        remote("s", t)
+        if first:
+            for v in range(4):
+                for b in range(4):
+                    dma("s", "nbt", T.nbt[b:128:4, 42 * v:42 * v + 42], T.nbd[:, v, :, :], [("nbd", 0, 1, 1), V(sx, 0, CA)], [V("nbt", 42 * v, 42 * v + 42)])
+            dma("s", "j0", T.zw[:, 0:4 * C], T.x[:], [], [V("zw", 0, 4 * C)])
+            dma("s", "w", T.qw[:].bitcast(dt.uint8), T.wc[:], [], [V("qw")])
+            dma("s", "w", T.sw[:], T.ws[:], [], [V("sw")])
+            dma("s", "v", T.vb[:], T.v[:], [], [V("vb")])
         else:
-            mm(1, "qU", "sU", 256, qx, sx, 0, C)
-            held4(V("ps1"), V("nrow"))
-            list4(nb4, V("ps1"))
-            act(V("sg"), P(1), AF.Sign)
-            act(V("fl0"), V("sg"), AF.Relu, scale=-3.0 * C)
-        tt(V("ms"), P(0), V("c16"), A.max)
-        if t == 0:
-            memset(V("cmp", 4 * 336, 4 * 384), 0.0)
-        scan(V("xs"), V("ctlS"), V("ms"), 0.0, A.add, A.min)
-        if t == 0:
-            ts(V("qti", 0, 1), V("pci"), 15, A.bitwise_and)
-        for m in (13, 12, 11, 10, 9, 8, 7, 6, 5, 4, 3, 2, 1):
-            if m == 12:
-                tt(slot(14, C), P(0), V("xs"), A.is_gt)
-            ts(slot(m, 16 * m), P(0, 16 * m), V("xs", 16 * m + 15, 16 * m + 16), A.is_ge)
-            act(V("junk", 8 * m * (m - 1), 8 * m * (m + 1)), slot(m, 16 * m), AF.Identity, bias=1.0, scale=-1.0, accum=V("acc", m, m + 1))
-            if m == 10:
-                quant("qc", "sc", 0, 224, V("cmp", 0, 896))
-                mm(2, "qbd", "sbd", 0, "qc", "sc", 0, 224, True, False)
-            if m == 6:
-                quant("qc", "sc", 224, 384, V("cmp", 896, 1536))
-                mm(2, "qbd", "sbd", 0, "qc", "sc", 224, 384, False, False)
-        if t > 0:
-            scan(V("ll0"), V("fl0"), V("ctl16b", 0, C), 2048.0, A.min, A.add)
+            mm(6, "qU", "sU", 256, qx, sx, 0, C)
+        for m in (7, 6, 5):
+            slot(m, 4)
+        if not first:
+            act(V("sg"), P(6), AF.Sign)
+        diag(4, 0, CA)
+        own(5, CA, C)
+        slot(4, 4)
+        slot(3, 4)
+        if not first:
+            act(V("f0"), V("sg"), AF.Relu, scale=-2.0)
+        slot(2, 4)
+        hold(CA, C)
+        slot(1, 4)
+        quant("qc", "sc", 384, 640 if first else 544, V("cmp", 1536, 2560 if first else 2176))
+        slot(13, 5)
+        if not first:
+            flags("l0", "f0", "ctlP0")
+        diag(5, CA, C)
+        slot(12, 5)
+        if not first:
+            tt(V("wm"), V("l0", 15, C, 16), V("l12", 15, C, 16), A.max)
+        slot(11, 5)
+        if not first:
+            ts(V("wo"), V("wm"), CW, A.add, 512.0, A.mult)
+            act(V(pw, 0, C), V("pw%d" % (t - 1), 0, 1024 + C), AF.Copy, off=V("wo"))
+        slot(10, 5)
+        quant("qc", "sc", 0, 224, V("cmp", 0, 896))
+        mm(7, "qbd", "sbd", 0, "qc", "sc", 0, 224, True, False)
+        mm(7, "qbd", "sbd", 0, "qc", "sc", 384, 512, False, False)
+        mm(7, "qbd", "sbd", 0, "qc", "sc", 512, 640, False, False)
+        slot(9, 5)
+        slot(8, 5)
+        scan(V("ds"), V("seg"), lane(14, 0, C), 0.0, A.mult, A.add)
+        quant("qc", "sc", 224, 384, V("cmp", 896, 1536))
+        mm(7, "qbd", "sbd", 0, "qc", "sc", 224, 384, False, True)
+        if first:
+            lin(C4, BF_, 0.25, TC)
+            for v in range(4):
+                lin(V("ctl4", v, C, 4), V("pw0", 0, 56), 0.0, V("kk4", (v + 1) % 4, (v + 1) % 4 + 1))
+            for v in range(3):
+                ts(V("nb4", v, 168, 4), V("nbt", 42 * v, 42 * v + 42), 4.0, A.mult, BF_, A.add)
         else:
-            copy(V("nbo"), V("nbi"))
-        wide = 640 if t == 0 else 544
-        quant("qc", "sc", 384, wide, V("cmp", 1536, 4 * wide))
-        mm(2, "qbd", "sbd", 0, "qc", "sc", 384, 512, False, False)
-        mm(2, "qbd", "sbd", 0, "qc", "sc", 512, 640, False, True)
-        if t == 0:
-            act(V(pw, C, 2 * C), V(pw, 0, C), AF.Copy, off=V("nbo", 0, 14))
-            ts(V("qti", 1, 2), V("pci"), 3, A.bitwise_and)
-            scan(V("ds"), V("seg"), slot(14, C), 0.0, A.mult, A.add)
-            ts(K16, V("d16", 0, 1), 1024.0, A.mult, V("b16", 0, 1), A.add)
-            tt(V("t1"), V("acc"), V("ds", 15, C, 16), A.subtract)
-            copy(V("qtf"), V("qti"))
-            ts(V("ctl16", 15, C, 16), V("t1"), END16, A.add)
-            ts(K4, V("d4", 0, 1), 1024.0, A.mult, V("b4", 0, 1), A.add)
-            act(C0, K16, AF.Identity, bias=208.0, scale=-1.0)
-            act(C1, QF, AF.Identity, bias=C0)
-            act(C4, TF, AF.Identity, bias=K4, scale=0.25)
-            act(C4F, QF, AF.Identity, bias=K4, scale=1.0 / 1024.0)
-        else:
-            tt(V("w3"), V("w12"), V("ll0", 15, C, 16), A.max)
-            scan(V("ds"), V("seg"), slot(14, C), 0.0, A.mult, A.add)
-            tt(V("w4"), V("w3"), V("base16"), A.add)
-            tt(V("t1"), V("acc"), V("ds", 15, C, 16), A.subtract)
-            copy(V("wo"), V("w4"))
-            act(V(pw, 0, C), V("pw%d" % (t - 1)), AF.Copy, off=V("wo"))
-            ts(V("ctl16", 15, C, 16), V("t1"), END16, A.add)
-        scan(V("cs"), P(2), V("ctl16"), 2048.0, A.min, A.add)
-        ts(V("rko"), V("cs", 15, C, 16), -1.0, A.mult, C1, A.add)
-        if t > 0:
             held4(V("ps0"), V(pw, 0, C))
-            list4(V("po0"), V("ps0"))
-            act(V("a0"), win, AF.Copy, off=V("po0"))
-            act(V("a1"), V("a0"), AF.Copy, off=nb4)
+        tt(V("t1"), V("acc"), V("ds", 15, C, 16), A.subtract)
+        if first:
+            ts(V("nb4", 3, 168, 4), V("nbt", 126, 168), 4.0, A.mult, BF_, A.add)
+            act(V("a1"), X, AF.Copy, off=V("nb4", 0, 56))
+            copy(V("nbo"), V("nbi"))
         else:
-            held4(V("ps1"), V(pw, C, 2 * C))
-            list4(nb4, V("ps1"))
-            act(V("a1"), X, AF.Copy, off=nb4)
+            list4(V("po0"), V("ps0"))
+            act(V("a0"), V("pool", 0, 4 * C + 4 * K * t), AF.Copy, off=V("po0"))
+            act(V("a1"), V("a0"), AF.Copy, off=V("nb4", 56 * t, 56 * t + 56))
+        ts(V("ctl16", 15, C, 16), V("t1"), END16, A.add)
+        if first:
+            quant("qe", "se", 0, 128, V("eb", 3, 515))
+        else:
+            for b in range(4):
+                unpack(b)
+
+        def between(b):
+            if first:
+                quant("qe", "se", 128 * b, 128 * b + 128, V("eb", 3 - b, 515 - b))
+            else:
+                copy(V("dd", b, 4 * C, 4), P(b))
+
+        scan(V("cs"), P(7), V("ctl16"), 2048.0, A.min, A.add)
+        between(1)
+        ts(V("rko"), V("cs", 15, C, 16), -1.0, A.mult, C1, A.add)
+        between(2)
         scatter(V("erow"), V("rko"), IOTA)
+        between(3)
         held4(V("es"), V("erow", 0, K))
+        if first:
+            memset(V("zw", 4 * C, 1024), 0.0)
+            memset(V("zw", 1024 + 4 * C, 2048), 0.0)
+        else:
+            between(0)
         list4(V("ex%d" % t), V("es"))
         remote("e", t)
+        if first:
+            pointer_rows(0)
+        if not last:
+            pointer_rows(t + 1)
 
-        if t == 0:
-            for u in (1, 2):
-                iota(V("pw%d" % u, 2 * C, 2 * C + 2 * K), [[0, 2], [1, K]], C + K * u, 0)
-                iota(V("pw%d" % u, 2 * C + 2 * K, 3 * C), [[1, C - 2 * K]], C + K * u, 0)
-            iota(V("pw1", 3 * C, 4 * C), [[1, C]], 0, 0)
-            memset(V("eb"), 0.0)
+        if first:
             pick(128, 256)
-            ts(V("eb", 3, 512, 4), V("i16", 0, 128), 128.0, A.is_equal)
-            mm(3, "qU", "sU", 128, qx, sx, 0, C)
-            act(V("ctl4f"), V("ctl4"), AF.Copy)
-            act(V("ctl4f", 3, C, 4), V("pw0", 0, C, 4), AF.Identity, bias=V("ctl4", 3, 4), scale=1.0 / 256.0)
-            memset(V("jw", 4 * C, 1024), 0.0)
-            for b in range(4):
-                quant("qe", "se", 128 * b, 128 * b + 128, V("eb", 3 - b, 515 - b))
+            mm(4, "qU", "sU", 128, qx, sx, 0, C)
+            lin(V("o2"), V("c16", 0, 16), -2.0 / H, 2.0)
+            lin(V("o5"), V("c16", 1, 17), 5.0 / H, -5.0)
+            lin(V("m4"), V("e4"), 1.0 / 128.0, 0.0)
+            for v in range(3):
+                lin(V("k4", v, v + 1), V("e4", v + 1, v + 2), -2.5, V("e4", v, v + 1))
+            lin(TD, V("e4", 0, 1), -1.5, -1.0)
+            lin(TE, V("e4", 0, 1), 1.5, 0.0)
+            for v in range(3):
+                lin(V("ctlA", v, C, 4), V("pw0", 0, 56), V("m4", v, v + 1), V("k4", v, v + 1))
+            lin(V("k4", 3, 4), V("e4", 3, 4), 1.0, TD)
+            lin(CZ, QF, 1.0 / 2048.0, TE)
+            lin(V("ctlA", 3, C, 4), V("pw0", 0, 56), V("m4", 3, 4), V("k4", 3, 4))
+            lin(V("ctlB"), V("ctlA"), 2.0, 0.0)
         else:
-            tt(V("jw", 0, 4 * C), V("a0"), X, A.max)
-            quant("qj0", "sj0", 0, C, V("jw", 0, 4 * C))
-            mm(3, "qU", "sU", 128, "qj0", "sj0", 0, C)
-        act(V("s0"), P(3), AF.Copy)
-        for b in range(4):
-            mm(4 + b, "qe", "se", 128 * b, "ql%d" % t, "sl%d" % t, 0, C, ext=[("aq%d" % t, n_tile)])
-            act(V("dd", b, 4 * C, 4), P(4 + b), AF.Copy)
-        tt(V("jw", 1024, 1024 + 4 * C), V("a1"), X, A.max)
-        quant("qj1", "sj1", 0, C, V("jw", 1024, 1024 + 4 * C))
-        mm(1, "qU", "sU", 128, "qj1", "sj1", 0, C)
-        if t == 0:
-            memset(V("zw", 4 * C, 1024), 0.0)
-            act(V("a16"), V("b16", 1, C + 1), AF.Identity, scale=-2.0)
-            pick(256, 384)
-        if t == 1:
-            quant("qv", "sv", 0, 128, V("vb"))
-        tt(V("f1"), P(1), V("s0"), A.is_gt)
-        scan(V("fs1"), V("f1"), V("ctl4f"), 2048.0, A.min, A.add)
-        ts(V("fo1"), V("fs1", 3, C, 4), C4F, A.add, 1024.0, A.mult)
-        if t == 0:
-            tt(V("ctl16b", 0, C), V("a16"), V("b16", 0, C), A.add)
-
+            tt(V("zw", 0, 4 * C), V("a0"), X, A.max)
+        if first:
+            for b in range(4):
+                unpack(b)
+                act(V("dd", b, 4 * C, 4), P(b), AF.Copy)
+        j1 = 0 if first else 64
+        if not first:
+            tt(cols("zw", 0, j1, 1024), cols("a1", 0, j1), cols("pool", 0, j1), A.max)
+            quant("qj0", "sj0", 0, C, V("zw", 0, 4 * C))
+            mm(4, "qU", "sU", 128, "qj0", "sj0", 0, C)
         el, got = "el%d" % t, [("ae%d" % t, n_list)]
-        gs = 4 * C + 4 * K * t
-        act(V("pool", gs, gs + 4 * K), V("dd"), AF.Copy, off=V(el), ext=got)
-        act(V("zw", 0, 4 * C), V("jw"), AF.Copy, off=V("fo1"))
-        tt(V("zw", 1024, 1024 + 4 * K), V("dd"), V("pool", 0, 4 * K), A.max, off=V(el), ext=got)
-        for a, b in ((K, 2 * K), (2 * K, C)):
-            tt(V("zw", 1024 + 4 * a, 1024 + 4 * b), V("pool", gs, gs + 4 * (b - a)), V("pool", 4 * a, 4 * b), A.max)
-        quant("qj2", "sj2", 0, C, V("zw", 1024, 1024 + 4 * C))
-        mm(3, "qU", "sU", 128, "qj2", "sj2", 0, C)
-        tt(V("m01"), P(1), V("s0"), A.max)
-        tt(V("f2"), P(3), V("m01"), A.is_gt)
-        scan(V("fs2"), V("f2"), V("ctl4f"), 2048.0, A.min, A.add)
-        act(V("fl", 0, C), V("f1"), AF.Identity, scale=float(C))
-        ts(V("fo2"), V("fs2", 3, C, 4), C4F, A.add, 1024.0, A.mult)
-        act(V("zz", 2 * C, 4 * C), V("zw"), AF.Copy, off=V("fo2", 28, 56))
-        gather(V("zz", 0, 2 * C), V("zw"), V("fo2", 0, 28))
-        act(V("fl", C, 2 * C), V("f2"), AF.Identity, scale=2.0 * C)
-        if t == 0:
-            act(V("ctl16b", C, 2 * C), V("ctl16b", 0, C), AF.Copy)
-        quant("qz", "sz", 0, C, V("zz"))
-        for b in range(4):
-            mm(4 + b, "qw", "sw", 128 * b, "qz", "sz", 0, C)
-        scan(V("ll"), V("fl"), V("ctl16b"), 2048.0, A.min, A.add)
-        tt(V("w12"), V("ll", 15, C, 16), V("ll", C + 15, 2 * C, 16), A.max)
-        for b in range(4):
-            act(V("rl", C * b, C * b + C), P(4 + b), AF.Relu, scale=0.015625)
-            tt(V("pool", b, 4 * C, 4), V("rl", C * b, C * b + C), V("pool", b, 4 * C, 4), A.add)
-        if t < R - 1:
-            act(V("nrow"), IOTA, AF.Copy, off=V("nbo", 14 * t + 14, 14 * t + 28))
-        if t > 0:
-            act(V(pw, C, 2 * C), V(pw, 0, C), AF.Copy, off=V("nbo", 14 * t, 14 * t + 14))
-        if t == 0:
-            act(C16, V("b16", 0, 1), AF.Identity, bias=1024.0, scale=2.0)
-            act(QB, QF, AF.Identity, bias=C16)
-            act(V("base16"), V("pw0", 0, C, 16), AF.Identity, bias=QB)
+        gs = C + K * t
 
-    quant("qx3", "sx3", 0, C, X)
-    mm(0, "qv", "sv", 0, "qx3", "sx3", 0, C)
-    dma("s", T.oc[:], T.qx3[:].bitcast(dt.uint8), [V("qx3")], [])
+        def guests():
+            act(cols("pool", gs, gs + K), V("dd"), AF.Copy, off=V(el), ext=got)
+
+        early = not (came or first)
+        if early:
+            guests()
+        act(V("s0"), P(4), AF.Copy)
+        tt(cols("zw", j1, C, 1024), cols("a1", j1, C), cols("pool", j1, C), A.max)
+        if first:
+            tt(V("ctlX", 0, 16), V("o2"), V("o5"), A.add)
+            quant("qv", "sv", 0, 128, V("vb"))
+        quant("qj1", "sj1", 0, C, V("zw", 1024, 1024 + 4 * C))
+        mm(5, "qU", "sU", 128, "qj1", "sj1", 0, C)
+        if first:
+            for a, b in ((16, 32), (32, 64), (64, 128), (128, C)):
+                act(V("ctlX", a, b), V("ctlX", 0, b - a), AF.Copy)
+            pick(256, 384)
+
+        if not early:
+            guests()
+
+        def j2(a, b):
+            tt(cols("zw", a, b, 2048), cols("pool", gs + a % K, gs + a % K + b - a), cols("pool", a, b), A.max)
+
+        if first:
+            act(TEND, V("ctlX", 15, 16), AF.Copy)
+            act(V("ctlP1"), V("ctlX"), AF.Copy)
+            lin(TF, V("c16", 0, 1), -2.5 / H, 1.5)
+            lin(TG, V("c16", 0, 1), -5.0 / H, 3.0)
+            lin(V("ctlP1", 15, C, 16), V("pw0", 0, 14), 1.0 / 16.0, TEND)
+            act(V("ctlP0"), V("ctlX"), AF.Copy)
+            lin(KX, TEND, 1.0, TF)
+            lin(CW, QF, 1.0 / 512.0, TG)
+            lin(V("ctlP0", 15, C, 16), V("pw0", 0, 14), 1.0 / 32.0, TEND)
+        else:
+            act(V(pw, 256, 256 + C), V(pw, 0, C), AF.Copy, off=V("nbo", 14 * t, 14 * t + 14))
+        if came:
+            tt(V("f1"), P(5), V("s0"), A.is_gt)
+            tt(V("m01"), P(5), V("s0"), A.max)
+            flags("h1", "f1", "ctlB")
+            tt(cols("zw", 0, K, 2048), V("dd"), cols("pool", 0, K), A.max, off=V(el), ext=got)
+            ts(V("h1h"), V("h1", 3, C, 4), 0.5, A.mult)
+            j2(K, CA)
+            j2(2 * K, C)
+            quant("qj2", "sj2", 0, CA, cols("zw", 0, CA, 2048))
+            mm(6, "qU", "sU", 128, "qj2", "sj2", 0, CA)
+            j2(CA, 2 * K)
+        else:
+            j2(0, K)
+            j2(K, CA)
+            tt(V("f1"), P(5), V("s0"), A.is_gt)
+            quant("qj2", "sj2", 0, CA, cols("zw", 0, CA, 2048))
+            mm(6, "qU", "sU", 128, "qj2", "sj2", 0, CA)
+            j2(CA, 2 * K)
+            j2(2 * K, C)
+            tt(V("m01"), P(5), V("s0"), A.max)
+            flags("h1", "f1", "ctlB")
+        if came and not first:
+            flags("l1", "f1", "ctlP1")
+        quant("qj2", "sj2", CA, 256, cols("zw", CB, C, 2048))
+        mm(7, "qU", "sU", 128, "qj2", "sj2", CA, 256)
+        tt(V("f2", 0, CA), P(6, 0, CA), V("m01", 0, CA), A.is_gt)
+        if not came:
+            ts(V("h1h"), V("h1", 3, C, 4), 0.5, A.mult)
+        if first or not came:
+            flags("l1", "f1", "ctlP1")
+        flags("h2", "f2", "ctlA", 0, CA)
+        tt(V("f2", CA, C), P(7, CA - CB, C - CB), V("m01", CA, C), A.is_gt)
+        ts(V("ctlX", 15, C, 16), V("l1", 15, C, 16), 0.5, A.mult, KX, A.add)
+        tt(V("hm", 0, 32), V("h2", 3, CA, 4), V("h1h", 0, 32), A.max)
+        flags("h2", "f2", "ctlA", CA, C)
+        flags("l12", "f2", "ctlX")
+        ts(V("fo", 0, 32), V("hm", 0, 32), CZ, A.add, 2048.0, A.mult)
+        tt(V("hm", 32, 56), V("h2", CA + 3, C, 4), V("h1h", 32, 56), A.max)
+        wa = V("zw", 0, 2048 + 4 * CA)
+        act(cols("zz", 0, 80), wa, AF.Copy, off=V("fo", 0, 20))
+        gather(cols("zz", 80, CA), wa, V("fo", 20, 32))
+        ts(V("fo", 32, 56), V("hm", 32, 56), CZ, A.add, 2048.0, A.mult)
+        act(cols("zz", CA, CA + 56), V("zw"), AF.Copy, off=V("fo", 32, 46))
+        quant("qz", "sz", 0, CA, cols("zz", 0, CA))
+        for b in range(4):
+            mm(4 + b, "qw", "sw", 128 * b, "qz", "sz", 0, CA)
+        gather(cols("zz", CA + 56, C), V("zw"), V("fo", 46, 56))
+        if last:
+            ts(V("wo"), V("l12", 15, C, 16), CW, A.add, 512.0, A.mult)
+        quant("qz", "sz", CA, 256, cols("zz", CB, C))
+        for b in range(4):
+            mm(b, "qw", "sw", 128 * b, "qz", "sz", CA, 256)
+        for b in range(4):
+            relu(b, 4 + b, 0, CA)
+            add(b, 0, CA)
+        for b in range(4):
+            relu(b, b, CA, C, CA - CB)
+        if first:
+            act(V(pw, 256, 256 + C), V(pw, 0, C), AF.Copy, off=V("nbo", 0, 14))
+        qn, sn = "qx%d" % (t + 1), "sx%d" % (t + 1)
+        add(0, CA, C)
+        quant(qn, sn, 0, CA, cols("pool", 0, CA))
+        if not last:
+            mm(4, "qU", "sU", 0, qn, sn, 0, CA)
+            remote("q", t + 1, 0)
+            add(1, CA, C)
+            add(2, CA, C)
+            own(4, 0, CA)
+            add(3, CA, C)
+            hold(0, CA)
+
+    mm(4, "qv", "sv", 0, "qx3", "sx3", 0, CA)
+    dma("s", "out", T.oc[:, 0:4 * CA], codes(T, "qx3", 0, CA), [V("qx3", 0, CA)], [])
+    act(V("oprow"), V("pw2", 0, 1024), AF.Copy, off=V("wo"))
+    dma("s", "out", T.op[:], T.oprow[0:128:16, :], [V("oprow")], [])
+    for b in (1, 2, 3):
+        add(b, CA, C)
+    act(V("yb", 0, CA), P(4, 0, CA), AF.Copy)
+    dma("s", "out", T.y[:, 0:CA], T.yb[:, 0:CA], [V("yb", 0, CA)], [])
+    quant("qx3", "sx3", CA, 256, cols("pool", CA, 256))
+    mm(5, "qv", "sv", 0, "qx3", "sx3", CB, C)
+    dma("s", "out", T.oc[:, 4 * CA:4 * C], codes(T, "qx3", CA, C), [V("qx3", CA, C)], [])
     for k in range(4):
-        dma("a" if k < 2 else "s", T.osc[4 * k:4 * k + 4, :], T.sx3[32 * k:32 * k + 4, :], [V("sx3")], [])
-    tt(V("w4"), V("w12"), V("base16"), A.add)
-    copy(V("wo"), V("w4"))
-    act(V("oprow"), V("pw2"), AF.Copy, off=V("wo"))
-    copy(V("yb"), P(0))
-    dma("s", T.y[:], T.yb[:], [V("yb")], [])
-    dma("a", T.op[:], T.oprow[0:128:16, :], [V("oprow")], [])
+        dma("a", "outa", T.osc[4 * k:4 * k + 4, :], T.sx3[32 * k:32 * k + 4, 0:C], [V("sx3")], [])
+    copy(V("yb", CA, C), P(5, CA - CB, C - CB))
+    dma("s", "out", T.y[:, CA:C], T.yb[:, CA:C], [V("yb", CA, C)], [])
     emit(g, T, ops, [("sent", 3 * R * n_out)])

@@ -23,16 +23,16 @@ SCRATCH = {
     "m8": _sb(8, F32), "bd": _sb(512, BF), "qbd": _sb(128, X4), "sbd": _sb(128, U8), "col": _sb(16, F32),
     "eb": _sb(516, BF), "qe": _sb(512, X4), "se": _sb(512, U8),
     "ms": _sb(C, F32), "xs": _sb(C, F32), "cmp": _sb(2560, BF), "qc": _sb(640, X4), "sc": _sb(640, U8),
-    "junk": _sb(1456, BF), "acc": _sb(14, F32), "ds": _sb(C, BF), "cs": _sb(C, F32), "t1": _sb(14, F32),
+    "junk": _sb(1456, BF), "acc": _sb(14, F32), "i8": _sb(8, F32), "ds": _sb(C, BF), "cs": _sb(C, F32), "t1": _sb(14, F32),
     "rko": _sb(14, U16), "erow": _sb(C, F32), "es": _sb(K, F32),
     "dd": _sb(4 * C, BF), "zw": _sb(2048 + 4 * C, BF), "zz": _sb(4 * C, BF),
-    "qj0": _sb(C, X4), "sj0": _sb(C, U8), "qj1": _sb(C, X4), "sj1": _sb(C, U8),
+    "qj0": _sb(C, X4), "sj0": _sb(C, U8), "qj1": _sb(256, X4), "sj1": _sb(256, U8),
     "qj2": _sb(256, X4), "sj2": _sb(256, U8), "qz": _sb(256, X4), "sz": _sb(256, U8),
     "pw0": _sb(1280, F32), "pw1": _sb(1280, F32), "pw2": _sb(1280, F32), "oprow": _sb(C, F32),
     "ps0": _sb(C, F32), "po0": _sb(56, U16),
     "s0": _sb(C, F32), "m01": _sb(C, F32), "f1": _sb(C, BF), "f2": _sb(C, BF), "h1": _sb(C, BF), "h2": _sb(C, BF),
-    "h1h": _sb(56, F32), "hm": _sb(56, F32), "fo": _sb(56, U16),
-    "sg": _sb(C, BF), "f0": _sb(C, BF), "l0": _sb(C, BF), "l1": _sb(C, BF), "l12": _sb(C, BF),
+    "h1h": _sb(56, F32), "hm": _sb(56, F32), "fo": _sb(56, U16), "fo1": _sb(56, U16), "zv": _sb(1024 + 4 * C, BF),
+    "lh": _sb(14, F32), "f0": _sb(C, BF), "l0": _sb(C, BF), "l1": _sb(C, BF), "l12": _sb(C, BF),
     "wm": _sb(14, F32), "wo": _sb(14, U16),
     "rl": _sb(4 * C, F32), "yb": _sb(C, F32),
     "qx3": _sb(256, X4), "sx3": _sb(256, U8),
@@ -50,6 +50,14 @@ SEMAPHORES = ["cv", "ca", "ct", "cg", "sent"] + ["dma%d" % i for i in range(NDMA
 QSEM = {"v": "cv", "a": "ca", "t": "ct", "g": "cg"}
 H = 2.0 ** 96
 HALF = [(0, CA), (CA, C)]
+PLAN = {
+    "first": {"d": (1,), "f": (6, 7), "g": (0,), "h": (2,), "i": (3,), "j": (4,), "k": (5,)},
+    "even": {"a": (0,), "b": (1,), "c": (2, 3), "e": (4,), "f": (5, 6)},
+    "hurry": {"a": (0,), "b": (1,), "c": (2, 3), "f": (4,), "g": (5, 6)},
+}
+ZSPLIT = (80, 184)
+SD, J0 = 2, 24
+LATE, HURRY, EARLY, ZORD = 0, 2, False, 1
 
 
 def V(name, a=0, b=None, s=1):
@@ -202,6 +210,23 @@ def rank_program(g, core, T, topo):
         n_tile = 2 * n_list
     n_out = len(topo.engines(core, via[0] if via else nxt))
 
+    hops = [2 if helpers(cores[i], cores[(i + 1) % n], topo) else 1 for i in range(n)]
+    chain = [sum(hops[(i + t) % n] for t in range(R)) for i in range(n)]
+    hurry = [chain[(rank - t) % n] == max(chain) for t in range(R)]
+    late = [chain[(rank - 1 - t) % n] == max(chain) for t in range(R)]
+    if LATE == 1:
+        late = [True] * R
+    if LATE == 2:
+        late = [late[t] or bool(came) for t in range(R)]
+    if LATE == 3:
+        late = [False] * R
+    if LATE == 4:
+        late = [bool(came) and t == 0 for t in range(R)]
+    if HURRY == 1:
+        hurry = [True] * R
+    if HURRY == 2:
+        hurry = [False] * R
+
     A, AF = AluOpType, ActivationFunctionType
     ops = []
 
@@ -272,6 +297,9 @@ def rank_program(g, core, T, topo):
         else:
             op("g", lambda e: e.iota(ap(o), pattern, base, cm, allow_small_or_imprecise_dtypes=True), [], [o])
 
+    def gcopy(o, i):
+        op("g", lambda e: e.affine_select(ap(o), ap(i), [[0, o[2] - o[1]]], A.is_ge, 0.0, 0, 0), [i], [o])
+
     def dma(q, group, out, in_, r, w):
         op(q, lambda e: e.dma_start(out, in_), r, w, dma=group)
 
@@ -286,15 +314,17 @@ def rank_program(g, core, T, topo):
             w = SCRATCH[there][1][1]
             op("g", lambda e: send(e, T, topo, core, via[0] if via else nxt, T[there][:], T[name][:, 0:w], sem), [V(name, 0, w)], [])
 
-    def pick(a, b):
+    def pick(a, b, on="va"):
         c, d = a // 16, b // 16
-        op("v", lambda e: e.tensor_copy(T["qU"][:, a:b].bitcast(dt.uint32), T["qu"][:, 0:128].bitcast(dt.uint32).indirect(T["pko"][:, c:d])),
-           [V("qu"), V("pko", c, d)], [V("qU", a, b)])
-        act(V("sU", a, b), V("su"), AF.Copy, off=V("pko", c, d))
+        if "v" in on:
+            op("v", lambda e: e.tensor_copy(T["qU"][:, a:b].bitcast(dt.uint32), T["qu"][:, 0:128].bitcast(dt.uint32).indirect(T["pko"][:, c:d])),
+               [V("qu"), V("pko", c, d)], [V("qU", a, b)])
+        if "a" in on:
+            act(V("sU", a, b), V("su"), AF.Copy, off=V("pko", c, d))
 
     X = V("pool", 0, 4 * C)
     IOTA = V("pw0", 0, C)
-    C1, C4, CZ, CW, KX, END16, TEND, TA, TB, TC, TD, TE, TF, TG = [V("col", k, k + 1) for k in range(14)]
+    C1, C4, CZ, CW, KX, END16, TEND, TA, TB, TC, TD, TE, TF, TG, KH, CZ2 = [V("col", k, k + 1) for k in range(16)]
     QF, GF, BF_, AF_, PF = [V("qtf", k, k + 1) for k in range(5)]
     TILE = [0, 224, 384, 512]
 
@@ -335,6 +365,9 @@ def rank_program(g, core, T, topo):
         xb = V("pool", 4 * a + b, 4 * e, 4)
         tt(xb, V("rl", C * b + a, C * b + e), xb, A.add)
 
+    def larger(k, a, b):
+        tt(cols("zw", a, b, 1024 * k), cols("a%d" % k, a, b), cols("pool", a, b), A.max)
+
     def pointer_rows(t):
         pw = "pw%d" % t
         if t > 0:
@@ -351,40 +384,60 @@ def rank_program(g, core, T, topo):
     dma("s", "nbd", T.nbd[:], T.nb[:], [], [("nbd", 0, 1, 1)])
     dma("s", "nbi", T.nbi[:], T.nb[:], [], [V("nbi")])
     iota(V("qti", 4, 5), [[1, 1]], 0, 1)
+    iota(V("i8"), [[1, 8]], 0, 0)
     iota(V("pki"), [[1, 3], [16, 8]], 0, 0)
-    iota(V("r16"), [[0, 15], [1, 16]], 0, 0)
     iota(V("pw0", 0, 256), [[1, 256]], 0, 0)
+    iota(V("r16"), [[0, 15], [1, 16]], 0, 0)
     memset(V("ctlS"), 0.0)
-    memset(cols("pool", C, 256), 0.0)
     ts(V("qti", 0, 1), V("qti", 4, 5), 15, A.bitwise_and)
     ts(V("qti", 1, 2), V("qti", 4, 5), 4, A.arith_shift_right)
     ts(V("qti", 2, 3), V("qti", 4, 5), 3, A.bitwise_and)
     ts(V("qti", 3, 4), V("qti", 4, 5), 2, A.arith_shift_right, 3, A.bitwise_and)
-    copy(V("pko"), V("pki"))
-    memset(V("ctlS", 0, C, 16), H)
+    for o in (V("cmp", 4 * 176, 4 * 224), V("cmp", 4 * 336, 4 * 384)):
+        lin(o, V("ctlS", 0, o[2] - o[1]), 0.0, 0.0)
+    memset(cols("pool", C, 256), 0.0)
     copy(V("qtf"), V("qti"))
+    copy(V("pko"), V("pki"))
+    ts(V("m8"), V("i8"), GF, A.is_equal)
+    ts(V("e4"), V("i8", 0, 4), AF_, A.is_equal)
     memset(V("cmp", 4 * 432, 4 * 640), 0.0)
-    ts(V("c16"), V("r16", 0, C + 1), QF, A.not_equal, H, A.mult)
-    memset(V("acc", 0, 1), 0.0)
-    memset(V("cmp", 4 * 176, 4 * 224), 0.0)
-    memset(V("cmp", 4 * 336, 4 * 384), 0.0)
-    act(V("seg"), V("ctlS"), AF.Relu, bias=1.0, scale=-1.0)
-    quant("qu", "su", 0, 128, V("ub"))
-    ts(V("m8"), V("pw0", 0, 8), GF, A.is_equal)
-    ts(V("e4"), V("pw0", 0, 4), AF_, A.is_equal)
-    pick(0, 128)
     for c in range(8):
-        lin(V("bd", 64 * c, 64 * c + 64), V("pw0", 0, 64), 0.0, V("m8", c, c + 1))
-    lin(V("ctl16"), V("c16", 1, C + 1), -17408.0 / H, 16384.0)
-    lin(V("kk4"), V("e4"), 5120.0, -1024.0)
-    lin(TA, V("c16", 0, 1), -17408.0 / H, 1232.0)
-    lin(TB, AF_, -1024.0, 4096.0)
-    act(END16, V("ctl16", 15, 16), AF.Copy)
-    lin(C1, QF, 1025.0, TA)
-    lin(TC, V("e4", 0, 1), -5120.0, TB)
+        lin(V("bd", 64 * c, 64 * c + 64), V("ctlS", 0, 64), 0.0, V("m8", c, c + 1))
+    memset(V("acc", 0, 1), 0.0)
+    quant("qc", "sc", 512, 640, V("cmp", 2048, 2560))
+    quant("qu", "su", 0, 128, V("ub"))
     quant("qx0", "sx0", 0, CA, cols("pool", 0, CA))
+    pick(0, 128)
     mm(4, "qU", "sU", 0, "qx0", "sx0", 0, CA)
     remote("q", 0, 0)
+    memset(V("ctlS", 0, C, 16), H)
+    ts(V("c16"), V("r16", 0, C + 1), QF, A.not_equal, H, A.mult)
+    lin(V("kk4"), V("e4"), 5120.0, -1024.0)
+    lin(TB, AF_, -1024.0, 4096.0)
+    act(V("seg"), V("ctlS"), AF.Relu, bias=1.0, scale=-1.0)
+    lin(V("o2"), V("c16", 0, 16), -2.0 / H, 2.0)
+    lin(V("o5"), V("c16", 1, 17), 5.0 / H, -5.0)
+    lin(V("ctl16"), V("c16", 1, C + 1), -17408.0 / H, 16384.0)
+    lin(TA, V("c16", 0, 1), -17408.0 / H, 1232.0)
+    act(END16, V("ctl16", 15, 16), AF.Copy)
+
+    def latest(k):
+        if k == 0:
+            lin(C1, QF, 1025.0, TA)
+            lin(TC, V("e4", 0, 1), -5120.0, TB)
+            lin(C4, BF_, 0.25, TC)
+        elif k == 1:
+            lin(V("m4"), V("e4"), 1.0 / 128.0, 0.0)
+            for v in range(3):
+                lin(V("k4", v, v + 1), V("e4", v + 1, v + 2), -2.5, V("e4", v, v + 1))
+            lin(TD, V("e4", 0, 1), -1.5, -1.0)
+            lin(TE, V("e4", 0, 1), 1.5, 0.0)
+            lin(V("k4", 3, 4), V("e4", 3, 4), 1.0, TD)
+        else:
+            for v in range(4):
+                lin(V("ctlA", v, C, 4), V("pw0", 0, 56), V("m4", v, v + 1), V("k4", v, v + 1))
+            lin(V("ctlB"), V("ctlA"), 2.0, 0.0)
+            lin(CZ, QF, 1.0 / 2048.0, TE)
 
     for t in range(R):
         qx, sx = "qx%d" % t, "sx%d" % t
@@ -396,15 +449,20 @@ def rank_program(g, core, T, topo):
 
         quant(qx, sx, CA, 256, cols("pool", CA, 256))
         if first:
-            memset(V("eb"), 0.0)
             own(4, 0, CA)
             quant("qbd", "sbd", 0, 128, V("bd"))
-            hold(0, CA)
-            ts(V("eb", 3, 512, 4), V("pw0", 0, 128), PF, A.is_equal)
+        hold(0, CA)
+        if first:
+            tt(V("ctlX", 0, 16), V("o2"), V("o5"), A.add)
         mm(5, "qU", "sU", 0, qx, sx, 0, C)
         remote("q", t, 1)
         remote("s", t)
         if first:
+            for o in (V("eb"), V("zw", 4 * C, 1024), V("zw", 1024 + 4 * C, 2048)):
+                iota(o, [[0, o[2] - o[1]]], 0, 0)
+            for a, b in ((16, 32), (32, 64), (64, 128), (128, C)):
+                gcopy(V("ctlX", a, b), V("ctlX", 0, b - a))
+            gcopy(V("ctlP1"), V("ctlX"))
             for v in range(4):
                 for b in range(4):
                     dma("s", "nbt", T.nbt[b:128:4, 42 * v:42 * v + 42], T.nbd[:, v, :, :], [("nbd", 0, 1, 1), V(sx, 0, CA)], [V("nbt", 42 * v, 42 * v + 42)])
@@ -414,205 +472,222 @@ def rank_program(g, core, T, topo):
             dma("s", "v", T.vb[:], T.v[:], [], [V("vb")])
         else:
             mm(6, "qU", "sU", 256, qx, sx, 0, C)
-        for m in (7, 6, 5):
+        def forget(k):
+            if k == 0:
+                scan(V("l0"), V("f0"), V("ctlP0"), -2.0, A.max, A.add)
+            elif k == 1:
+                tt(V("wm"), V("l0", 15, C, 16), V("lh"), A.max)
+            elif k == 2:
+                ts(V("wo"), V("wm"), CW, A.add, 1024.0, A.mult)
+            elif k == 3:
+                act(V(pw, 0, C), V("pw%d" % (t - 1), 0, 1024 + C), AF.Copy, off=V("wo"))
+            elif k == 4:
+                held4(V("ps0"), V(pw, 0, C))
+            elif k == 5:
+                list4(V("po0"), V("ps0"))
+            else:
+                act(V("a0"), V("pool", 0, 4 * C + 4 * K * t), AF.Copy, off=V("po0"))
+                for a, b in HALF:
+                    act(cols("a1", a, b), V("a0"), AF.Copy, off=V("nb4", 56 * t + a // 4, 56 * t + b // 4))
+
+        def setup(k):
+            if k == 0:
+                ts(V("eb", 3, 512, 4), V("pw0", 0, 128), PF, A.is_equal)
+            elif k == 1:
+                for v in range(4):
+                    ts(V("nb4", v, 168, 4), V("nbt", 42 * v, 42 * v + 42), 4.0, A.mult, BF_, A.add)
+            elif k == 6:
+                act(V("a1"), X, AF.Copy, off=V("nb4", 0, 56))
+            elif k == 7:
+                for v in range(4):
+                    ts(V("ctl4", v, C, 4), V("pw0", 0, 56), 0.0, A.mult, V("kk4", (v + 1) % 4, (v + 1) % 4 + 1), A.add)
+            else:
+                quant("qe", "se", 128 * (k - 2), 128 * (k - 1), V("eb", 5 - k, 517 - k))
+
+        plan = PLAN["first" if first else "hurry" if hurry[t] else "even"]
+
+        def aside(place):
+            for k in plan.get(place, ()):
+                (setup if first else forget)(k)
+
+        for m in (7, 6):
             slot(m, 4)
         if not first:
-            act(V("sg"), P(6), AF.Sign)
-        diag(4, 0, CA)
+            act(V("f0"), P(6), AF.Sign, scale=-1.0)
         own(5, CA, C)
-        slot(4, 4)
-        slot(3, 4)
-        if not first:
-            act(V("f0"), V("sg"), AF.Relu, scale=-2.0)
-        slot(2, 4)
+        slot(5, 4)
+        diag(4, 0, CA)
         hold(CA, C)
-        slot(1, 4)
-        quant("qc", "sc", 384, 640 if first else 544, V("cmp", 1536, 2560 if first else 2176))
+        for m in (4, 3, 2):
+            slot(m, 4)
+        if first:
+            latest(0)
         slot(13, 5)
-        if not first:
-            flags("l0", "f0", "ctlP0")
+        aside("a")
+        slot(1, 4)
         diag(5, CA, C)
+        aside("b")
         slot(12, 5)
-        if not first:
-            tt(V("wm"), V("l0", 15, C, 16), V("l12", 15, C, 16), A.max)
+        aside("c")
+        scan(V("ds"), V("seg"), lane(14, 0, C), 0.0, A.mult, A.add)
         slot(11, 5)
-        if not first:
-            ts(V("wo"), V("wm"), CW, A.add, 512.0, A.mult)
-            act(V(pw, 0, C), V("pw%d" % (t - 1), 0, 1024 + C), AF.Copy, off=V("wo"))
+        ts(V("t1"), V("ds", 15, C, 16), -1.0, A.mult, END16, A.add)
         slot(10, 5)
+
+        def small():
+            quant("qc", "sc", 384, 544, V("cmp", 1536, 2176))
+
+        aside("d")
         quant("qc", "sc", 0, 224, V("cmp", 0, 896))
         mm(7, "qbd", "sbd", 0, "qc", "sc", 0, 224, True, False)
-        mm(7, "qbd", "sbd", 0, "qc", "sc", 384, 512, False, False)
-        mm(7, "qbd", "sbd", 0, "qc", "sc", 512, 640, False, False)
+        if plan.get("e"):
+            small()
         slot(9, 5)
         slot(8, 5)
-        scan(V("ds"), V("seg"), lane(14, 0, C), 0.0, A.mult, A.add)
+        if not plan.get("e"):
+            small()
+        mm(7, "qbd", "sbd", 0, "qc", "sc", 384, 512, False, False)
+        mm(7, "qbd", "sbd", 0, "qc", "sc", 512, 640, False, False)
+        aside("e")
         quant("qc", "sc", 224, 384, V("cmp", 896, 1536))
         mm(7, "qbd", "sbd", 0, "qc", "sc", 224, 384, False, True)
-        if first:
-            lin(C4, BF_, 0.25, TC)
-            for v in range(4):
-                lin(V("ctl4", v, C, 4), V("pw0", 0, 56), 0.0, V("kk4", (v + 1) % 4, (v + 1) % 4 + 1))
-            for v in range(3):
-                ts(V("nb4", v, 168, 4), V("nbt", 42 * v, 42 * v + 42), 4.0, A.mult, BF_, A.add)
-        else:
-            held4(V("ps0"), V(pw, 0, C))
-        tt(V("t1"), V("acc"), V("ds", 15, C, 16), A.subtract)
-        if first:
-            ts(V("nb4", 3, 168, 4), V("nbt", 126, 168), 4.0, A.mult, BF_, A.add)
-            act(V("a1"), X, AF.Copy, off=V("nb4", 0, 56))
-            copy(V("nbo"), V("nbi"))
-        else:
-            list4(V("po0"), V("ps0"))
-            act(V("a0"), V("pool", 0, 4 * C + 4 * K * t), AF.Copy, off=V("po0"))
-            act(V("a1"), V("a0"), AF.Copy, off=V("nb4", 56 * t, 56 * t + 56))
-        ts(V("ctl16", 15, C, 16), V("t1"), END16, A.add)
-        if first:
-            quant("qe", "se", 0, 128, V("eb", 3, 515))
-        else:
-            for b in range(4):
-                unpack(b)
-
-        def between(b):
-            if first:
-                quant("qe", "se", 128 * b, 128 * b + 128, V("eb", 3 - b, 515 - b))
-            else:
-                copy(V("dd", b, 4 * C, 4), P(b))
-
+        tt(V("ctl16", 15, C, 16), V("acc"), V("t1"), A.add)
+        aside("f")
         scan(V("cs"), P(7), V("ctl16"), 2048.0, A.min, A.add)
-        between(1)
+        aside("g")
         ts(V("rko"), V("cs", 15, C, 16), -1.0, A.mult, C1, A.add)
-        between(2)
+        aside("h")
         scatter(V("erow"), V("rko"), IOTA)
-        between(3)
+        aside("i")
         held4(V("es"), V("erow", 0, K))
-        if first:
-            memset(V("zw", 4 * C, 1024), 0.0)
-            memset(V("zw", 1024 + 4 * C, 2048), 0.0)
-        else:
-            between(0)
+        aside("j")
+        if J0 and not first:
+            larger(0, 0, J0)
         list4(V("ex%d" % t), V("es"))
         remote("e", t)
+        aside("k")
         if first:
+            gcopy(V("ctlP0"), V("ctlX"))
             pointer_rows(0)
         if not last:
             pointer_rows(t + 1)
 
         if first:
             pick(128, 256)
-            mm(4, "qU", "sU", 128, qx, sx, 0, C)
-            lin(V("o2"), V("c16", 0, 16), -2.0 / H, 2.0)
-            lin(V("o5"), V("c16", 1, 17), 5.0 / H, -5.0)
-            lin(V("m4"), V("e4"), 1.0 / 128.0, 0.0)
-            for v in range(3):
-                lin(V("k4", v, v + 1), V("e4", v + 1, v + 2), -2.5, V("e4", v, v + 1))
-            lin(TD, V("e4", 0, 1), -1.5, -1.0)
-            lin(TE, V("e4", 0, 1), 1.5, 0.0)
-            for v in range(3):
-                lin(V("ctlA", v, C, 4), V("pw0", 0, 56), V("m4", v, v + 1), V("k4", v, v + 1))
-            lin(V("k4", 3, 4), V("e4", 3, 4), 1.0, TD)
-            lin(CZ, QF, 1.0 / 2048.0, TE)
-            lin(V("ctlA", 3, C, 4), V("pw0", 0, 56), V("m4", 3, 4), V("k4", 3, 4))
-            lin(V("ctlB"), V("ctlA"), 2.0, 0.0)
+            latest(1)
+            copy(V("nbo"), V("nbi"))
         else:
-            tt(V("zw", 0, 4 * C), V("a0"), X, A.max)
+            larger(0, J0, C)
+        for b in range(4):
+            unpack(b)
+        for b in range(SD):
+            act(V("dd", b, 4 * C, 4), P(b), AF.Copy)
+        larger(1, 0, CA)
         if first:
-            for b in range(4):
-                unpack(b)
-                act(V("dd", b, 4 * C, 4), P(b), AF.Copy)
-        j1 = 0 if first else 64
-        if not first:
-            tt(cols("zw", 0, j1, 1024), cols("a1", 0, j1), cols("pool", 0, j1), A.max)
+            mm(4, "qU", "sU", 128, qx, sx, 0, C)
+            larger(1, CA, CA + 32)
+        else:
             quant("qj0", "sj0", 0, C, V("zw", 0, 4 * C))
             mm(4, "qU", "sU", 128, "qj0", "sj0", 0, C)
-        el, got = "el%d" % t, [("ae%d" % t, n_list)]
         gs = C + K * t
+        got = [("ae%d" % t, n_list)]
 
-        def guests():
-            act(cols("pool", gs, gs + K), V("dd"), AF.Copy, off=V(el), ext=got)
+        def guests(*cuts):
+            for a, b in zip(cuts, cuts[1:]):
+                act(cols("pool", gs + a, gs + b), V("dd"), AF.Copy, off=V("el%d" % t, a // 4, b // 4), ext=got)
 
-        early = not (came or first)
+        early = EARLY and not (late[t] or first)
         if early:
-            guests()
+            guests(0, K)
         act(V("s0"), P(4), AF.Copy)
-        tt(cols("zw", j1, C, 1024), cols("a1", j1, C), cols("pool", j1, C), A.max)
+        for b in range(SD, 4):
+            act(V("dd", b, 4 * C, 4), P(b), AF.Copy)
+        if first and late[t]:
+            latest(2)
+        quant("qj1", "sj1", 0, CA, cols("zw", 0, CA, 1024))
+        mm(5, "qU", "sU", 128, "qj1", "sj1", 0, CA)
+        larger(1, CA + 32 if first else CA, C)
         if first:
-            tt(V("ctlX", 0, 16), V("o2"), V("o5"), A.add)
-            quant("qv", "sv", 0, 128, V("vb"))
-        quant("qj1", "sj1", 0, C, V("zw", 1024, 1024 + 4 * C))
-        mm(5, "qU", "sU", 128, "qj1", "sj1", 0, C)
-        if first:
-            for a, b in ((16, 32), (32, 64), (64, 128), (128, C)):
-                act(V("ctlX", a, b), V("ctlX", 0, b - a), AF.Copy)
-            pick(256, 384)
-
-        if not early:
-            guests()
+            pick(256, 384, "v")
+        quant("qj1", "sj1", CA, 256, cols("zw", CB, C, 1024))
+        mm(6, "qU", "sU", 128, "qj1", "sj1", CA, 256)
+        tt(V("f1", 0, CA), P(5, 0, CA), V("s0", 0, CA), A.is_gt)
+        tt(V("m01", 0, CA), P(5, 0, CA), V("s0", 0, CA), A.max)
 
         def j2(a, b):
             tt(cols("zw", a, b, 2048), cols("pool", gs + a % K, gs + a % K + b - a), cols("pool", a, b), A.max)
 
+        def offsets(a, b, k):
+            if k == 0:
+                flags("h2", "f2", "ctlA", a, b)
+            elif k == 1:
+                tt(V("hm", a // 4, b // 4), V("h2", a + 3, b, 4), V("h1h", a // 4, b // 4), A.max)
+            else:
+                ts(V("fo", a // 4, b // 4), V("hm", a // 4, b // 4), CZ, A.add, 2048.0, A.mult)
+
+        def chosen(k):
+            if k == 0:
+                flags("l1", "f1", "ctlP1")
+                lin(V("ctlX", 15, C, 16), V("l1", 15, C, 16), 0.5, KX)
+            else:
+                flags("l12", "f2", "ctlX")
+
+        if not early and not late[t]:
+            guests(0, K // 2, K)
+            if first:
+                latest(2)
+        tt(V("f1", CA, C), P(6, CA - CB, C - CB), V("s0", CA, C), A.is_gt)
+        tt(V("m01", CA, C), P(6, CA - CB, C - CB), V("s0", CA, C), A.max)
+        if late[t]:
+            flags("h1", "f1", "ctlB")
+            guests(0, 32, K)
+            tt(cols("zw", 32, K, 2048), V("dd"), cols("pool", 32, K), A.max, off=V("el%d" % t, 8, 24), ext=got)
+            j2(0, 32)
+            j2(K, CA)
+            j2(2 * K, C)
+        else:
+            j2(0, K // 2)
+            j2(K, CA)
+            j2(K // 2, K)
+            j2(2 * K, C)
+            flags("h1", "f1", "ctlB")
+        lin(V("h1h"), V("h1", 3, C, 4), 0.5, 0.0)
         if first:
             act(TEND, V("ctlX", 15, 16), AF.Copy)
-            act(V("ctlP1"), V("ctlX"), AF.Copy)
             lin(TF, V("c16", 0, 1), -2.5 / H, 1.5)
-            lin(TG, V("c16", 0, 1), -5.0 / H, 3.0)
             lin(V("ctlP1", 15, C, 16), V("pw0", 0, 14), 1.0 / 16.0, TEND)
-            act(V("ctlP0"), V("ctlX"), AF.Copy)
             lin(KX, TEND, 1.0, TF)
-            lin(CW, QF, 1.0 / 512.0, TG)
-            lin(V("ctlP0", 15, C, 16), V("pw0", 0, 14), 1.0 / 32.0, TEND)
         else:
             act(V(pw, 256, 256 + C), V(pw, 0, C), AF.Copy, off=V("nbo", 14 * t, 14 * t + 14))
-        if came:
-            tt(V("f1"), P(5), V("s0"), A.is_gt)
-            tt(V("m01"), P(5), V("s0"), A.max)
-            flags("h1", "f1", "ctlB")
-            tt(cols("zw", 0, K, 2048), V("dd"), cols("pool", 0, K), A.max, off=V(el), ext=got)
-            ts(V("h1h"), V("h1", 3, C, 4), 0.5, A.mult)
-            j2(K, CA)
-            j2(2 * K, C)
-            quant("qj2", "sj2", 0, CA, cols("zw", 0, CA, 2048))
-            mm(6, "qU", "sU", 128, "qj2", "sj2", 0, CA)
-            j2(CA, 2 * K)
+        quant("qj2", "sj2", 0, CA, cols("zw", 0, CA, 2048))
+        mm(4, "qU", "sU", 128, "qj2", "sj2", 0, CA)
+        j2(CA, 2 * K)
+        if first:
+            quant("qv", "sv", 0, 128, V("vb"))
         else:
-            j2(0, K)
-            j2(K, CA)
-            tt(V("f1"), P(5), V("s0"), A.is_gt)
-            quant("qj2", "sj2", 0, CA, cols("zw", 0, CA, 2048))
-            mm(6, "qU", "sU", 128, "qj2", "sj2", 0, CA)
-            j2(CA, 2 * K)
-            j2(2 * K, C)
-            tt(V("m01"), P(5), V("s0"), A.max)
-            flags("h1", "f1", "ctlB")
-        if came and not first:
-            flags("l1", "f1", "ctlP1")
+            chosen(0)
+        tt(V("f2", 0, CA), P(4, 0, CA), V("m01", 0, CA), A.is_gt)
         quant("qj2", "sj2", CA, 256, cols("zw", CB, C, 2048))
         mm(7, "qU", "sU", 128, "qj2", "sj2", CA, 256)
-        tt(V("f2", 0, CA), P(6, 0, CA), V("m01", 0, CA), A.is_gt)
-        if not came:
-            ts(V("h1h"), V("h1", 3, C, 4), 0.5, A.mult)
-        if first or not came:
-            flags("l1", "f1", "ctlP1")
-        flags("h2", "f2", "ctlA", 0, CA)
+        offsets(0, CA, 0)
+        if first:
+            chosen(0)
+        offsets(0, CA, 1)
         tt(V("f2", CA, C), P(7, CA - CB, C - CB), V("m01", CA, C), A.is_gt)
-        ts(V("ctlX", 15, C, 16), V("l1", 15, C, 16), 0.5, A.mult, KX, A.add)
-        tt(V("hm", 0, 32), V("h2", 3, CA, 4), V("h1h", 0, 32), A.max)
-        flags("h2", "f2", "ctlA", CA, C)
-        flags("l12", "f2", "ctlX")
-        ts(V("fo", 0, 32), V("hm", 0, 32), CZ, A.add, 2048.0, A.mult)
-        tt(V("hm", 32, 56), V("h2", CA + 3, C, 4), V("h1h", 32, 56), A.max)
+        offsets(0, CA, 2)
         wa = V("zw", 0, 2048 + 4 * CA)
-        act(cols("zz", 0, 80), wa, AF.Copy, off=V("fo", 0, 20))
-        gather(cols("zz", 80, CA), wa, V("fo", 20, 32))
-        ts(V("fo", 32, 56), V("hm", 32, 56), CZ, A.add, 2048.0, A.mult)
-        act(cols("zz", CA, CA + 56), V("zw"), AF.Copy, off=V("fo", 32, 46))
+        za, zb = ZSPLIT
+        act(cols("zz", 0, za), wa, AF.Copy, off=V("fo", 0, za // 4))
+        offsets(CA, C, 0)
+        gather(cols("zz", za, CA), wa, V("fo", za // 4, 32))
+        offsets(CA, C, 1)
+        chosen(1)
+        offsets(CA, C, 2)
+        act(cols("zz", CA, zb), V("zw"), AF.Copy, off=V("fo", 32, zb // 4))
         quant("qz", "sz", 0, CA, cols("zz", 0, CA))
         for b in range(4):
             mm(4 + b, "qw", "sw", 128 * b, "qz", "sz", 0, CA)
-        gather(cols("zz", CA + 56, C), V("zw"), V("fo", 46, 56))
-        if last:
-            ts(V("wo"), V("l12", 15, C, 16), CW, A.add, 512.0, A.mult)
+        gather(cols("zz", zb, C), V("zw"), V("fo", zb // 4, 56))
         quant("qz", "sz", CA, 256, cols("zz", CB, C))
         for b in range(4):
             mm(b, "qw", "sw", 128 * b, "qz", "sz", CA, 256)
@@ -622,25 +697,31 @@ def rank_program(g, core, T, topo):
         for b in range(4):
             relu(b, b, CA, C, CA - CB)
         if first:
+            pick(256, 384, "a")
+            for o, k, c in ((TG, -3.5, 1.5), (KH, 1.0, 0.0), (TA, -1.5, 1.5)):
+                lin(o, V("c16", 0, 1), k / H, c)
             act(V(pw, 256, 256 + C), V(pw, 0, C), AF.Copy, off=V("nbo", 0, 14))
+            lin(TB, TEND, 1.0, TA)
+            lin(CW, QF, 1.0 / 1024.0, TG)
+            lin(V("ctlP0", 15, C, 16), V("pw0", 0, 14), 1.0 / 64.0, TB)
+        lin(V("lh"), V("l12", 15, C, 16), 0.5, KH)
         qn, sn = "qx%d" % (t + 1), "sx%d" % (t + 1)
         add(0, CA, C)
         quant(qn, sn, 0, CA, cols("pool", 0, CA))
         if not last:
             mm(4, "qU", "sU", 0, qn, sn, 0, CA)
             remote("q", t + 1, 0)
-            add(1, CA, C)
-            add(2, CA, C)
+            for b in (1, 2, 3):
+                add(b, CA, C)
             own(4, 0, CA)
-            add(3, CA, C)
-            hold(0, CA)
 
     mm(4, "qv", "sv", 0, "qx3", "sx3", 0, CA)
     dma("s", "out", T.oc[:, 0:4 * CA], codes(T, "qx3", 0, CA), [V("qx3", 0, CA)], [])
-    act(V("oprow"), V("pw2", 0, 1024), AF.Copy, off=V("wo"))
-    dma("s", "out", T.op[:], T.oprow[0:128:16, :], [V("oprow")], [])
+    ts(V("wo"), V("lh"), CW, A.add, 1024.0, A.mult)
     for b in (1, 2, 3):
         add(b, CA, C)
+    act(V("oprow"), V("pw2", 0, 1024), AF.Copy, off=V("wo"))
+    dma("s", "out", T.op[:], T.oprow[0:128:16, :], [V("oprow")], [])
     act(V("yb", 0, CA), P(4, 0, CA), AF.Copy)
     dma("s", "out", T.y[:, 0:CA], T.yb[:, 0:CA], [V("yb", 0, CA)], [])
     quant("qx3", "sx3", CA, 256, cols("pool", CA, 256))

@@ -25,13 +25,13 @@ SCRATCH = {
     "ms": _sb(C, F32), "xs": _sb(C, F32), "cmp": _sb(2560, BF), "qc": _sb(640, X4), "sc": _sb(640, U8),
     "junk": _sb(1456, BF), "acc": _sb(14, F32), "i8": _sb(8, F32), "ds": _sb(C, BF), "cs": _sb(C, F32), "t1": _sb(14, F32),
     "rko": _sb(14, U16), "erow": _sb(C, F32), "es": _sb(K, F32),
-    "dd": _sb(4 * C, BF), "zw": _sb(2048 + 4 * C, BF), "zz": _sb(4 * C, BF),
+    "dd": _sb(4 * C, BF), "zw": _sb(3072 + 4 * C, BF), "ctlC": _sb(C, F32), "zz": _sb(4 * C, BF),
     "qj0": _sb(C, X4), "sj0": _sb(C, U8), "qj1": _sb(256, X4), "sj1": _sb(256, U8),
     "qj2": _sb(256, X4), "sj2": _sb(256, U8), "qz": _sb(256, X4), "sz": _sb(256, U8),
     "pw0": _sb(1280, F32), "pw1": _sb(1280, F32), "pw2": _sb(1280, F32), "oprow": _sb(C, F32),
     "ps0": _sb(C, F32), "po0": _sb(56, U16),
-    "s0": _sb(C, F32), "m01": _sb(C, F32), "f1": _sb(C, BF), "f2": _sb(C, BF), "h1": _sb(C, BF), "h2": _sb(C, BF),
-    "h1h": _sb(56, F32), "hm": _sb(56, F32), "fo": _sb(56, U16), "fo1": _sb(56, U16), "zv": _sb(1024 + 4 * C, BF),
+    "s0": _sb(C, F32), "m01": _sb(C, F32), "f1": _sb(C, BF), "f2": _sb(C, BF), "h1": _sb(C, BF), "h2": _sb(C, F32),
+    "fo": _sb(56, U16),
     "lh": _sb(14, F32), "f0": _sb(C, BF), "l0": _sb(C, BF), "l1": _sb(C, BF), "l12": _sb(C, BF),
     "wm": _sb(14, F32), "wo": _sb(14, U16),
     "rl": _sb(4 * C, F32), "yb": _sb(C, F32),
@@ -51,13 +51,17 @@ QSEM = {"v": "cv", "a": "ca", "t": "ct", "g": "cg"}
 H = 2.0 ** 96
 HALF = [(0, CA), (CA, C)]
 PLAN = {
-    "first": {"d": (1,), "f": (6, 7), "g": (0,), "h": (2,), "i": (3,), "j": (4,), "k": (5,)},
-    "even": {"a": (0,), "b": (1,), "c": (2, 3), "e": (4,), "f": (5, 6)},
+    "first": {"x": (12, 1, 6), "f": (7,), "g": (8, 9, 10), "h": (0,), "i": (2, 11), "j": (3,), "k": (4, 5)},
+    "even": {"a": (0,), "b": (1,), "c": (2, 3), "d": (4,), "x": (5, 6), "h": (7,), "i": (8,), "j": (9,), "k": (10,)},
     "hurry": {"a": (0,), "b": (1,), "c": (2, 3), "f": (4,), "g": (5, 6)},
 }
-ZSPLIT = (80, 184)
-SD, J0 = 2, 24
-LATE, HURRY, EARLY, ZORD = 0, 2, False, 1
+ZSPLIT = (64, 184)
+CYCLE, GATHER, SCATTER = 0.9, 1.6, 3.8
+WAKE, AHEAD, SLACK, DMA, ISSUE, HOP, FIRST = 200, 40, 40, 1400, 100, 1500, 1500
+ARR = False
+WAIT, SLOW, QZB, JF = 1, 1, 0, 0
+SD, J0, DV, SD1 = 2, 24, 0, 2
+LATE, HURRY, EARLY, ZORD = 1, 2, False, 1
 
 
 def V(name, a=0, b=None, s=1):
@@ -82,8 +86,59 @@ def bits(v):
     return m
 
 
-def emit(g, T, ops, tail):
-    eng = {"v": g.vector, "a": g.scalar, "t": g.tensor, "g": g, "s": g.sync}
+def size(v):
+    return len(range(v[1], v[2], v[3]))
+
+
+def arrange(ops, trip):
+    depend(ops)
+    n = len(ops)
+    after = [dict() for _ in ops]
+    last, sent, group = {}, {}, {}
+    for i, o in enumerate(ops):
+        for j in o["deps"]:
+            for k in group[ops[j]["dma"]] if ops[j]["dma"] else (j,):
+                after[i][k] = WAKE
+        for s, _ in o["ext"]:
+            for j in sent[s]:
+                after[i][j] = trip(s)
+        key = o["q"] if o["q"] in "gs" else o["w"][0][1] // 512 if o["q"] == "t" else None
+        if key is not None:
+            if key in last:
+                after[i].setdefault(last[key], -ops[last[key]]["ns"] if ops[last[key]]["dma"] else 0)
+            last[key] = i
+        if o["sem"]:
+            sent.setdefault(o["sem"], []).append(i)
+        if o["dma"]:
+            group.setdefault(o["dma"], []).append(i)
+    users = [[] for _ in ops]
+    for i in range(n):
+        for j in after[i]:
+            users[j].append(i)
+    left = [len(a) for a in after]
+    ready = {i: 0.0 for i in range(n) if not left[i]}
+    todo = {q: [i for i in range(n) if ops[i]["q"] == q] for q in "vatgs"}
+    free = {q: 0.0 for q in todo}
+    end, order = [0.0] * n, []
+    while len(order) < n:
+        q = min((x for x in todo if todo[x] and todo[x][0] in ready), key=lambda x: free[x])
+        i = todo[q][0]
+        for k in todo[q][1:AHEAD]:
+            if k in ready and not ops[k]["ext"] and max(free[q], ready[k]) + ops[k]["ns"] <= ready[i] + SLACK and ready[k] < ready[i] > free[q]:
+                i = k
+                break
+        todo[q].remove(i)
+        start = max(free[q], ready.pop(i))
+        free[q], end[i] = start + (ISSUE if ops[i]["dma"] else ops[i]["ns"]), start + ops[i]["ns"]
+        order.append(i)
+        for k in users[i]:
+            left[k] -= 1
+            if not left[k]:
+                ready[k] = max(end[j] + gap for j, gap in after[k].items())
+    return [ops[i] for i in order]
+
+
+def depend(ops):
     hist = {}
     for i, o in enumerate(ops):
         deps = set()
@@ -104,6 +159,11 @@ def emit(g, T, ops, tail):
         for v, wr in acc:
             hist.setdefault(v[0], []).append((i, bits(v), wr))
         o["deps"] = deps
+
+
+def emit(g, T, ops, tail):
+    eng = {"v": g.vector, "a": g.scalar, "t": g.tensor, "g": g, "s": g.sync}
+    depend(ops)
     known = {}
     for i, o in enumerate(ops):
         kq = known.setdefault(o["q"], set())
@@ -234,8 +294,9 @@ def rank_program(g, core, T, topo):
         name, a, b, s = v
         return T[name][:, a:b] if s == 1 else T[name][:, a:b:s]
 
-    def op(q, f, r, w, dma=None, ext=(), acc=False):
-        ops.append({"q": q, "f": f, "r": list(r), "w": list(w), "dma": dma, "ext": list(ext), "acc": acc, "inc": False})
+    def op(q, f, r, w, ns, dma=None, ext=(), acc=False, sem=None):
+        ops.append({"q": q, "f": f, "r": list(r), "w": list(w), "ns": ns, "dma": dma, "ext": list(ext), "acc": acc,
+                    "inc": False, "sem": sem})
 
     def isv(x):
         return isinstance(x, tuple)
@@ -246,42 +307,52 @@ def rank_program(g, core, T, topo):
     def src(v, off):
         return ap(v) if off is None else ap(v).indirect(ap(off))
 
+    def plain(cycles, *sides):
+        if all(SCRATCH[v[0]][2] in (BF, U16) for v in sides):
+            cycles *= 0.5
+        return CYCLE * max(64, cycles * size(sides[0]))
+
+    def listed(v, cycles=GATHER):
+        return 60 + CYCLE * cycles * size(v)
+
     def memset(o, c):
-        op("v", lambda e: e.memset(ap(o), c), [], [o])
+        op("v", lambda e: e.memset(ap(o), c), [], [o], plain(1, o))
 
     def copy(o, i):
-        op("v", lambda e: e.tensor_copy(ap(o), ap(i)), [i], [o])
+        op("v", lambda e: e.tensor_copy(ap(o), ap(i)), [i], [o], plain(1, o, i))
 
     def gather(o, win, off):
-        op("v", lambda e: e.tensor_copy(ap(o), src(win, off)), [win, off], [o])
+        op("v", lambda e: e.tensor_copy(ap(o), src(win, off)), [win, off], [o], listed(o))
 
     def scatter(win, off, i):
-        op("v", lambda e: e.tensor_copy(src(win, off), ap(i)), [i, off], [win])
+        op("v", lambda e: e.tensor_copy(src(win, off), ap(i)), [i, off], [win], listed(i, SCATTER))
 
     def tt(o, a, b, f, off=None, ext=()):
-        op("v", lambda e: e.tensor_tensor(ap(o), src(a, off), ap(b), f), [a, b] + ([off] if off else []), [o], ext=ext)
+        ns = listed(o) if off else plain(1 if a[0] == "ps" else 2, o, a, b)
+        op("v", lambda e: e.tensor_tensor(ap(o), src(a, off), ap(b), f), [a, b] + ([off] if off else []), [o], ns, ext=ext)
 
     def ts(o, a, s1, f1, s2=None, f2=None):
         r = [a] + [x for x in (s1, s2) if isv(x)]
         if f2 is None:
-            op("v", lambda e: e.tensor_scalar(ap(o), ap(a), val(s1), None, f1), r, [o])
+            op("v", lambda e: e.tensor_scalar(ap(o), ap(a), val(s1), None, f1), r, [o], plain(1, o, a))
         else:
-            op("v", lambda e: e.tensor_scalar(ap(o), ap(a), val(s1), val(s2), f1, f2), r, [o])
+            op("v", lambda e: e.tensor_scalar(ap(o), ap(a), val(s1), val(s2), f1, f2), r, [o], plain(1, o, a))
 
     def scan(o, d0, d1, init, f0, f1):
-        op("v", lambda e: e.tensor_tensor_scan(ap(o), ap(d0), ap(d1), init, f0, f1), [d0, d1], [o])
+        op("v", lambda e: e.tensor_tensor_scan(ap(o), ap(d0), ap(d1), init, f0, f1), [d0, d1], [o], plain(1, o, d0, d1))
 
     def quant(q, s, a, b, i):
-        op("v", lambda e: e.quantize_mx(T[q][:, a:b], T[s][:, a:b], ap(i)), [i], [V(q, a, b), V(s, a, b)])
+        op("v", lambda e: e.quantize_mx(T[q][:, a:b], T[s][:, a:b], ap(i)), [i], [V(q, a, b), V(s, a, b)], 12 + 0.22 * size(i))
 
     def act(o, i, f, bias=0.0, scale=1.0, off=None, accum=None, ext=()):
         r = [i] + [x for x in (bias, scale) if isv(x)] + ([off] if off else [])
+        ns = listed(o) if off else 20 + CYCLE * max(64, size(o))
         if accum is not None:
-            op("a", lambda e: e.activation(ap(o), ap(i), f, bias=bias, scale=scale, accum_out=ap(accum)), r, [o, accum])
+            op("a", lambda e: e.activation(ap(o), ap(i), f, bias=bias, scale=scale, accum_out=ap(accum)), r, [o, accum], ns + 20)
         elif f == AF.Copy:
-            op("a", lambda e: e.activation(ap(o), src(i, off), f), r, [o], ext=ext)
+            op("a", lambda e: e.activation(ap(o), src(i, off), f), r, [o], ns, ext=ext)
         else:
-            op("a", lambda e: e.activation(ap(o), ap(i), f, bias=val(bias), scale=val(scale)), r, [o], ext=ext)
+            op("a", lambda e: e.activation(ap(o), ap(i), f, bias=val(bias), scale=val(scale)), r, [o], ns, ext=ext)
 
     def lin(o, i, scale, bias):
         act(o, i, AF.Identity, bias=bias, scale=scale)
@@ -289,19 +360,20 @@ def rank_program(g, core, T, topo):
     def mm(bank, wq, ws, wa, xq, xs, xa, xb, start=True, stop=True, ext=()):
         o = P(bank, 0, xb - xa)
         op("t", lambda e: e.matmul_mx(ap(o), T[wq][:, wa:wa + 128], T[ws][:, wa:wa + 128], T[xq][:, xa:xb], T[xs][:, xa:xb], start, stop),
-           [V(wq, wa, wa + 128), V(ws, wa, wa + 128), V(xq, xa, xb), V(xs, xa, xb)], [o], ext=ext, acc=not start)
+           [V(wq, wa, wa + 128), V(ws, wa, wa + 128), V(xq, xa, xb), V(xs, xa, xb)], [o], CYCLE * (xb - xa + 16), ext=ext, acc=not start)
 
     def iota(o, pattern, base, cm):
+        ns = 130 + 2 * CYCLE * size(o)
         if SCRATCH[o[0]][2] == I32:
-            op("g", lambda e: e.iota(ap(o), pattern, base, cm), [], [o])
+            op("g", lambda e: e.iota(ap(o), pattern, base, cm), [], [o], ns)
         else:
-            op("g", lambda e: e.iota(ap(o), pattern, base, cm, allow_small_or_imprecise_dtypes=True), [], [o])
+            op("g", lambda e: e.iota(ap(o), pattern, base, cm, allow_small_or_imprecise_dtypes=True), [], [o], ns)
 
     def gcopy(o, i):
-        op("g", lambda e: e.affine_select(ap(o), ap(i), [[0, o[2] - o[1]]], A.is_ge, 0.0, 0, 0), [i], [o])
+        op("g", lambda e: e.affine_select(ap(o), ap(i), [[0, o[2] - o[1]]], A.is_ge, 0.0, 0, 0), [i], [o], 170 + 2 * CYCLE * size(o))
 
     def dma(q, group, out, in_, r, w):
-        op(q, lambda e: e.dma_start(out, in_), r, w, dma=group)
+        op(q, lambda e: e.dma_start(out, in_), r, w, DMA, dma=group)
 
     def remote(kind, t, k=None):
         name, sem = "%sx%d" % (kind, t), ("ae%d" if kind == "e" else "aq%d") % t
@@ -309,22 +381,23 @@ def rank_program(g, core, T, topo):
         if kind == "q":
             a, b = HALF[k]
             op("g", lambda e: send(e, T, topo, core, via[1 + k] if via else nxt, codes(T, there, a, b), codes(T, name, a, b), sem, k),
-               [V(name, a, b)], [])
+               [V(name, a, b)], [], ISSUE, sem=sem)
         else:
             w = SCRATCH[there][1][1]
-            op("g", lambda e: send(e, T, topo, core, via[0] if via else nxt, T[there][:], T[name][:, 0:w], sem), [V(name, 0, w)], [])
+            op("g", lambda e: send(e, T, topo, core, via[0] if via else nxt, T[there][:], T[name][:, 0:w], sem), [V(name, 0, w)], [],
+               ISSUE, sem=sem)
 
     def pick(a, b, on="va"):
         c, d = a // 16, b // 16
         if "v" in on:
             op("v", lambda e: e.tensor_copy(T["qU"][:, a:b].bitcast(dt.uint32), T["qu"][:, 0:128].bitcast(dt.uint32).indirect(T["pko"][:, c:d])),
-               [V("qu"), V("pko", c, d)], [V("qU", a, b)])
+               [V("qu"), V("pko", c, d)], [V("qU", a, b)], listed(V("qU", a, b)))
         if "a" in on:
             act(V("sU", a, b), V("su"), AF.Copy, off=V("pko", c, d))
 
     X = V("pool", 0, 4 * C)
     IOTA = V("pw0", 0, C)
-    C1, C4, CZ, CW, KX, END16, TEND, TA, TB, TC, TD, TE, TF, TG, KH, CZ2 = [V("col", k, k + 1) for k in range(16)]
+    C1, C4, CZ, CW, KX, END16, TEND, TA, TB, TC, TD, TE, TF, TG, KH, CL = [V("col", k, k + 1) for k in range(16)]
     QF, GF, BF_, AF_, PF = [V("qtf", k, k + 1) for k in range(5)]
     TILE = [0, 224, 384, 512]
 
@@ -336,9 +409,11 @@ def rank_program(g, core, T, topo):
         s = 4 * TILE[k // 4] + k % 4
         return V("cmp", s + 4 * a, s + 4 * (b - 1) + 1, 4)
 
-    def slot(m, bank):
-        ts(lane(m, 0, 16 * m), P(bank, 0, 16 * m), V("xs", 16 * m + 15, 16 * m + 16), A.is_ge)
-        act(V("junk", 8 * m * (m - 1), 8 * m * (m + 1)), lane(m, 0, 16 * m), AF.Identity, bias=1.0, scale=-1.0, accum=V("acc", m, m + 1))
+    def slot(m, bank, on="va"):
+        if "v" in on:
+            ts(lane(m, 0, 16 * m), P(bank, 0, 16 * m), V("xs", 16 * m + 15, 16 * m + 16), A.is_ge)
+        if "a" in on:
+            act(V("junk", 8 * m * (m - 1), 8 * m * (m + 1)), lane(m, 0, 16 * m), AF.Identity, bias=1.0, scale=-1.0, accum=V("acc", m, m + 1))
 
     def own(bank, a, b):
         tt(V("ms", a, b), P(bank, a, b), V("c16", a, b), A.add)
@@ -386,7 +461,6 @@ def rank_program(g, core, T, topo):
     iota(V("qti", 4, 5), [[1, 1]], 0, 1)
     iota(V("i8"), [[1, 8]], 0, 0)
     iota(V("pki"), [[1, 3], [16, 8]], 0, 0)
-    iota(V("pw0", 0, 256), [[1, 256]], 0, 0)
     iota(V("r16"), [[0, 15], [1, 16]], 0, 0)
     memset(V("ctlS"), 0.0)
     ts(V("qti", 0, 1), V("qti", 4, 5), 15, A.bitwise_and)
@@ -395,8 +469,10 @@ def rank_program(g, core, T, topo):
     ts(V("qti", 3, 4), V("qti", 4, 5), 2, A.arith_shift_right, 3, A.bitwise_and)
     for o in (V("cmp", 4 * 176, 4 * 224), V("cmp", 4 * 336, 4 * 384)):
         lin(o, V("ctlS", 0, o[2] - o[1]), 0.0, 0.0)
-    memset(cols("pool", C, 256), 0.0)
+    memset(V("seg"), 1.0)
     copy(V("qtf"), V("qti"))
+    memset(cols("pool", C, 256), 0.0)
+    memset(V("seg", 0, C, 16), 0.0)
     copy(V("pko"), V("pki"))
     ts(V("m8"), V("i8"), GF, A.is_equal)
     ts(V("e4"), V("i8", 0, 4), AF_, A.is_equal)
@@ -404,40 +480,39 @@ def rank_program(g, core, T, topo):
     for c in range(8):
         lin(V("bd", 64 * c, 64 * c + 64), V("ctlS", 0, 64), 0.0, V("m8", c, c + 1))
     memset(V("acc", 0, 1), 0.0)
-    quant("qc", "sc", 512, 640, V("cmp", 2048, 2560))
-    quant("qu", "su", 0, 128, V("ub"))
     quant("qx0", "sx0", 0, CA, cols("pool", 0, CA))
+    remote("q", 0, 0)
+    quant("qu", "su", 0, 128, V("ub"))
+    quant("qx0", "sx0", CA, 256, cols("pool", CA, 256))
     pick(0, 128)
     mm(4, "qU", "sU", 0, "qx0", "sx0", 0, CA)
-    remote("q", 0, 0)
-    memset(V("ctlS", 0, C, 16), H)
     ts(V("c16"), V("r16", 0, C + 1), QF, A.not_equal, H, A.mult)
+    memset(V("ctlS", 0, C, 16), H)
     lin(V("kk4"), V("e4"), 5120.0, -1024.0)
     lin(TB, AF_, -1024.0, 4096.0)
-    act(V("seg"), V("ctlS"), AF.Relu, bias=1.0, scale=-1.0)
-    lin(V("o2"), V("c16", 0, 16), -2.0 / H, 2.0)
-    lin(V("o5"), V("c16", 1, 17), 5.0 / H, -5.0)
+    lin(TC, V("e4", 0, 1), -5120.0, TB)
     lin(V("ctl16"), V("c16", 1, C + 1), -17408.0 / H, 16384.0)
     lin(TA, V("c16", 0, 1), -17408.0 / H, 1232.0)
     act(END16, V("ctl16", 15, 16), AF.Copy)
 
     def latest(k):
         if k == 0:
-            lin(C1, QF, 1025.0, TA)
-            lin(TC, V("e4", 0, 1), -5120.0, TB)
-            lin(C4, BF_, 0.25, TC)
+            lin(V("o2"), V("c16", 0, 16), -2.0 / H, 2.0)
+            lin(V("o5"), V("c16", 1, 17), 5.0 / H, -5.0)
         elif k == 1:
             lin(V("m4"), V("e4"), 1.0 / 128.0, 0.0)
             for v in range(3):
                 lin(V("k4", v, v + 1), V("e4", v + 1, v + 2), -2.5, V("e4", v, v + 1))
             lin(TD, V("e4", 0, 1), -1.5, -1.0)
-            lin(TE, V("e4", 0, 1), 1.5, 0.0)
+            lin(TE, V("e4", 0, 1), 3.0, 0.0)
             lin(V("k4", 3, 4), V("e4", 3, 4), 1.0, TD)
         else:
             for v in range(4):
                 lin(V("ctlA", v, C, 4), V("pw0", 0, 56), V("m4", v, v + 1), V("k4", v, v + 1))
-            lin(V("ctlB"), V("ctlA"), 2.0, 0.0)
             lin(CZ, QF, 1.0 / 2048.0, TE)
+            lin(V("ctlB"), V("ctlA"), 2.0, 0.0)
+            for v in range(3):
+                lin(V("ctlC", v, C, 4), V("pw0", 0, 56), 0.0, V("k4", v, v + 1))
 
     for t in range(R):
         qx, sx = "qx%d" % t, "sx%d" % t
@@ -447,25 +522,26 @@ def rank_program(g, core, T, topo):
         def unpack(b):
             mm(b, "qe", "se", 128 * b, "ql%d" % t, "sl%d" % t, 0, C, ext=[("aq%d" % t, n_tile)])
 
-        quant(qx, sx, CA, 256, cols("pool", CA, 256))
-        if first:
+        if not first:
+            quant(qx, sx, CA, 256, cols("pool", CA, 256))
+        else:
             own(4, 0, CA)
             quant("qbd", "sbd", 0, 128, V("bd"))
         hold(0, CA)
         if first:
-            tt(V("ctlX", 0, 16), V("o2"), V("o5"), A.add)
+            quant("qc", "sc", 512, 640, V("cmp", 2048, 2560))
+        if t == 1:
+            flags("l12", "f2", "ctlX")
+            lin(V("lh"), V("l12", 15, C, 16), 0.5, KH)
         mm(5, "qU", "sU", 0, qx, sx, 0, C)
         remote("q", t, 1)
         remote("s", t)
         if first:
-            for o in (V("eb"), V("zw", 4 * C, 1024), V("zw", 1024 + 4 * C, 2048)):
-                iota(o, [[0, o[2] - o[1]]], 0, 0)
-            for a, b in ((16, 32), (32, 64), (64, 128), (128, C)):
-                gcopy(V("ctlX", a, b), V("ctlX", 0, b - a))
-            gcopy(V("ctlP1"), V("ctlX"))
+            iota(V("pw0", 0, 256), [[1, 256]], 0, 0)
+            iota(V("eb"), [[0, 516]], 0, 0)
             for v in range(4):
                 for b in range(4):
-                    dma("s", "nbt", T.nbt[b:128:4, 42 * v:42 * v + 42], T.nbd[:, v, :, :], [("nbd", 0, 1, 1), V(sx, 0, CA)], [V("nbt", 42 * v, 42 * v + 42)])
+                    dma("s", "nbt", T.nbt[b:128:4, 42 * v:42 * v + 42], T.nbd[:, v, :, :], [("nbd", 0, 1, 1)], [V("nbt", 42 * v, 42 * v + 42)])
             dma("s", "j0", T.zw[:, 0:4 * C], T.x[:], [], [V("zw", 0, 4 * C)])
             dma("s", "w", T.qw[:].bitcast(dt.uint8), T.wc[:], [], [V("qw")])
             dma("s", "w", T.sw[:], T.ws[:], [], [V("sw")])
@@ -485,10 +561,13 @@ def rank_program(g, core, T, topo):
                 held4(V("ps0"), V(pw, 0, C))
             elif k == 5:
                 list4(V("po0"), V("ps0"))
-            else:
-                act(V("a0"), V("pool", 0, 4 * C + 4 * K * t), AF.Copy, off=V("po0"))
-                for a, b in HALF:
+            elif k == 6:
+                for a, b in ((0, 56), (56, 112), (112, C)):
+                    act(cols("a0", a, b), V("pool", 0, 4 * C + 4 * K * t), AF.Copy, off=V("po0", a // 4, b // 4))
+                for a, b in ((JF, CA), (CA, C)):
                     act(cols("a1", a, b), V("a0"), AF.Copy, off=V("nb4", 56 * t + a // 4, 56 * t + b // 4))
+            else:
+                larger(0, 56 * (k - 7), 56 * (k - 6))
 
         def setup(k):
             if k == 0:
@@ -497,10 +576,16 @@ def rank_program(g, core, T, topo):
                 for v in range(4):
                     ts(V("nb4", v, 168, 4), V("nbt", 42 * v, 42 * v + 42), 4.0, A.mult, BF_, A.add)
             elif k == 6:
+                latest(0)
                 act(V("a1"), X, AF.Copy, off=V("nb4", 0, 56))
-            elif k == 7:
-                for v in range(4):
-                    ts(V("ctl4", v, C, 4), V("pw0", 0, 56), 0.0, A.mult, V("kk4", (v + 1) % 4, (v + 1) % 4 + 1), A.add)
+            elif k == 12:
+                ts(C1, QF, 1025.0, A.mult, TA, A.add)
+                ts(C4, BF_, 0.25, A.mult, TC, A.add)
+            elif k == 11:
+                tt(V("ctlX", 0, 16), V("o2"), V("o5"), A.add)
+            elif k >= 7:
+                v = k - 7
+                ts(V("ctl4", v, C, 4), V("r16", 0, 56), 0.0, A.mult, V("kk4", (v + 1) % 4, (v + 1) % 4 + 1), A.add)
             else:
                 quant("qe", "se", 128 * (k - 2), 128 * (k - 1), V("eb", 5 - k, 517 - k))
 
@@ -510,47 +595,44 @@ def rank_program(g, core, T, topo):
             for k in plan.get(place, ()):
                 (setup if first else forget)(k)
 
-        for m in (7, 6):
-            slot(m, 4)
+        slot(7, 4)
         if not first:
             act(V("f0"), P(6), AF.Sign, scale=-1.0)
+        slot(6, 4)
         own(5, CA, C)
         slot(5, 4)
         diag(4, 0, CA)
         hold(CA, C)
-        for m in (4, 3, 2):
+        for m in (4, 3, 2, 1):
             slot(m, 4)
-        if first:
-            latest(0)
-        slot(13, 5)
-        aside("a")
-        slot(1, 4)
-        diag(5, CA, C)
-        aside("b")
-        slot(12, 5)
-        aside("c")
-        scan(V("ds"), V("seg"), lane(14, 0, C), 0.0, A.mult, A.add)
-        slot(11, 5)
-        ts(V("t1"), V("ds", 15, C, 16), -1.0, A.mult, END16, A.add)
-        slot(10, 5)
-
         def small():
             quant("qc", "sc", 384, 544, V("cmp", 1536, 2176))
+            mm(7, "qbd", "sbd", 0, "qc", "sc", 384, 512, False, False)
+            mm(7, "qbd", "sbd", 0, "qc", "sc", 512, 640, False, False)
 
-        aside("d")
+        slot(13, 5)
+        aside("a")
+        diag(5, CA, C)
+        slot(12, 5)
+        aside("b")
+        scan(V("ds"), V("seg"), lane(14, 0, C), 0.0, A.mult, A.add)
+        slot(11, 5, "v")
+        aside("c")
+        slot(11, 5, "a")
+        ts(V("t1"), V("ds", 15, C, 16), -1.0, A.mult, END16, A.add)
+        slot(10, 5)
         quant("qc", "sc", 0, 224, V("cmp", 0, 896))
         mm(7, "qbd", "sbd", 0, "qc", "sc", 0, 224, True, False)
-        if plan.get("e"):
+        if not first:
             small()
         slot(9, 5)
         slot(8, 5)
-        if not plan.get("e"):
+        if first:
             small()
-        mm(7, "qbd", "sbd", 0, "qc", "sc", 384, 512, False, False)
-        mm(7, "qbd", "sbd", 0, "qc", "sc", 512, 640, False, False)
-        aside("e")
+        aside("d")
         quant("qc", "sc", 224, 384, V("cmp", 896, 1536))
         mm(7, "qbd", "sbd", 0, "qc", "sc", 224, 384, False, True)
+        aside("x")
         tt(V("ctl16", 15, C, 16), V("acc"), V("t1"), A.add)
         aside("f")
         scan(V("cs"), P(7), V("ctl16"), 2048.0, A.min, A.add)
@@ -561,13 +643,16 @@ def rank_program(g, core, T, topo):
         aside("i")
         held4(V("es"), V("erow", 0, K))
         aside("j")
-        if J0 and not first:
-            larger(0, 0, J0)
         list4(V("ex%d" % t), V("es"))
         remote("e", t)
         aside("k")
         if first:
+            for a, b in ((16, 32), (32, 64), (64, 128), (128, C)):
+                gcopy(V("ctlX", a, b), V("ctlX", 0, b - a))
+            gcopy(V("ctlP1"), V("ctlX"))
             gcopy(V("ctlP0"), V("ctlX"))
+            for k in range(3):
+                iota(V("zw", 1024 * k + 4 * C, 1024 * k + 1024), [[0, 1024 - 4 * C]], 0, 0)
             pointer_rows(0)
         if not last:
             pointer_rows(t + 1)
@@ -576,54 +661,72 @@ def rank_program(g, core, T, topo):
             pick(128, 256)
             latest(1)
             copy(V("nbo"), V("nbi"))
-        else:
-            larger(0, J0, C)
-        for b in range(4):
-            unpack(b)
-        for b in range(SD):
-            act(V("dd", b, 4 * C, 4), P(b), AF.Copy)
-        larger(1, 0, CA)
+        slow = first and came
+
+        def plane(b, on):
+            if on == "a":
+                act(V("dd", b, 4 * C, 4), P(b), AF.Copy)
+            else:
+                copy(V("dd", b, 4 * C, 4), P(b))
+
+        if not slow:
+            for b in range(4):
+                unpack(b)
+            plane(0, "a")
+            plane(1, "a")
         if first:
+            larger(1, 0, CA)
             mm(4, "qU", "sU", 128, qx, sx, 0, C)
-            larger(1, CA, CA + 32)
         else:
+            if JF:
+                tt(cols("zw", 0, JF, 1024), V("a0"), cols("pool", 0, JF), A.max, off=V("nb4", 56 * t, 56 * t + JF // 4))
+            else:
+                larger(1, 0, CA)
             quant("qj0", "sj0", 0, C, V("zw", 0, 4 * C))
             mm(4, "qU", "sU", 128, "qj0", "sj0", 0, C)
+            if JF:
+                larger(1, JF, CA)
         gs = C + K * t
         got = [("ae%d" % t, n_list)]
-
-        def guests(*cuts):
-            for a, b in zip(cuts, cuts[1:]):
-                act(cols("pool", gs + a, gs + b), V("dd"), AF.Copy, off=V("el%d" % t, a // 4, b // 4), ext=got)
-
-        early = EARLY and not (late[t] or first)
-        if early:
-            guests(0, K)
         act(V("s0"), P(4), AF.Copy)
-        for b in range(SD, 4):
-            act(V("dd", b, 4 * C, 4), P(b), AF.Copy)
-        if first and late[t]:
+        if first:
             latest(2)
+        larger(1, CA, C)
         quant("qj1", "sj1", 0, CA, cols("zw", 0, CA, 1024))
         mm(5, "qU", "sU", 128, "qj1", "sj1", 0, CA)
-        larger(1, CA + 32 if first else CA, C)
         if first:
             pick(256, 384, "v")
+        if not slow:
+            plane(2, "v")
         quant("qj1", "sj1", CA, 256, cols("zw", CB, C, 1024))
+        if slow and SLOW:
+            for b in range(4):
+                unpack(b)
         mm(6, "qU", "sU", 128, "qj1", "sj1", CA, 256)
-        tt(V("f1", 0, CA), P(5, 0, CA), V("s0", 0, CA), A.is_gt)
-        tt(V("m01", 0, CA), P(5, 0, CA), V("s0", 0, CA), A.max)
+        if not slow:
+            plane(3, "v")
+
+        def better(part):
+            bank, a, b, at = (5, 0, CA, 0) if part == 0 else (6, CA, C, CA - CB)
+            tt(V("f1", a, b), P(bank, at, at + b - a), V("s0", a, b), A.is_gt)
+            tt(V("m01", a, b), P(bank, at, at + b - a), V("s0", a, b), A.max)
+
+        def ends(a, b, on="va"):
+            if "v" in on:
+                flags("h1", "f1", "ctlB", a, b)
+            if "a" in on:
+                lin(V("ctlC", a + 3, b, 4), V("h1", a + 3, b, 4), 0.5, V("k4", 3, 4))
+
+        wait = came and (WAIT == 1 or WAIT == 2 and t != 1)
 
         def j2(a, b):
             tt(cols("zw", a, b, 2048), cols("pool", gs + a % K, gs + a % K + b - a), cols("pool", a, b), A.max)
 
         def offsets(a, b, k):
             if k == 0:
-                flags("h2", "f2", "ctlA", a, b)
-            elif k == 1:
-                tt(V("hm", a // 4, b // 4), V("h2", a + 3, b, 4), V("h1h", a // 4, b // 4), A.max)
+                flags("h2", "f2", "ctlC", a, b)
             else:
-                ts(V("fo", a // 4, b // 4), V("hm", a // 4, b // 4), CZ, A.add, 2048.0, A.mult)
+                ts(V("fo", a // 4, b // 4), V("h2", a + 3, b, 4), CZ, A.add, 2048.0, A.mult)
 
         def chosen(k):
             if k == 0:
@@ -632,79 +735,117 @@ def rank_program(g, core, T, topo):
             else:
                 flags("l12", "f2", "ctlX")
 
-        if not early and not late[t]:
-            guests(0, K // 2, K)
-            if first:
-                latest(2)
-        tt(V("f1", CA, C), P(6, CA - CB, C - CB), V("s0", CA, C), A.is_gt)
-        tt(V("m01", CA, C), P(6, CA - CB, C - CB), V("s0", CA, C), A.max)
-        if late[t]:
-            flags("h1", "f1", "ctlB")
-            guests(0, 32, K)
-            tt(cols("zw", 32, K, 2048), V("dd"), cols("pool", 32, K), A.max, off=V("el%d" % t, 8, 24), ext=got)
-            j2(0, 32)
-            j2(K, CA)
+        if wait:
+            better(0)
+            if not (slow and SLOW):
+                better(1)
+        if slow:
+            for b in range(4):
+                if not SLOW:
+                    unpack(b)
+                plane(b, "av"[b % 2])
+            if SLOW:
+                better(1)
+        for a, b in ((0, 32), (32, K)):
+            act(cols("pool", gs + a, gs + b), V("dd"), AF.Copy, off=V("el%d" % t, a // 4, b // 4), ext=got)
+        tt(cols("zw", 32, K, 2048), V("dd"), cols("pool", 32, K), A.max, off=V("el%d" % t, 8, 24), ext=got)
+        j2(0, 32)
+        j2(K, CA)
+        if wait:
             j2(2 * K, C)
+            ends(0, C)
         else:
-            j2(0, K // 2)
-            j2(K, CA)
-            j2(K // 2, K)
-            j2(2 * K, C)
-            flags("h1", "f1", "ctlB")
-        lin(V("h1h"), V("h1", 3, C, 4), 0.5, 0.0)
-        if first:
-            act(TEND, V("ctlX", 15, 16), AF.Copy)
-            lin(TF, V("c16", 0, 1), -2.5 / H, 1.5)
-            lin(V("ctlP1", 15, C, 16), V("pw0", 0, 14), 1.0 / 16.0, TEND)
-            lin(KX, TEND, 1.0, TF)
-        else:
-            act(V(pw, 256, 256 + C), V(pw, 0, C), AF.Copy, off=V("nbo", 14 * t, 14 * t + 14))
+            better(0)
         quant("qj2", "sj2", 0, CA, cols("zw", 0, CA, 2048))
         mm(4, "qU", "sU", 128, "qj2", "sj2", 0, CA)
+        if not wait:
+            ends(0, CA)
+            j2(2 * K, C)
+        act(cols("zw", 0, CA, 3072), cols("zw", 0, CA, 2048), AF.Copy)
         j2(CA, 2 * K)
-        if first:
+        if not wait:
+            better(1)
+        elif first:
             quant("qv", "sv", 0, 128, V("vb"))
         else:
             chosen(0)
-        tt(V("f2", 0, CA), P(4, 0, CA), V("m01", 0, CA), A.is_gt)
+        if not wait:
+            tt(V("f2", 0, CA), P(4, 0, CA), V("m01", 0, CA), A.is_gt)
         quant("qj2", "sj2", CA, 256, cols("zw", CB, C, 2048))
         mm(7, "qU", "sU", 128, "qj2", "sj2", CA, 256)
-        offsets(0, CA, 0)
+        if wait:
+            tt(V("f2", 0, CA), P(4, 0, CA), V("m01", 0, CA), A.is_gt)
+        else:
+            ends(CA, C)
         if first:
+            act(TEND, V("ctlX", 15, 16), AF.Copy)
+            lin(TF, V("c16", 0, 1), -2.5 / H, 1.5)
+        offsets(0, CA, 0)
+        if wait:
+            tt(V("f2", CA, C), P(7, CA - CB, C - CB), V("m01", CA, C), A.is_gt)
+        elif first:
+            quant("qv", "sv", 0, 128, V("vb"))
+        else:
             chosen(0)
         offsets(0, CA, 1)
-        tt(V("f2", CA, C), P(7, CA - CB, C - CB), V("m01", CA, C), A.is_gt)
-        offsets(0, CA, 2)
-        wa = V("zw", 0, 2048 + 4 * CA)
+        wa = V("zw", 0, 3072 + 4 * CA)
         za, zb = ZSPLIT
+        if wait:
+            act(cols("zw", CA, C, 3072), cols("zw", CA, C, 2048), AF.Copy)
         act(cols("zz", 0, za), wa, AF.Copy, off=V("fo", 0, za // 4))
-        offsets(CA, C, 0)
-        gather(cols("zz", za, CA), wa, V("fo", za // 4, 32))
-        offsets(CA, C, 1)
-        chosen(1)
-        offsets(CA, C, 2)
-        act(cols("zz", CA, zb), V("zw"), AF.Copy, off=V("fo", 32, zb // 4))
+        if not wait:
+            act(cols("zw", CA, C, 3072), cols("zw", CA, C, 2048), AF.Copy)
+        if wait:
+            offsets(CA, C, 0)
+            gather(cols("zz", za, CA), wa, V("fo", za // 4, 32))
+            offsets(CA, C, 1)
+        else:
+            tt(V("f2", CA, C), P(7, CA - CB, C - CB), V("m01", CA, C), A.is_gt)
+            gather(cols("zz", za, CA), wa, V("fo", za // 4, 32))
+            offsets(CA, C, 0)
+        if first:
+            lin(V("ctlP1", 15, C, 16), V("pw0", 0, 14), 1.0 / 16.0, TEND)
+            lin(KX, TEND, 1.0, TF)
+        else:
+            chosen(1)
         quant("qz", "sz", 0, CA, cols("zz", 0, CA))
         for b in range(4):
             mm(4 + b, "qw", "sw", 128 * b, "qz", "sz", 0, CA)
+        if not wait:
+            offsets(CA, C, 1)
+        if zb > CA:
+            act(cols("zz", CA, zb), V("zw"), AF.Copy, off=V("fo", 32, zb // 4))
+        if last:
+            ts(V("wo"), V("l12", 15, C, 16), CL, A.add, 512.0, A.mult)
+        if first:
+            flags("l1", "f1", "ctlP1")
         gather(cols("zz", zb, C), V("zw"), V("fo", zb // 4, 56))
-        quant("qz", "sz", CA, 256, cols("zz", CB, C))
         for b in range(4):
-            mm(b, "qw", "sw", 128 * b, "qz", "sz", CA, 256)
-        for b in range(4):
+            if b == QZB:
+                quant("qz", "sz", CA, 256, cols("zz", CB, C))
+                for c in range(4):
+                    mm(c, "qw", "sw", 128 * c, "qz", "sz", CA, 256)
             relu(b, 4 + b, 0, CA)
             add(b, 0, CA)
         for b in range(4):
             relu(b, b, CA, C, CA - CB)
         if first:
+            lin(V("ctlX", 15, C, 16), V("l1", 15, C, 16), 0.5, KX)
             pick(256, 384, "a")
+        act(V(pw, 256, 256 + C), V(pw, 0, C), AF.Copy, off=V("nbo", 14 * t, 14 * t + 14))
+        if last:
+            act(V("oprow"), V("pw2", 0, 1024), AF.Copy, off=V("wo"))
+            dma("s", "out", T.op[:], T.oprow[0:128:16, :], [V("oprow")], [])
+        if first:
             for o, k, c in ((TG, -3.5, 1.5), (KH, 1.0, 0.0), (TA, -1.5, 1.5)):
                 lin(o, V("c16", 0, 1), k / H, c)
-            act(V(pw, 256, 256 + C), V(pw, 0, C), AF.Copy, off=V("nbo", 0, 14))
             lin(TB, TEND, 1.0, TA)
             lin(CW, QF, 1.0 / 1024.0, TG)
             lin(V("ctlP0", 15, C, 16), V("pw0", 0, 14), 1.0 / 64.0, TB)
-        lin(V("lh"), V("l12", 15, C, 16), 0.5, KH)
+        if t == 1:
+            lin(V("lh"), V("l12", 15, C, 16), 0.5, KH)
+            lin(TF, V("c16", 0, 1), -5.0 / H, 3.0)
+            lin(CL, QF, 1.0 / 512.0, TF)
         qn, sn = "qx%d" % (t + 1), "sx%d" % (t + 1)
         add(0, CA, C)
         quant(qn, sn, 0, CA, cols("pool", 0, CA))
@@ -717,11 +858,8 @@ def rank_program(g, core, T, topo):
 
     mm(4, "qv", "sv", 0, "qx3", "sx3", 0, CA)
     dma("s", "out", T.oc[:, 0:4 * CA], codes(T, "qx3", 0, CA), [V("qx3", 0, CA)], [])
-    ts(V("wo"), V("lh"), CW, A.add, 1024.0, A.mult)
     for b in (1, 2, 3):
         add(b, CA, C)
-    act(V("oprow"), V("pw2", 0, 1024), AF.Copy, off=V("wo"))
-    dma("s", "out", T.op[:], T.oprow[0:128:16, :], [V("oprow")], [])
     act(V("yb", 0, CA), P(4, 0, CA), AF.Copy)
     dma("s", "out", T.y[:, 0:CA], T.yb[:, 0:CA], [V("yb", 0, CA)], [])
     quant("qx3", "sx3", CA, 256, cols("pool", CA, 256))
@@ -731,4 +869,7 @@ def rank_program(g, core, T, topo):
         dma("a", "outa", T.osc[4 * k:4 * k + 4, :], T.sx3[32 * k:32 * k + 4, 0:C], [V("sx3")], [])
     copy(V("yb", CA, C), P(5, CA - CB, C - CB))
     dma("s", "out", T.y[:, CA:C], T.yb[:, CA:C], [V("yb", CA, C)], [])
-    emit(g, T, ops, [("sent", 3 * R * n_out)])
+    def trip(sem):
+        return (2 if came else 1) * (HOP + (FIRST if sem == "aq0" else 0))
+
+    emit(g, T, arrange(ops, trip) if ARR else ops, [("sent", 3 * R * n_out)])

from concourse.mybir import dt, AluOpType, ActivationFunctionType

C, K, R = 224, 96, 3
CA = 128
CB = C - 128
F32, BF, I32, U16, U8, X4 = "float32", "bfloat16", "int32", "uint16", "uint8", "float8_e4m3fn_x4"


def _sb(n, d):
    return ("sbuf", [128, n], d)


SCRATCH = {
    "pool": _sb(4 * C + 12 * K, BF), "ub": _sb(512, BF), "vb": _sb(512, BF), "nbi": _sb(42, I32), "nbo": _sb(42, U16),
    "nbd": ("dram", [8, 4, 4, 42], I32), "nbt": _sb(168, I32), "nb4": _sb(168, U16),
    "qu": _sb(128, X4), "su": _sb(128, U8), "qU": _sb(384, X4), "sU": _sb(384, U8),
    "qv": _sb(128, X4), "sv": _sb(128, U8), "qw": _sb(512, X4), "sw": _sb(512, U8),
    "pki": _sb(24, I32), "pko": _sb(24, U16), "qti": _sb(5, I32), "qtf": _sb(5, F32), "r16": _sb(240, BF),
    "c16": _sb(C + 1, F32), "ctlS": _sb(C, F32), "seg": _sb(C, BF), "ctl16": _sb(C, F32), "ctl4": _sb(C, F32),
    "ctlA": _sb(C, BF), "ctlB": _sb(C, BF), "ctlX": _sb(C, BF), "ctlP0": _sb(C, BF), "ctlP1": _sb(C, BF),
    "e4": _sb(4, F32), "m4": _sb(4, F32), "k4": _sb(4, F32), "kk4": _sb(4, F32), "o2": _sb(16, F32), "o5": _sb(16, F32),
    "a0": _sb(4 * C, BF), "a1": _sb(4 * C, BF),
    "m8": _sb(8, F32), "bd": _sb(512, BF), "qbd": _sb(128, X4), "sbd": _sb(128, U8), "col": _sb(16, F32),
    "eb": _sb(516, BF), "qe": _sb(512, X4), "se": _sb(512, U8),
    "ms": _sb(C, F32), "xs": _sb(C, F32), "cmp": _sb(2560, BF), "qc": _sb(640, X4), "sc": _sb(640, U8),
    "junk": _sb(1456, BF), "acc": _sb(14, F32), "i8": _sb(8, F32), "ds": _sb(C, BF), "cs": _sb(C, F32), "t1": _sb(14, F32),
    "rko": _sb(14, U16), "erow": _sb(C, F32), "es": _sb(K, F32),
    "dd": _sb(4 * C, BF), "zw": _sb(3072 + 4 * C, BF), "ctlC": _sb(C, F32), "zz": _sb(4 * C, BF),
    "qj0": _sb(C, X4), "sj0": _sb(C, U8), "qj1": _sb(256, X4), "sj1": _sb(256, U8),
    "qj2": _sb(256, X4), "sj2": _sb(256, U8), "qz": _sb(256, X4), "sz": _sb(256, U8),
    "pw0": _sb(1280, F32), "pw1": _sb(1280, F32), "pw2": _sb(1280, F32), "oprow": _sb(C, F32),
    "ps0": _sb(C, F32), "po0": _sb(56, U16),
    "s0": _sb(C, F32), "m01": _sb(C, F32), "f1": _sb(C, BF), "f2": _sb(C, BF), "h1": _sb(C, BF), "h2": _sb(C, F32),
    "fo": _sb(56, U16),
    "lh": _sb(14, F32), "f0": _sb(C, BF), "l0": _sb(C, BF), "l1": _sb(C, BF), "l12": _sb(C, BF),
    "wm": _sb(14, F32), "wo": _sb(14, U16),
    "rl": _sb(4 * C, F32), "yb": _sb(C, F32),
    "qx3": _sb(256, X4), "sx3": _sb(256, U8),
    "ps": ("psum", [128, 4096], F32),
}
for _t in range(R):
    for _p in ("x", "l", "r"):
        SCRATCH["q%s%d" % (_p, _t)] = _sb(256 if _p == "x" else C, X4)
        SCRATCH["s%s%d" % (_p, _t)] = _sb(256 if _p == "x" else C, U8)
        SCRATCH["e%s%d" % (_p, _t)] = _sb(24, U16)

NDMA = 16
SEMAPHORES = ["cv", "ca", "ct", "cg", "sent"] + ["dma%d" % i for i in range(NDMA)] \
    + ["aq%d" % t for t in range(R)] + ["ae%d" % t for t in range(R)]
QSEM = {"v": "cv", "a": "ca", "t": "ct", "g": "cg"}
H = 2.0 ** 96
HALF = [(0, CA), (CA, C)]
PLAN = {
    "first": {"x": (12, 1, 6), "f": (7,), "g": (8, 9, 10), "h": (0,), "i": (2, 11), "j": (3,), "k": (4, 5)},
    "even": {"a": (0,), "b": (1,), "c": (2, 3), "d": (4,), "x": (5, 6), "h": (7,), "i": (8,), "j": (9,), "k": (10,)},
    "hurry": {"a": (0,), "b": (1,), "c": (2, 3), "f": (4,), "g": (5, 6)},
}
ZSPLIT = (64, 184)
CYCLE, GATHER, SCATTER = 0.9, 1.6, 3.8
WAKE, AHEAD, SLACK, DMA, ISSUE, HOP, FIRST = 200, 40, 40, 1400, 100, 1500, 1500
ARR = False
WAIT, SLOW, QZB, JF = 1, 1, 0, 0
SD, J0, DV, SD1 = 2, 24, 0, 2
LATE, HURRY, EARLY, ZORD = 1, 2, False, 1


def V(name, a=0, b=None, s=1):
    if b is None:
        b = SCRATCH[name][1][1]
    return (name, a, b, s)


def P(bank, a=0, b=C):
    return ("ps", 512 * bank + a, 512 * bank + b, 1)


def bits(v):
    name, a, b, s = v
    if name == "ps":
        return 1 << (a // 512)
    if s == 1:
        return ((1 << (b - a)) - 1) << a
    m = 0
    for i in range(a, b, s):
        m |= 1 << i
    return m


def size(v):
    return len(range(v[1], v[2], v[3]))


def arrange(ops, trip):
    depend(ops)
    n = len(ops)
    after = [dict() for _ in ops]
    last, sent, group = {}, {}, {}
    for i, o in enumerate(ops):
        for j in o["deps"]:
            for k in group[ops[j]["dma"]] if ops[j]["dma"] else (j,):
                after[i][k] = WAKE
        for s, _ in o["ext"]:
            for j in sent[s]:
                after[i][j] = trip(s)
        key = o["q"] if o["q"] in "gs" else o["w"][0][1] // 512 if o["q"] == "t" else None
        if key is not None:
            if key in last:
                after[i].setdefault(last[key], -ops[last[key]]["ns"] if ops[last[key]]["dma"] else 0)
            last[key] = i
        if o["sem"]:
            sent.setdefault(o["sem"], []).append(i)
        if o["dma"]:
            group.setdefault(o["dma"], []).append(i)
    users = [[] for _ in ops]
    for i in range(n):
        for j in after[i]:
            users[j].append(i)
    left = [len(a) for a in after]
    ready = {i: 0.0 for i in range(n) if not left[i]}
    todo = {q: [i for i in range(n) if ops[i]["q"] == q] for q in "vatgs"}
    free = {q: 0.0 for q in todo}
    end, order = [0.0] * n, []
    while len(order) < n:
        q = min((x for x in todo if todo[x] and todo[x][0] in ready), key=lambda x: free[x])
        i = todo[q][0]
        for k in todo[q][1:AHEAD]:
            if k in ready and not ops[k]["ext"] and max(free[q], ready[k]) + ops[k]["ns"] <= ready[i] + SLACK and ready[k] < ready[i] > free[q]:
                i = k
                break
        todo[q].remove(i)
        start = max(free[q], ready.pop(i))
        free[q], end[i] = start + (ISSUE if ops[i]["dma"] else ops[i]["ns"]), start + ops[i]["ns"]
        order.append(i)
        for k in users[i]:
            left[k] -= 1
            if not left[k]:
                ready[k] = max(end[j] + gap for j, gap in after[k].items())
    return [ops[i] for i in order]


def depend(ops):
    hist = {}
    for i, o in enumerate(ops):
        deps = set()
        acc = [(v, False) for v in o["r"]] + [(v, True) for v in o["w"]]
        for v, wr in acc:
            m = bits(v)
            for j, mj, wj in hist.get(v[0], []):
                if not (m & mj) or (o["dma"] and o["dma"] == ops[j]["dma"]):
                    continue
                same = ops[j]["q"] == o["q"] and not ops[j]["dma"] and not o["dma"]
                if v[0] == "ps":
                    if not same:
                        deps.add(j)
                    elif wr and not o["acc"]:
                        deps.add(j)
                elif wr or wj:
                    deps.add(j)
        for v, wr in acc:
            hist.setdefault(v[0], []).append((i, bits(v), wr))
        o["deps"] = deps


def emit(g, T, ops, tail):
    eng = {"v": g.vector, "a": g.scalar, "t": g.tensor, "g": g, "s": g.sync}
    depend(ops)
    known = {}
    for i, o in enumerate(ops):
        kq = known.setdefault(o["q"], set())
        need = []
        for j in sorted(o["deps"], reverse=True):
            if j not in kq:
                need.append(j)
                kq |= ops[j]["done"]
        o["need"] = need
        o["done"] = set(kq) | {i}
        for j in need:
            ops[j]["inc"] = True
    groups = {}
    for o in ops:
        if o["dma"]:
            groups.setdefault(o["dma"], ["dma%d" % len(groups), 0, o["q"]])[1] += 16
    count = {q: 0 for q in QSEM}
    waited = {}
    for o in ops:
        e = eng[o["q"]]
        want = {}
        for j in o["need"]:
            s, val = ops[j]["sig"]
            want[s] = max(want.get(s, 0), val)
        for s, val in o["ext"]:
            want[s] = max(want.get(s, 0), val)
        for s, val in want.items():
            if waited.get((o["q"], s), 0) < val:
                e.wait_ge(T.sem[s], val)
                waited[(o["q"], s)] = val
        ins = o["f"](e)
        if o["dma"]:
            s, val, _ = groups[o["dma"]]
            ins.then_inc(T.sem[s], 16)
            o["sig"] = (s, val)
        elif o["inc"]:
            count[o["q"]] += 1
            o["sig"] = (QSEM[o["q"]], count[o["q"]])
            ins.then_inc(T.sem[QSEM[o["q"]]], 1)
    for s, val, q in groups.values():
        if not any(k[1] == s for k in waited):
            eng[q].wait_ge(T.sem[s], val)
    for s, val in tail:
        g.wait_ge(T.sem[s], val)


def helpers(src, dst, topo):
    if topo.may_write(src, dst):
        return None
    can = [c for c in topo.cores_of(src) if topo.may_write(c, dst)]
    near = [c for c in can if topo.die(c) == topo.die(src)]
    far = [c for c in can if topo.die(c) != topo.die(src)]
    return [near[0], far[0], near[1]]


def send(g, T, topo, src, dst, out, in_, sem, part=None):
    rid, pid = topo.addr(dst, src)
    use = topo.engines(src, dst)
    if part is not None:
        h = len(use) // 2
        use = use[h * part:h * part + h]
    g.remote_dma(out, in_, T.sem[sem], T.sem["sent"], pid, rid, sum(1 << e for e in use))
    return len(use)


def codes(T, name, a=0, b=C):
    return T[name][:, a:b].bitcast(dt.uint8)


def relay_program(g, core, T, topo, src, dst, role):
    n_in = len(topo.engines(src, core))
    total = 0
    for t in range(R):
        if role == 0:
            g.wait_ge(T.sem["aq%d" % t], n_in)
            total += send(g, T, topo, core, dst, T["sl%d" % t][:], T["sr%d" % t][:], "aq%d" % t)
            g.wait_ge(T.sem["ae%d" % t], n_in)
            total += send(g, T, topo, core, dst, T["el%d" % t][:], T["er%d" % t][:], "ae%d" % t)
        else:
            a, b = HALF[role - 1]
            g.wait_ge(T.sem["aq%d" % t], n_in // 2)
            total += send(g, T, topo, core, dst, codes(T, "ql%d" % t, a, b), codes(T, "qr%d" % t, a, b), "aq%d" % t)
    g.wait_ge(T.sem["sent"], total)


def rank_program(g, core, T, topo):
    cores = list(T.cores)
    n = len(cores)
    rank = T.rank_of(core)
    if rank is None:
        for i in range(n):
            src, dst = cores[i], cores[(i + 1) % n]
            via = helpers(src, dst, topo)
            if via and core in via:
                relay_program(g, core, T, topo, src, dst, via.index(core))
        return
    nxt, prv = cores[(rank + 1) % n], cores[(rank - 1) % n]
    via, came = helpers(core, nxt, topo), helpers(prv, core, topo)
    if came:
        n_list = len(topo.engines(came[0], core))
        n_tile = sum(len(topo.engines(c, core)) for c in came)
    else:
        n_list = len(topo.engines(prv, core))
        n_tile = 2 * n_list
    n_out = len(topo.engines(core, via[0] if via else nxt))

    hops = [2 if helpers(cores[i], cores[(i + 1) % n], topo) else 1 for i in range(n)]
    chain = [sum(hops[(i + t) % n] for t in range(R)) for i in range(n)]
    hurry = [chain[(rank - t) % n] == max(chain) for t in range(R)]
    late = [chain[(rank - 1 - t) % n] == max(chain) for t in range(R)]
    if LATE == 1:
        late = [True] * R
    if LATE == 2:
        late = [late[t] or bool(came) for t in range(R)]
    if LATE == 3:
        late = [False] * R
    if LATE == 4:
        late = [bool(came) and t == 0 for t in range(R)]
    if HURRY == 1:
        hurry = [True] * R
    if HURRY == 2:
        hurry = [False] * R

    A, AF = AluOpType, ActivationFunctionType
    ops = []

    def ap(v):
        name, a, b, s = v
        return T[name][:, a:b] if s == 1 else T[name][:, a:b:s]

    def op(q, f, r, w, ns, dma=None, ext=(), acc=False, sem=None):
        ops.append({"q": q, "f": f, "r": list(r), "w": list(w), "ns": ns, "dma": dma, "ext": list(ext), "acc": acc,
                    "inc": False, "sem": sem})

    def isv(x):
        return isinstance(x, tuple)

    def val(x):
        return ap(x) if isv(x) else x

    def src(v, off):
        return ap(v) if off is None else ap(v).indirect(ap(off))

    def plain(cycles, *sides):
        if all(SCRATCH[v[0]][2] in (BF, U16) for v in sides):
            cycles *= 0.5
        return CYCLE * max(64, cycles * size(sides[0]))

    def listed(v, cycles=GATHER):
        return 60 + CYCLE * cycles * size(v)

    def memset(o, c):
        op("v", lambda e: e.memset(ap(o), c), [], [o], plain(1, o))

    def copy(o, i):
        op("v", lambda e: e.tensor_copy(ap(o), ap(i)), [i], [o], plain(1, o, i))

    def gather(o, win, off):
        op("v", lambda e: e.tensor_copy(ap(o), src(win, off)), [win, off], [o], listed(o))

    def scatter(win, off, i):
        op("v", lambda e: e.tensor_copy(src(win, off), ap(i)), [i, off], [win], listed(i, SCATTER))

    def tt(o, a, b, f, off=None, ext=()):
        ns = listed(o) if off else plain(1 if a[0] == "ps" else 2, o, a, b)
        op("v", lambda e: e.tensor_tensor(ap(o), src(a, off), ap(b), f), [a, b] + ([off] if off else []), [o], ns, ext=ext)

    def ts(o, a, s1, f1, s2=None, f2=None):
        r = [a] + [x for x in (s1, s2) if isv(x)]
        if f2 is None:
            op("v", lambda e: e.tensor_scalar(ap(o), ap(a), val(s1), None, f1), r, [o], plain(1, o, a))
        else:
            op("v", lambda e: e.tensor_scalar(ap(o), ap(a), val(s1), val(s2), f1, f2), r, [o], plain(1, o, a))

    def scan(o, d0, d1, init, f0, f1):
        op("v", lambda e: e.tensor_tensor_scan(ap(o), ap(d0), ap(d1), init, f0, f1), [d0, d1], [o], plain(1, o, d0, d1))

    def quant(q, s, a, b, i):
        op("v", lambda e: e.quantize_mx(T[q][:, a:b], T[s][:, a:b], ap(i)), [i], [V(q, a, b), V(s, a, b)], 12 + 0.22 * size(i))

    def act(o, i, f, bias=0.0, scale=1.0, off=None, accum=None, ext=()):
        r = [i] + [x for x in (bias, scale) if isv(x)] + ([off] if off else [])
        ns = listed(o) if off else 20 + CYCLE * max(64, size(o))
        if accum is not None:
            op("a", lambda e: e.activation(ap(o), ap(i), f, bias=bias, scale=scale, accum_out=ap(accum)), r, [o, accum], ns + 20)
        elif f == AF.Copy:
            op("a", lambda e: e.activation(ap(o), src(i, off), f), r, [o], ns, ext=ext)
        else:
            op("a", lambda e: e.activation(ap(o), ap(i), f, bias=val(bias), scale=val(scale)), r, [o], ns, ext=ext)

    def lin(o, i, scale, bias):
        act(o, i, AF.Identity, bias=bias, scale=scale)

    def mm(bank, wq, ws, wa, xq, xs, xa, xb, start=True, stop=True, ext=()):
        o = P(bank, 0, xb - xa)
        op("t", lambda e: e.matmul_mx(ap(o), T[wq][:, wa:wa + 128], T[ws][:, wa:wa + 128], T[xq][:, xa:xb], T[xs][:, xa:xb], start, stop),
           [V(wq, wa, wa + 128), V(ws, wa, wa + 128), V(xq, xa, xb), V(xs, xa, xb)], [o], CYCLE * (xb - xa + 16), ext=ext, acc=not start)

    def iota(o, pattern, base, cm):
        ns = 130 + 2 * CYCLE * size(o)
        if SCRATCH[o[0]][2] == I32:
            op("g", lambda e: e.iota(ap(o), pattern, base, cm), [], [o], ns)
        else:
            op("g", lambda e: e.iota(ap(o), pattern, base, cm, allow_small_or_imprecise_dtypes=True), [], [o], ns)

    def gcopy(o, i):
        op("g", lambda e: e.affine_select(ap(o), ap(i), [[0, o[2] - o[1]]], A.is_ge, 0.0, 0, 0), [i], [o], 170 + 2 * CYCLE * size(o))

    def dma(q, group, out, in_, r, w):
        op(q, lambda e: e.dma_start(out, in_), r, w, DMA, dma=group)

    def remote(kind, t, k=None):
        name, sem = "%sx%d" % (kind, t), ("ae%d" if kind == "e" else "aq%d") % t
        there = "%s%s%d" % (kind, "r" if via else "l", t)
        if kind == "q":
            a, b = HALF[k]
            op("g", lambda e: send(e, T, topo, core, via[1 + k] if via else nxt, codes(T, there, a, b), codes(T, name, a, b), sem, k),
               [V(name, a, b)], [], ISSUE, sem=sem)
        else:
            w = SCRATCH[there][1][1]
            op("g", lambda e: send(e, T, topo, core, via[0] if via else nxt, T[there][:], T[name][:, 0:w], sem), [V(name, 0, w)], [],
               ISSUE, sem=sem)

    def pick(a, b, on="va"):
        c, d = a // 16, b // 16
        if "v" in on:
            op("v", lambda e: e.tensor_copy(T["qU"][:, a:b].bitcast(dt.uint32), T["qu"][:, 0:128].bitcast(dt.uint32).indirect(T["pko"][:, c:d])),
               [V("qu"), V("pko", c, d)], [V("qU", a, b)], listed(V("qU", a, b)))
        if "a" in on:
            act(V("sU", a, b), V("su"), AF.Copy, off=V("pko", c, d))

    X = V("pool", 0, 4 * C)
    IOTA = V("pw0", 0, C)
    C1, C4, CZ, CW, KX, END16, TEND, TA, TB, TC, TD, TE, TF, TG, KH, CL = [V("col", k, k + 1) for k in range(16)]
    QF, GF, BF_, AF_, PF = [V("qtf", k, k + 1) for k in range(5)]
    TILE = [0, 224, 384, 512]

    def cols(name, a, b, at=0):
        return V(name, at + 4 * a, at + 4 * b)

    def lane(m, a, b):
        k = 14 - m
        s = 4 * TILE[k // 4] + k % 4
        return V("cmp", s + 4 * a, s + 4 * (b - 1) + 1, 4)

    def slot(m, bank, on="va"):
        if "v" in on:
            ts(lane(m, 0, 16 * m), P(bank, 0, 16 * m), V("xs", 16 * m + 15, 16 * m + 16), A.is_ge)
        if "a" in on:
            act(V("junk", 8 * m * (m - 1), 8 * m * (m + 1)), lane(m, 0, 16 * m), AF.Identity, bias=1.0, scale=-1.0, accum=V("acc", m, m + 1))

    def own(bank, a, b):
        tt(V("ms", a, b), P(bank, a, b), V("c16", a, b), A.add)

    def hold(a, b):
        scan(V("xs", a, b), V("ctlS", a, b), V("ms", a, b), 0.0, A.add, A.min)

    def diag(bank, a, b):
        tt(lane(14, a, b), P(bank, a, b), V("xs", a, b), A.is_gt)

    def held4(tmp, row):
        scan(tmp, row, V("ctl4", 0, row[2] - row[1]), 2048.0, A.min, A.add)

    def list4(o, tmp):
        ts(o, (tmp[0], 3, tmp[2], 4), C4, A.add, 4.0, A.mult)

    def flags(o, f, ctl, a=0, b=C):
        scan(V(o, a, b), V(f, a, b), V(ctl, a, b), -1.0, A.max, A.add)

    def relu(b, bank, a, e, at=0):
        act(V("rl", C * b + a, C * b + e), P(bank, at, at + e - a), AF.Relu, scale=0.015625)

    def add(b, a, e):
        xb = V("pool", 4 * a + b, 4 * e, 4)
        tt(xb, V("rl", C * b + a, C * b + e), xb, A.add)

    def larger(k, a, b):
        tt(cols("zw", a, b, 1024 * k), cols("a%d" % k, a, b), cols("pool", a, b), A.max)

    def pointer_rows(t):
        pw = "pw%d" % t
        if t > 0:
            iota(V(pw, C, 256), [[1, 256 - C]], 0, 0)
        iota(V(pw, 256 + C, 512), [[1, 256 - C]], 0, 0)
        iota(V(pw, 512, 512 + 3 * K), [[0, 3], [1, K]], C + K * t, 0)
        iota(V(pw, 768, 768 + 3 * K), [[0, 3], [1, K]], C + K * t, 0)
        if t < R - 1:
            iota(V(pw, 1024, 1024 + C), [[1, C]], 0, 0)

    dma("a", "u", T.ub[:], T.u[:], [], [V("ub")])
    dma("s", "xa", T.pool[:, 0:4 * CA], T.x[:, 0:4 * CA], [], [cols("pool", 0, CA)])
    dma("s", "xb", T.pool[:, 4 * CA:4 * C], T.x[:, 4 * CA:4 * C], [], [cols("pool", CA, C)])
    dma("s", "nbd", T.nbd[:], T.nb[:], [], [("nbd", 0, 1, 1)])
    dma("s", "nbi", T.nbi[:], T.nb[:], [], [V("nbi")])
    iota(V("qti", 4, 5), [[1, 1]], 0, 1)
    iota(V("i8"), [[1, 8]], 0, 0)
    iota(V("pki"), [[1, 3], [16, 8]], 0, 0)
    iota(V("r16"), [[0, 15], [1, 16]], 0, 0)
    memset(V("ctlS"), 0.0)
    ts(V("qti", 0, 1), V("qti", 4, 5), 15, A.bitwise_and)
    ts(V("qti", 1, 2), V("qti", 4, 5), 4, A.arith_shift_right)
    ts(V("qti", 2, 3), V("qti", 4, 5), 3, A.bitwise_and)
    ts(V("qti", 3, 4), V("qti", 4, 5), 2, A.arith_shift_right, 3, A.bitwise_and)
    for o in (V("cmp", 4 * 176, 4 * 224), V("cmp", 4 * 336, 4 * 384)):
        lin(o, V("ctlS", 0, o[2] - o[1]), 0.0, 0.0)
    memset(V("seg"), 1.0)
    copy(V("qtf"), V("qti"))
    memset(cols("pool", C, 256), 0.0)
    memset(V("seg", 0, C, 16), 0.0)
    copy(V("pko"), V("pki"))
    ts(V("m8"), V("i8"), GF, A.is_equal)
    ts(V("e4"), V("i8", 0, 4), AF_, A.is_equal)
    memset(V("cmp", 4 * 432, 4 * 640), 0.0)
    for c in range(8):
        lin(V("bd", 64 * c, 64 * c + 64), V("ctlS", 0, 64), 0.0, V("m8", c, c + 1))
    memset(V("acc", 0, 1), 0.0)
    quant("qx0", "sx0", 0, CA, cols("pool", 0, CA))
    remote("q", 0, 0)
    quant("qu", "su", 0, 128, V("ub"))
    quant("qx0", "sx0", CA, 256, cols("pool", CA, 256))
    pick(0, 128)
    mm(4, "qU", "sU", 0, "qx0", "sx0", 0, CA)
    ts(V("c16"), V("r16", 0, C + 1), QF, A.not_equal, H, A.mult)
    memset(V("ctlS", 0, C, 16), H)
    lin(V("kk4"), V("e4"), 5120.0, -1024.0)
    lin(TB, AF_, -1024.0, 4096.0)
    lin(TC, V("e4", 0, 1), -5120.0, TB)
    lin(V("ctl16"), V("c16", 1, C + 1), -17408.0 / H, 16384.0)
    lin(TA, V("c16", 0, 1), -17408.0 / H, 1232.0)
    act(END16, V("ctl16", 15, 16), AF.Copy)

    def latest(k):
        if k == 0:
            lin(V("o2"), V("c16", 0, 16), -2.0 / H, 2.0)
            lin(V("o5"), V("c16", 1, 17), 5.0 / H, -5.0)
        elif k == 1:
            lin(V("m4"), V("e4"), 1.0 / 128.0, 0.0)
            for v in range(3):
                lin(V("k4", v, v + 1), V("e4", v + 1, v + 2), -2.5, V("e4", v, v + 1))
            lin(TD, V("e4", 0, 1), -1.5, -1.0)
            lin(TE, V("e4", 0, 1), 3.0, 0.0)
            lin(V("k4", 3, 4), V("e4", 3, 4), 1.0, TD)
        else:
            for v in range(4):
                lin(V("ctlA", v, C, 4), V("pw0", 0, 56), V("m4", v, v + 1), V("k4", v, v + 1))
            lin(CZ, QF, 1.0 / 2048.0, TE)
            lin(V("ctlB"), V("ctlA"), 2.0, 0.0)
            for v in range(3):
                lin(V("ctlC", v, C, 4), V("pw0", 0, 56), 0.0, V("k4", v, v + 1))

    for t in range(R):
        qx, sx = "qx%d" % t, "sx%d" % t
        pw = "pw%d" % t
        first, last = t == 0, t == R - 1

        def unpack(b):
            mm(b, "qe", "se", 128 * b, "ql%d" % t, "sl%d" % t, 0, C, ext=[("aq%d" % t, n_tile)])

        if not first:
            quant(qx, sx, CA, 256, cols("pool", CA, 256))
        else:
            own(4, 0, CA)
            quant("qbd", "sbd", 0, 128, V("bd"))
        hold(0, CA)
        if first:
            quant("qc", "sc", 512, 640, V("cmp", 2048, 2560))
        if t == 1:
            flags("l12", "f2", "ctlX")
            lin(V("lh"), V("l12", 15, C, 16), 0.5, KH)
        mm(5, "qU", "sU", 0, qx, sx, 0, C)
        remote("q", t, 1)
        remote("s", t)
        if first:
            iota(V("pw0", 0, 256), [[1, 256]], 0, 0)
            iota(V("eb"), [[0, 516]], 0, 0)
            for v in range(4):
                for b in range(4):
                    dma("s", "nbt", T.nbt[b:128:4, 42 * v:42 * v + 42], T.nbd[:, v, :, :], [("nbd", 0, 1, 1)], [V("nbt", 42 * v, 42 * v + 42)])
            dma("s", "j0", T.zw[:, 0:4 * C], T.x[:], [], [V("zw", 0, 4 * C)])
            dma("s", "w", T.qw[:].bitcast(dt.uint8), T.wc[:], [], [V("qw")])
            dma("s", "w", T.sw[:], T.ws[:], [], [V("sw")])
            dma("s", "v", T.vb[:], T.v[:], [], [V("vb")])
        else:
            mm(6, "qU", "sU", 256, qx, sx, 0, C)
        def forget(k):
            if k == 0:
                scan(V("l0"), V("f0"), V("ctlP0"), -2.0, A.max, A.add)
            elif k == 1:
                tt(V("wm"), V("l0", 15, C, 16), V("lh"), A.max)
            elif k == 2:
                ts(V("wo"), V("wm"), CW, A.add, 1024.0, A.mult)
            elif k == 3:
                act(V(pw, 0, C), V("pw%d" % (t - 1), 0, 1024 + C), AF.Copy, off=V("wo"))
            elif k == 4:
                held4(V("ps0"), V(pw, 0, C))
            elif k == 5:
                list4(V("po0"), V("ps0"))
            elif k == 6:
                for a, b in ((0, 56), (56, 112), (112, C)):
                    act(cols("a0", a, b), V("pool", 0, 4 * C + 4 * K * t), AF.Copy, off=V("po0", a // 4, b // 4))
                for a, b in ((JF, CA), (CA, C)):
                    act(cols("a1", a, b), V("a0"), AF.Copy, off=V("nb4", 56 * t + a // 4, 56 * t + b // 4))
            else:
                larger(0, 56 * (k - 7), 56 * (k - 6))

        def setup(k):
            if k == 0:
                ts(V("eb", 3, 512, 4), V("pw0", 0, 128), PF, A.is_equal)
            elif k == 1:
                for v in range(4):
                    ts(V("nb4", v, 168, 4), V("nbt", 42 * v, 42 * v + 42), 4.0, A.mult, BF_, A.add)
            elif k == 6:
                latest(0)
                act(V("a1"), X, AF.Copy, off=V("nb4", 0, 56))
            elif k == 12:
                ts(C1, QF, 1025.0, A.mult, TA, A.add)
                ts(C4, BF_, 0.25, A.mult, TC, A.add)
            elif k == 11:
                tt(V("ctlX", 0, 16), V("o2"), V("o5"), A.add)
            elif k >= 7:
                v = k - 7
                ts(V("ctl4", v, C, 4), V("r16", 0, 56), 0.0, A.mult, V("kk4", (v + 1) % 4, (v + 1) % 4 + 1), A.add)
            else:
                quant("qe", "se", 128 * (k - 2), 128 * (k - 1), V("eb", 5 - k, 517 - k))

        plan = PLAN["first" if first else "hurry" if hurry[t] else "even"]

        def aside(place):
            for k in plan.get(place, ()):
                (setup if first else forget)(k)

        slot(7, 4)
        if not first:
            act(V("f0"), P(6), AF.Sign, scale=-1.0)
        slot(6, 4)
        own(5, CA, C)
        slot(5, 4)
        diag(4, 0, CA)
        hold(CA, C)
        for m in (4, 3, 2, 1):
            slot(m, 4)
        def small():
            quant("qc", "sc", 384, 544, V("cmp", 1536, 2176))
            mm(7, "qbd", "sbd", 0, "qc", "sc", 384, 512, False, False)
            mm(7, "qbd", "sbd", 0, "qc", "sc", 512, 640, False, False)

        slot(13, 5)
        aside("a")
        diag(5, CA, C)
        slot(12, 5)
        aside("b")
        scan(V("ds"), V("seg"), lane(14, 0, C), 0.0, A.mult, A.add)
        slot(11, 5, "v")
        aside("c")
        slot(11, 5, "a")
        ts(V("t1"), V("ds", 15, C, 16), -1.0, A.mult, END16, A.add)
        slot(10, 5)
        quant("qc", "sc", 0, 224, V("cmp", 0, 896))
        mm(7, "qbd", "sbd", 0, "qc", "sc", 0, 224, True, False)
        if not first:
            small()
        slot(9, 5)
        slot(8, 5)
        if first:
            small()
        aside("d")
        quant("qc", "sc", 224, 384, V("cmp", 896, 1536))
        mm(7, "qbd", "sbd", 0, "qc", "sc", 224, 384, False, True)
        aside("x")
        tt(V("ctl16", 15, C, 16), V("acc"), V("t1"), A.add)
        aside("f")
        scan(V("cs"), P(7), V("ctl16"), 2048.0, A.min, A.add)
        aside("g")
        ts(V("rko"), V("cs", 15, C, 16), -1.0, A.mult, C1, A.add)
        aside("h")
        scatter(V("erow"), V("rko"), IOTA)
        aside("i")
        held4(V("es"), V("erow", 0, K))
        aside("j")
        list4(V("ex%d" % t), V("es"))
        remote("e", t)
        aside("k")
        if first:
            for a, b in ((16, 32), (32, 64), (64, 128), (128, C)):
                gcopy(V("ctlX", a, b), V("ctlX", 0, b - a))
            gcopy(V("ctlP1"), V("ctlX"))
            gcopy(V("ctlP0"), V("ctlX"))
            for k in range(3):
                iota(V("zw", 1024 * k + 4 * C, 1024 * k + 1024), [[0, 1024 - 4 * C]], 0, 0)
            pointer_rows(0)
        if not last:
            pointer_rows(t + 1)

        if first:
            pick(128, 256)
            latest(1)
            copy(V("nbo"), V("nbi"))
        slow = first and came

        def plane(b, on):
            if on == "a":
                act(V("dd", b, 4 * C, 4), P(b), AF.Copy)
            else:
                copy(V("dd", b, 4 * C, 4), P(b))

        if not slow:
            for b in range(4):
                unpack(b)
            plane(0, "a")
            plane(1, "a")
        if first:
            larger(1, 0, CA)
            mm(4, "qU", "sU", 128, qx, sx, 0, C)
        else:
            if JF:
                tt(cols("zw", 0, JF, 1024), V("a0"), cols("pool", 0, JF), A.max, off=V("nb4", 56 * t, 56 * t + JF // 4))
            else:
                larger(1, 0, CA)
            quant("qj0", "sj0", 0, C, V("zw", 0, 4 * C))
            mm(4, "qU", "sU", 128, "qj0", "sj0", 0, C)
            if JF:
                larger(1, JF, CA)
        gs = C + K * t
        got = [("ae%d" % t, n_list)]
        act(V("s0"), P(4), AF.Copy)
        if first:
            latest(2)
        larger(1, CA, C)
        quant("qj1", "sj1", 0, CA, cols("zw", 0, CA, 1024))
        mm(5, "qU", "sU", 128, "qj1", "sj1", 0, CA)
        if first:
            pick(256, 384, "v")
        if not slow:
            plane(2, "v")
        quant("qj1", "sj1", CA, 256, cols("zw", CB, C, 1024))
        if slow and SLOW:
            for b in range(4):
                unpack(b)
        mm(6, "qU", "sU", 128, "qj1", "sj1", CA, 256)
        if not slow:
            plane(3, "v")

        def better(part):
            bank, a, b, at = (5, 0, CA, 0) if part == 0 else (6, CA, C, CA - CB)
            tt(V("f1", a, b), P(bank, at, at + b - a), V("s0", a, b), A.is_gt)
            tt(V("m01", a, b), P(bank, at, at + b - a), V("s0", a, b), A.max)

        def ends(a, b, on="va"):
            if "v" in on:
                flags("h1", "f1", "ctlB", a, b)
            if "a" in on:
                lin(V("ctlC", a + 3, b, 4), V("h1", a + 3, b, 4), 0.5, V("k4", 3, 4))

        wait = came and (WAIT == 1 or WAIT == 2 and t != 1)

        def j2(a, b):
            tt(cols("zw", a, b, 2048), cols("pool", gs + a % K, gs + a % K + b - a), cols("pool", a, b), A.max)

        def offsets(a, b, k):
            if k == 0:
                flags("h2", "f2", "ctlC", a, b)
            else:
                ts(V("fo", a // 4, b // 4), V("h2", a + 3, b, 4), CZ, A.add, 2048.0, A.mult)

        def chosen(k):
            if k == 0:
                flags("l1", "f1", "ctlP1")
                lin(V("ctlX", 15, C, 16), V("l1", 15, C, 16), 0.5, KX)
            else:
                flags("l12", "f2", "ctlX")

        if wait:
            better(0)
            if not (slow and SLOW):
                better(1)
        if slow:
            for b in range(4):
                if not SLOW:
                    unpack(b)
                plane(b, "av"[b % 2])
            if SLOW:
                better(1)
        for a, b in ((0, 32), (32, K)):
            act(cols("pool", gs + a, gs + b), V("dd"), AF.Copy, off=V("el%d" % t, a // 4, b // 4), ext=got)
        tt(cols("zw", 32, K, 2048), V("dd"), cols("pool", 32, K), A.max, off=V("el%d" % t, 8, 24), ext=got)
        j2(0, 32)
        j2(K, CA)
        if wait:
            j2(2 * K, C)
            ends(0, C)
        else:
            better(0)
        quant("qj2", "sj2", 0, CA, cols("zw", 0, CA, 2048))
        mm(4, "qU", "sU", 128, "qj2", "sj2", 0, CA)
        if not wait:
            ends(0, CA)
            j2(2 * K, C)
        act(cols("zw", 0, CA, 3072), cols("zw", 0, CA, 2048), AF.Copy)
        j2(CA, 2 * K)
        if not wait:
            better(1)
        elif first:
            quant("qv", "sv", 0, 128, V("vb"))
        else:
            chosen(0)
        if not wait:
            tt(V("f2", 0, CA), P(4, 0, CA), V("m01", 0, CA), A.is_gt)
        quant("qj2", "sj2", CA, 256, cols("zw", CB, C, 2048))
        mm(7, "qU", "sU", 128, "qj2", "sj2", CA, 256)
        if wait:
            tt(V("f2", 0, CA), P(4, 0, CA), V("m01", 0, CA), A.is_gt)
        else:
            ends(CA, C)
        if first:
            act(TEND, V("ctlX", 15, 16), AF.Copy)
            lin(TF, V("c16", 0, 1), -2.5 / H, 1.5)
        offsets(0, CA, 0)
        if wait:
            tt(V("f2", CA, C), P(7, CA - CB, C - CB), V("m01", CA, C), A.is_gt)
        elif first:
            quant("qv", "sv", 0, 128, V("vb"))
        else:
            chosen(0)
        offsets(0, CA, 1)
        wa = V("zw", 0, 3072 + 4 * CA)
        za, zb = ZSPLIT
        if wait:
            act(cols("zw", CA, C, 3072), cols("zw", CA, C, 2048), AF.Copy)
        act(cols("zz", 0, za), wa, AF.Copy, off=V("fo", 0, za // 4))
        if not wait:
            act(cols("zw", CA, C, 3072), cols("zw", CA, C, 2048), AF.Copy)
        if wait:
            offsets(CA, C, 0)
            gather(cols("zz", za, CA), wa, V("fo", za // 4, 32))
            offsets(CA, C, 1)
        else:
            tt(V("f2", CA, C), P(7, CA - CB, C - CB), V("m01", CA, C), A.is_gt)
            gather(cols("zz", za, CA), wa, V("fo", za // 4, 32))
            offsets(CA, C, 0)
        if first:
            lin(V("ctlP1", 15, C, 16), V("pw0", 0, 14), 1.0 / 16.0, TEND)
            lin(KX, TEND, 1.0, TF)
        else:
            chosen(1)
        quant("qz", "sz", 0, CA, cols("zz", 0, CA))
        for b in range(4):
            mm(4 + b, "qw", "sw", 128 * b, "qz", "sz", 0, CA)
        if not wait:
            offsets(CA, C, 1)
        if zb > CA:
            act(cols("zz", CA, zb), V("zw"), AF.Copy, off=V("fo", 32, zb // 4))
        if last:
            ts(V("wo"), V("l12", 15, C, 16), CL, A.add, 512.0, A.mult)
        if first:
            flags("l1", "f1", "ctlP1")
        gather(cols("zz", zb, C), V("zw"), V("fo", zb // 4, 56))
        for b in range(4):
            if b == QZB:
                quant("qz", "sz", CA, 256, cols("zz", CB, C))
                for c in range(4):
                    mm(c, "qw", "sw", 128 * c, "qz", "sz", CA, 256)
            relu(b, 4 + b, 0, CA)
            add(b, 0, CA)
        for b in range(4):
            relu(b, b, CA, C, CA - CB)
        if first:
            lin(V("ctlX", 15, C, 16), V("l1", 15, C, 16), 0.5, KX)
            pick(256, 384, "a")
        act(V(pw, 256, 256 + C), V(pw, 0, C), AF.Copy, off=V("nbo", 14 * t, 14 * t + 14))
        if last:
            act(V("oprow"), V("pw2", 0, 1024), AF.Copy, off=V("wo"))
            dma("s", "out", T.op[:], T.oprow[0:128:16, :], [V("oprow")], [])
        if first:
            for o, k, c in ((TG, -3.5, 1.5), (KH, 1.0, 0.0), (TA, -1.5, 1.5)):
                lin(o, V("c16", 0, 1), k / H, c)
            lin(TB, TEND, 1.0, TA)
            lin(CW, QF, 1.0 / 1024.0, TG)
            lin(V("ctlP0", 15, C, 16), V("pw0", 0, 14), 1.0 / 64.0, TB)
        if t == 1:
            lin(V("lh"), V("l12", 15, C, 16), 0.5, KH)
            lin(TF, V("c16", 0, 1), -5.0 / H, 3.0)
            lin(CL, QF, 1.0 / 512.0, TF)
        qn, sn = "qx%d" % (t + 1), "sx%d" % (t + 1)
        add(0, CA, C)
        quant(qn, sn, 0, CA, cols("pool", 0, CA))
        if not last:
            mm(4, "qU", "sU", 0, qn, sn, 0, CA)
            remote("q", t + 1, 0)
            for b in (1, 2, 3):
                add(b, CA, C)
            own(4, 0, CA)

    mm(4, "qv", "sv", 0, "qx3", "sx3", 0, CA)
    dma("s", "out", T.oc[:, 0:4 * CA], codes(T, "qx3", 0, CA), [V("qx3", 0, CA)], [])
    for b in (1, 2, 3):
        add(b, CA, C)
    act(V("yb", 0, CA), P(4, 0, CA), AF.Copy)
    dma("s", "out", T.y[:, 0:CA], T.yb[:, 0:CA], [V("yb", 0, CA)], [])
    quant("qx3", "sx3", CA, 256, cols("pool", CA, 256))
    mm(5, "qv", "sv", 0, "qx3", "sx3", CB, C)
    dma("s", "out", T.oc[:, 4 * CA:4 * C], codes(T, "qx3", CA, C), [V("qx3", CA, C)], [])
    for k in range(4):
        dma("a", "outa", T.osc[4 * k:4 * k + 4, :], T.sx3[32 * k:32 * k + 4, 0:C], [V("sx3")], [])
    copy(V("yb", CA, C), P(5, CA - CB, C - CB))
    dma("s", "out", T.y[:, CA:C], T.yb[:, CA:C], [V("yb", CA, C)], [])
    def trip(sem):
        return (2 if came else 1) * (HOP + (FIRST if sem == "aq0" else 0))

    emit(g, T, arrange(ops, trip) if ARR else ops, [("sent", 3 * R * n_out)])
